import numpy as np
import ml_dtypes


def mxq(x, axis, fmt="e4m3"):
    dtype, down = {"e4m3": (ml_dtypes.float8_e4m3fn, 7), "e5m2": (ml_dtypes.float8_e5m2, 14)}[fmt]
    v = np.moveaxis(np.asarray(x, np.float32).astype(ml_dtypes.bfloat16).astype(np.float64), axis, -1)
    blocks = v.reshape(v.shape[:-1] + (-1, 32))
    amax = np.abs(blocks).max(-1, keepdims=True)
    byte = np.maximum(np.where(amax > 0, np.frexp(amax)[1] - 1 + 127, 0) - down, 1)
    scale = np.exp2(byte - 127.0)
    codes = (blocks / scale).astype(np.float32).astype(dtype).astype(np.float64)
    return np.moveaxis((codes * scale).reshape(v.shape), -1, axis)


WIDE = False


def mx_kscale(k):
    if not WIDE:
        return np.ones(k)
    levels = np.array([10, -10, 5, -5, 0])
    if k % 512:
        return np.exp2(np.random.permutation(np.resize(levels, k // 32))).repeat(32)
    a = np.empty((k // 512, 16))
    for p in range(k // 512):
        a[p, :8] = np.random.permutation(np.resize(levels, 8))
        for g in range(8):
            far = levels[np.abs(levels - a[p, g]) >= 10]
            a[p, g + 8] = far[np.random.randint(len(far))]
    return np.exp2(a.ravel()).repeat(32)


def f64(x):
    return np.asarray(x).astype(np.float64)


def striped(idx):
    return np.tile(idx.reshape(-1, 16).T, (8, 1)).astype(np.uint16)


def unstriped(offs):
    return offs[:16].T.reshape(-1).astype(np.int64)


E2M1 = np.array([0.0, 0.5, 1.0, 1.5, 2.0, 3.0, 4.0, 6.0, -0.0, -0.5, -1.0, -1.5, -2.0, -3.0, -4.0, -6.0])


def pack_weight(w, fmt):
    k, n = w.shape
    w = f64(np.asarray(w, np.float32).astype(ml_dtypes.bfloat16)).reshape(k // 32, 32, n)
    amax = np.abs(w).max(1)
    if fmt == "e4m3":
        byte = np.frexp(amax)[1] - 1 + 127 - 7
    else:
        mant, ex = np.frexp(amax / 6.0)
        byte = np.where(mant > 0.5, ex, ex - 1) + 127
    byte = np.clip(np.where(amax > 0, byte, 1), 1, 254)
    scaled = (w * np.exp2(127.0 - byte)[:, None, :]).reshape(k, n).astype(np.float32)
    by_word = np.ascontiguousarray(scaled.reshape(k // 512, 128, 4, n).transpose(0, 1, 3, 2))
    if fmt == "e4m3":
        words = by_word.astype(ml_dtypes.float8_e4m3fn).view(np.uint8)
    else:
        c = by_word.astype(ml_dtypes.float4_e2m1fn).view(np.uint8) & 0xF
        words = (c[..., 0::2] | (c[..., 1::2] << 4)).reshape(k // 512, 128, 2 * n)
    return np.ascontiguousarray(words), np.ascontiguousarray(byte.astype(np.uint8).reshape(k // 512, 16, n))


def unpack_weight(words, scales, fmt):
    g, _, n = scales.shape
    words = np.ascontiguousarray(words).reshape(g, 128, n, -1)
    if fmt == "e4m3":
        vals = words.view(ml_dtypes.float8_e4m3fn).astype(np.float64)
    else:
        nib = np.empty((g, 128, n, 4), np.uint8)
        nib[..., 0::2] = words & 0xF
        nib[..., 1::2] = words >> 4
        vals = E2M1[nib]
    vals = vals * np.repeat(np.exp2(scales.astype(np.float64) - 127.0), 8, axis=1)[..., None]
    return vals.transpose(0, 1, 3, 2).reshape(g * 512, n)


def gelu(v):
    return 0.5 * v * (1.0 + np.tanh(np.sqrt(2.0 / np.pi) * (v + 0.044715 * v**3)))


def bf(x):
    return np.asarray(x, np.float32).astype(ml_dtypes.bfloat16)

def planes(Y):
    n, m = Y.shape
    b = f64(bf(Y)).reshape(n // 32, 32, m)
    amax = np.abs(b).max(1)
    byte = np.clip(np.where(amax > 0, np.frexp(amax)[1] - 1 + 127 - 7, 1), 1, 254)
    codes = (b * np.exp2(127.0 - byte)[:, None, :]).reshape(n, m).astype(np.float32).astype(ml_dtypes.float8_e4m3fn).view(np.uint8)
    words = codes.reshape(n // 512, 128, 4, m).transpose(0, 1, 3, 2)
    return np.ascontiguousarray(words), np.ascontiguousarray(byte.astype(np.uint8).reshape(n // 512, 16, m))


K, T, S, T2, S2, N = 1024, 4096, 1536, 2048, 512, 1024

def setup_inputs():
    n = np.random.standard_normal
    s = mx_kscale(K)[:, None]
    u = mx_kscale(S)[:, None]
    tab_words, tab_scales = pack_weight(n((K, T)) * s, "e4m3")
    tab2_words, tab2_scales = pack_weight(1.5 * n((K, T2)) / (s * np.sqrt(K)), "e4m3")
    wd_words, wd_scales = pack_weight(3.0 * n((S, N)) / (u * np.sqrt(S)), "e2m1")
    wc = 3.0 * n((S, N)) * np.exp(0.8 * n(N)) / (u * np.sqrt(S))
    return {
        "tab_words": tab_words, "tab_scales": tab_scales,
        "tab2_words": tab2_words, "tab2_scales": tab2_scales,
        "offs": striped(np.random.permutation(T)[:S]),
        "offs2": striped(np.random.permutation(T2)[:S2]),
        "pathb": (-np.abs(n((S, S2)))).astype(np.float32),
        "trust": (np.exp(0.3 * n(S)) * u[:, 0]).astype(np.float32),
        "wc": wc.astype(np.float32),
        "wd_words": wd_words, "wd_scales": wd_scales,
    }

def reference(tab_words, tab_scales, tab2_words, tab2_scales, offs, offs2, pathb, trust, wc, wd_words, wd_scales):
    v = unpack_weight(tab_words, tab_scales, "e4m3")[:, unstriped(offs)]
    v2 = unpack_weight(tab2_words, tab2_scales, "e4m3")[:, unstriped(offs2)]
    a = (v.T @ v2) + f64(pathb)
    p = f64(trust)[:, None] * (1.0 / (1.0 + np.exp(-a)))
    pq = mxq(p, 0, "e4m3")
    c = mxq(f64(wc), 0, "e4m3").T @ pq
    d = unpack_weight(wd_words, wd_scales, "e2m1").T @ pq
    y = c * (1.0 / (1.0 + np.exp(-d)))
    words, scales = planes(y)
    return y, words, scales

@@ -1,0 +1,279 @@
+from contextlib import ExitStack
+
+import concourse.mybir as mybir
+
+K, T, S, T2, S2, N = 1024, 4096, 1536, 2048, 512, 1024
+FLOPS = 2 * K * S * S2 + 2 * 2 * S * N * S2
+
+F32 = mybir.dt.float32
+BF16 = mybir.dt.bfloat16
+I32 = mybir.dt.int32
+U32 = mybir.dt.uint32
+U16 = mybir.dt.uint16
+U8 = mybir.dt.uint8
+FP8X4 = mybir.dt.float8_e4m3fn_x4
+FP4X4 = mybir.dt.float4_e2m1fn_x4
+ADD = mybir.AluOpType.add
+MULT = mybir.AluOpType.mult
+SIGMOID = mybir.ActivationFunctionType.Sigmoid
+
+P = 128
+PACK = 4
+GROUP = P * PACK
+KP = K // GROUP
+SP = S // GROUP
+NG = N // GROUP
+
+
+def tile_list_code_search_context_kernel(
+    tc, tab_words, tab_scales, tab2_words, tab2_scales, offs, offs2, pathb, trust, wc, wd_words, wd_scales,
+    out_0, out_1, out_2,
+):
+    nc = tc.nc
+    with ExitStack() as ctx:
+        keep = ctx.enter_context(tc.tile_pool(name="keep", bufs=1))
+        ring = ctx.enter_context(tc.tile_pool(name="ring", bufs=2))
+        wring = ctx.enter_context(tc.tile_pool(name="wring", bufs=4))
+        psum = ctx.enter_context(tc.psum_pool(name="psum", bufs=1))
+
+        def held(shape, dtype, name):
+            return keep.tile(shape, dtype, name=name, align_bytes=64)
+
+        list1 = keep.tile([P, S // 16], U16, name="list1")
+        list2 = keep.tile([P, S2 // 16], U16, name="list2")
+        v_table = [held([P, T], U32, f"v_table{a}") for a in range(KP)]
+        q_table = [held([P, T2], U32, f"q_table{a}") for a in range(KP)]
+        v_table_scales = held([P, T], U8, "v_table_scales")
+        q_table_scales = held([P, T2], U8, "q_table_scales")
+        wd_raw = held([P, SP, 2 * N], U8, "wd_raw")
+        wd_raw_scales = held([P, SP, N], U8, "wd_raw_scales")
+        trust_sb = held([P, SP, PACK], F32, "trust_sb")
+        score = [held([P, PACK, S2], F32, f"score{g}") for g in range(SP)]
+
+        nc.vector.memset(v_table_scales[:].bitcast(I32), 0)
+        nc.gpsimd.memset(q_table_scales[:].bitcast(I32), 0)
+        nc.gpsimd.memset(wd_raw_scales[:].rearrange("p a n -> p (a n)").bitcast(I32), 0)
+
+        def load_scales(sb, dram):
+            for quad in range(4):
+                nc.sync.dma_start(
+                    sb[32 * quad : 32 * quad + 4 * KP, :].bitcast(I32),
+                    dram[:, 4 * quad : 4 * quad + 4, :].bitcast(I32),
+                )
+
+        def load_words(sb, dram):
+            nc.sync.dma_start(sb[:].bitcast(I32), dram.rearrange("p n t -> p (n t)").bitcast(I32))
+
+        wc_raw = {}
+
+        def load_wc(a, g):
+            raw = wring.tile([P, PACK, GROUP], F32, name="wc_raw")
+            nc.sync.dma_start(
+                raw[:],
+                wc[a * GROUP : (a + 1) * GROUP, g * GROUP : (g + 1) * GROUP].rearrange("(p j) n -> p j n", j=PACK),
+            )
+            wc_raw[a, g] = raw
+
+        def load_pathb(g):
+            nc.sync.dma_start(score[g][:], pathb[g * GROUP : (g + 1) * GROUP, :].rearrange("(p t) j -> p t j", t=PACK))
+
+        nc.sync.dma_start(list1[:], offs)
+        nc.sync.dma_start(list2[:], offs2)
+        nc.sync.dma_start(trust_sb[:], trust.rearrange("(g p t) -> p g t", p=P, t=PACK))
+        load_scales(v_table_scales, tab_scales)
+        load_words(v_table[0], tab_words[0])
+        load_words(v_table[1], tab_words[1])
+        load_scales(q_table_scales, tab2_scales)
+        load_words(q_table[0], tab2_words[0])
+        load_words(q_table[1], tab2_words[1])
+        for g in range(SP):
+            load_pathb(g)
+        load_wc(0, 0)
+        nc.sync.dma_start(wd_raw[:].bitcast(I32), wd_words.rearrange("a p n -> p a n").bitcast(I32))
+        for quad in range(4):
+            nc.sync.dma_start(
+                wd_raw_scales[32 * quad : 32 * quad + 4, :, :].bitcast(I32),
+                wd_scales[:, 4 * quad : 4 * quad + 4, :].rearrange("a r n -> r a n").bitcast(I32),
+            )
+        load_wc(1, 0)
+        load_wc(2, 0)
+        for a in range(SP):
+            load_wc(a, 1)
+
+        q_words = [held([P, S2], U32, f"q_words{a}") for a in range(KP)]
+        q_scales = held([P, S2], U8, "q_scales")
+        v_picked_scales = held([P, S], U8, "v_picked_scales")
+        v_scales = held([P, SP, PACK, P], U8, "v_scales")
+        v_words = [held([P, SP, PACK, P], U32, f"v_words{a}") for a in range(KP)]
+
+        def gather_v(a):
+            nc.vector.tensor_copy(v_words[a][:].rearrange("p g t m -> p g m t"), v_table[a][:].indirect(list1[:]))
+
+        banks = {}
+
+        def bank(b):
+            banks[b] = psum.tile([P, S2], F32, name=f"bank{b}")
+            return banks[b]
+
+        def score_matmuls(g):
+            for t in range(PACK):
+                acc = bank(4 + t)
+                for a in range(KP):
+                    nc.tensor.matmul_mx(
+                        out=acc[:],
+                        lhsT=v_words[a][:, g, t, :].bitcast(FP8X4),
+                        lhsT_scale=v_scales[4 * a : P, g, t, :],
+                        rhs=q_words[a][:].bitcast(FP8X4),
+                        rhs_scale=q_scales[4 * a : P, :],
+                        start=(a == 0),
+                        stop=(a == KP - 1),
+                    )
+
+        p_slices = {}
+
+        def relevance(g):
+            rounded = ring.tile([P, PACK, S2], BF16, name="p_slices", align_bytes=64, bufs=3)
+            p_slices[g] = rounded
+            for t in range(PACK):
+                z = score[g][:, t, :]
+                nc.vector.tensor_tensor(z, banks[4 + t][:], z, ADD)
+                nc.scalar.activation(z, z, SIGMOID)
+                nc.gpsimd.tensor_scalar(rounded[:, t, :], z, trust_sb[:, g, t : t + 1], 0.0, MULT, ADD)
+
+        def weave(engine_copy, src, name):
+            woven = ring.tile([P, S2, PACK], BF16, name=name, align_bytes=64)
+            engine_copy(woven[:].rearrange("p (c i) t -> p c t i", i=4), src[:].rearrange("p t (c i) -> p c t i", i=4))
+            return woven
+
+        def quantize(woven, name):
+            words = held([P, GROUP], U32, name + "_words")
+            scales = held([P, GROUP], U8, name + "_scales")
+            nc.vector.quantize_mx(out=words[:].bitcast(FP8X4), scales=scales[:], in_=woven)
+            return words, scales
+
+        wc_woven = {}
+        wc_q = {}
+        p_q = {}
+
+        def round_wc(engine_copy, a, g):
+            woven = wring.tile([P, PACK, P, PACK], BF16, name="wc_woven", align_bytes=64, bufs=4)
+            engine_copy(
+                woven[:].rearrange("p t m j -> p m j t"),
+                wc_raw[a, g][:].rearrange("p j (m t) -> p m j t", t=PACK),
+            )
+            wc_woven[a, g] = woven
+
+        def quantize_wc(a, g):
+            wc_q[a, g] = quantize(wc_woven[a, g][:].rearrange("p t m j -> p (t m j)"), f"wc{a}{g}")
+
+        wd_dealt = [held([P, PACK, SP, 2 * P], U8, f"wd_dealt{g}") for g in range(NG)]
+        wd_dealt_scales = [held([P, PACK, SP, P], U8, f"wd_dealt_scales{g}") for g in range(NG)]
+
+        def deal_wd(g):
+            nc.vector.tensor_copy(
+                wd_dealt[g][:].bitcast(U16),
+                wd_raw[:, :, 2 * g * GROUP : 2 * (g + 1) * GROUP].bitcast(U16).rearrange("p a (m t) -> p t a m", t=PACK),
+            )
+            nc.vector.tensor_copy(
+                wd_dealt_scales[g][:],
+                wd_raw_scales[:, :, g * GROUP : (g + 1) * GROUP].rearrange("p a (m t) -> p t a m", t=PACK),
+            )
+
+        def doc_pass(g, t, a):
+            acc = bank(t) if a == 0 else banks[t]
+            nc.tensor.matmul_mx(
+                out=acc[:],
+                lhsT=wd_dealt[g][:, t, a, :].bitcast(FP4X4),
+                lhsT_scale=wd_dealt_scales[g][:, t, a, :],
+                rhs=p_q[a][0][:].bitcast(FP8X4),
+                rhs_scale=p_q[a][1][:],
+                start=(a == 0),
+                stop=(a == SP - 1),
+            )
+
+        def code_pass(g, t, a):
+            acc = bank(4 + t) if a == 0 else banks[4 + t]
+            words, scales = wc_q[a, g]
+            nc.tensor.matmul_mx(
+                out=acc[:],
+                lhsT=words[:, t * P : (t + 1) * P].bitcast(FP8X4),
+                lhsT_scale=scales[:, t * P : (t + 1) * P],
+                rhs=p_q[a][0][:].bitcast(FP8X4),
+                rhs_scale=p_q[a][1][:],
+                start=(a == 0),
+                stop=(a == SP - 1),
+            )
+
+        def flat(woven):
+            return woven[:].rearrange("p j t -> p (j t)")
+
+        nc.vector.tensor_copy(v_picked_scales[:], v_table_scales[:].indirect(list1[:]))
+        gather_v(0)
+        nc.vector.tensor_copy(
+            v_scales[:].rearrange("p g t m -> p t g m"),
+            v_picked_scales[:].rearrange("p (g m t) -> p t g m", m=P, t=PACK),
+        )
+        gather_v(1)
+        nc.vector.tensor_copy(q_scales[:], q_table_scales[:].indirect(list2[:]))
+        nc.vector.tensor_copy(q_words[0][:], q_table[0][:].indirect(list2[:]))
+        nc.vector.tensor_copy(q_words[1][:], q_table[1][:].indirect(list2[:]))
+
+        for g in range(SP):
+            score_matmuls(g)
+            relevance(g)
+        for a in range(SP):
+            round_wc(nc.scalar.copy, a, 0)
+        woven = weave(nc.vector.tensor_copy, p_slices[0], "p_woven")
+        for a in range(SP):
+            ahead = weave(nc.vector.tensor_copy, p_slices[a + 1], "p_woven") if a + 1 < SP else None
+            p_q[a] = quantize(flat(woven), f"p{a}")
+            woven = ahead
+        deal_wd(0)
+        for a in range(SP):
+            quantize_wc(a, 0)
+
+        result = [held([P, PACK, S2], F32, f"result{g}") for g in range(NG)]
+
+        def gate(g, t):
+            nc.scalar.activation(result[g][:, t, :], banks[t][:], SIGMOID)
+
+        def gated(g, t):
+            y = result[g][:, t, :]
+            nc.vector.tensor_tensor(y, banks[4 + t][:], y, MULT)
+            nc.sync.dma_start(out_0[g * GROUP : (g + 1) * GROUP, :].rearrange("(p t) j -> p t j", t=PACK)[:, t, :], y)
+
+        def planes(g, woven):
+            words, scales = quantize(flat(woven), f"y{g}")
+            nc.sync.dma_start(out_1[g].rearrange("p m t -> p (m t)").bitcast(I32), words[:].bitcast(I32))
+            for quad in range(4):
+                nc.sync.dma_start(
+                    out_2[g, 4 * quad : 4 * quad + 4, :].bitcast(I32), scales[32 * quad : 32 * quad + 4, :].bitcast(I32)
+                )
+
+        for a in range(SP):
+            for t in range(PACK):
+                doc_pass(0, t, a)
+        for t in range(PACK):
+            gate(0, t)
+        deal_wd(1)
+        for a in range(SP):
+            for t in range(PACK):
+                code_pass(0, t, a)
+        for a in range(SP):
+            round_wc(nc.scalar.copy, a, 1)
+        for t in range(PACK):
+            gated(0, t)
+        for t in range(PACK):
+            for a in range(SP):
+                doc_pass(1, t, a)
+            gate(1, t)
+        for a in range(SP):
+            quantize_wc(a, 1)
+        woven = weave(nc.vector.tensor_copy, result[0], "y_woven")
+        planes(0, woven)
+        for t in range(PACK):
+            for a in range(SP):
+                code_pass(1, t, a)
+            gated(1, t)
+        woven = weave(nc.vector.tensor_copy, result[1], "y_woven")
+        planes(1, woven)

@@ -51,12 +51,12 @@ def tile_list_code_search_context_kernel(
         score = [held([P, PACK, S2], F32, f"score{g}") for g in range(SP)]
 
         nc.vector.memset(v_table_scales[:].bitcast(I32), 0)
-        nc.gpsimd.memset(q_table_scales[:].bitcast(I32), 0)
-        nc.gpsimd.memset(wd_raw_scales[:].rearrange("p a n -> p (a n)").bitcast(I32), 0)
+        nc.vector.memset(q_table_scales[:].bitcast(I32), 0)
+        nc.vector.memset(wd_raw_scales[:].rearrange("p a n -> p (a n)").bitcast(I32), 0)
 
         def load_scales(sb, dram):
             for quad in range(4):
-                nc.sync.dma_start(
+                nc.gpsimd.dma_start(
                     sb[32 * quad : 32 * quad + 4 * KP, :].bitcast(I32),
                     dram[:, 4 * quad : 4 * quad + 4, :].bitcast(I32),
                 )
@@ -64,10 +64,17 @@ def tile_list_code_search_context_kernel(
         def load_words(sb, dram):
             nc.sync.dma_start(sb[:].bitcast(I32), dram.rearrange("p n t -> p (n t)").bitcast(I32))
 
+        def load_wd_scales():
+            for quad in range(4):
+                nc.gpsimd.dma_start(
+                    wd_raw_scales[32 * quad : 32 * quad + 4, :, :].bitcast(I32),
+                    wd_scales[:, 4 * quad : 4 * quad + 4, :].rearrange("a r n -> r a n").bitcast(I32),
+                )
+
         wc_raw = {}
 
         def load_wc(a, g):
-            raw = wring.tile([P, PACK, GROUP], F32, name="wc_raw")
+            raw = keep.tile([P, PACK, GROUP], F32, name=f"wc_raw{a}{g}", tag=f"wc_raw{a}{g}")
             nc.sync.dma_start(
                 raw[:],
                 wc[a * GROUP : (a + 1) * GROUP, g * GROUP : (g + 1) * GROUP].rearrange("(p j) n -> p j n", j=PACK),
@@ -77,37 +84,45 @@ def tile_list_code_search_context_kernel(
         def load_pathb(g):
             nc.sync.dma_start(score[g][:], pathb[g * GROUP : (g + 1) * GROUP, :].rearrange("(p t) j -> p t j", t=PACK))
 
-        nc.sync.dma_start(list1[:], offs)
-        nc.sync.dma_start(list2[:], offs2)
-        nc.sync.dma_start(trust_sb[:], trust.rearrange("(g p t) -> p g t", p=P, t=PACK))
         load_scales(v_table_scales, tab_scales)
-        load_words(v_table[0], tab_words[0])
-        load_words(v_table[1], tab_words[1])
         load_scales(q_table_scales, tab2_scales)
+        load_wd_scales()
+        nc.sync.dma_start(list2[:], offs2)
         load_words(q_table[0], tab2_words[0])
+        nc.sync.dma_start(list1[:], offs)
+        load_words(v_table[0], tab_words[0])
         load_words(q_table[1], tab2_words[1])
-        for g in range(SP):
-            load_pathb(g)
         load_wc(0, 0)
-        nc.sync.dma_start(wd_raw[:].bitcast(I32), wd_words.rearrange("a p n -> p a n").bitcast(I32))
-        for quad in range(4):
-            nc.sync.dma_start(
-                wd_raw_scales[32 * quad : 32 * quad + 4, :, :].bitcast(I32),
-                wd_scales[:, 4 * quad : 4 * quad + 4, :].rearrange("a r n -> r a n").bitcast(I32),
-            )
+        load_words(v_table[1], tab_words[1])
         load_wc(1, 0)
+        nc.sync.dma_start(trust_sb[:], trust.rearrange("(g p t) -> p g t", p=P, t=PACK))
+        load_pathb(0)
+        load_pathb(1)
+        load_pathb(2)
+        nc.sync.dma_start(wd_raw[:].bitcast(I32), wd_words.rearrange("a p n -> p a n").bitcast(I32))
         load_wc(2, 0)
-        for a in range(SP):
-            load_wc(a, 1)
+        load_wc(0, 1)
+        load_wc(1, 1)
+        load_wc(2, 1)
 
         q_words = [held([P, S2], U32, f"q_words{a}") for a in range(KP)]
         q_scales = held([P, S2], U8, "q_scales")
         v_picked_scales = held([P, S], U8, "v_picked_scales")
         v_scales = held([P, SP, PACK, P], U8, "v_scales")
-        v_words = [held([P, SP, PACK, P], U32, f"v_words{a}") for a in range(KP)]
+        v_words = {(a, g): held([P, PACK, P], U32, f"v_words{a}{g}") for a in range(KP) for g in range(SP)}
+        cols = GROUP // 16
 
-        def gather_v(a):
-            nc.vector.tensor_copy(v_words[a][:].rearrange("p g t m -> p g m t"), v_table[a][:].indirect(list1[:]))
+        picked = {}
+
+        def gather_v(a, g):
+            picked[a, g] = ring.tile([P, GROUP], U32, name="picked", align_bytes=64)
+            nc.vector.tensor_copy(picked[a, g][:], v_table[a][:].indirect(list1[:, g * cols : (g + 1) * cols]))
+
+        def deal_v(a, g):
+            nc.vector.tensor_copy(
+                v_words[a, g][:].rearrange("p t (c i) -> p c t i", i=4),
+                picked[a, g][:].rearrange("p (c i t) -> p c t i", i=4, t=PACK),
+            )
 
         banks = {}
 
@@ -121,7 +136,7 @@ def tile_list_code_search_context_kernel(
                 for a in range(KP):
                     nc.tensor.matmul_mx(
                         out=acc[:],
-                        lhsT=v_words[a][:, g, t, :].bitcast(FP8X4),
+                        lhsT=v_words[a, g][:, t, :].bitcast(FP8X4),
                         lhsT_scale=v_scales[4 * a : P, g, t, :],
                         rhs=q_words[a][:].bitcast(FP8X4),
                         rhs_scale=q_scales[4 * a : P, :],
@@ -156,7 +171,7 @@ def tile_list_code_search_context_kernel(
         p_q = {}
 
         def round_wc(engine_copy, a, g):
-            woven = wring.tile([P, PACK, P, PACK], BF16, name="wc_woven", align_bytes=64, bufs=4)
+            woven = wring.tile([P, PACK, P, PACK], BF16, name="wc_woven", align_bytes=64, bufs=3)
             engine_copy(
                 woven[:].rearrange("p t m j -> p m j t"),
                 wc_raw[a, g][:].rearrange("p j (m t) -> p m j t", t=PACK),
@@ -207,34 +222,11 @@ def tile_list_code_search_context_kernel(
         def flat(woven):
             return woven[:].rearrange("p j t -> p (j t)")
 
-        nc.vector.tensor_copy(v_picked_scales[:], v_table_scales[:].indirect(list1[:]))
-        gather_v(0)
-        nc.vector.tensor_copy(
-            v_scales[:].rearrange("p g t m -> p t g m"),
-            v_picked_scales[:].rearrange("p (g m t) -> p t g m", m=P, t=PACK),
-        )
-        gather_v(1)
-        nc.vector.tensor_copy(q_scales[:], q_table_scales[:].indirect(list2[:]))
-        nc.vector.tensor_copy(q_words[0][:], q_table[0][:].indirect(list2[:]))
-        nc.vector.tensor_copy(q_words[1][:], q_table[1][:].indirect(list2[:]))
-
-        for g in range(SP):
-            score_matmuls(g)
-            relevance(g)
-        for a in range(SP):
-            round_wc(nc.scalar.copy, a, 0)
-        woven = weave(nc.vector.tensor_copy, p_slices[0], "p_woven")
-        for a in range(SP):
-            ahead = weave(nc.vector.tensor_copy, p_slices[a + 1], "p_woven") if a + 1 < SP else None
-            p_q[a] = quantize(flat(woven), f"p{a}")
-            woven = ahead
-        deal_wd(0)
-        for a in range(SP):
-            quantize_wc(a, 0)
-
-        result = [held([P, PACK, S2], F32, f"result{g}") for g in range(NG)]
+        result = {}
 
         def gate(g, t):
+            if t == 0:
+                result[g] = keep.tile([P, PACK, S2], F32, name=f"result{g}", tag=("wc_raw11", "wc_raw21")[g])
             nc.scalar.activation(result[g][:, t, :], banks[t][:], SIGMOID)
 
         def gated(g, t):
@@ -250,30 +242,80 @@ def tile_list_code_search_context_kernel(
                     out_2[g, 4 * quad : 4 * quad + 4, :].bitcast(I32), scales[32 * quad : 32 * quad + 4, :].bitcast(I32)
                 )
 
-        for a in range(SP):
-            for t in range(PACK):
-                doc_pass(0, t, a)
+        woven = {}
+        nc.vector.tensor_copy(q_words[0][:], q_table[0][:].indirect(list2[:]))
+        nc.vector.tensor_copy(v_picked_scales[:], v_table_scales[:].indirect(list1[:]))
+        gather_v(0, 0)
+        nc.vector.tensor_copy(
+            v_scales[:].rearrange("p g t m -> p t g m"),
+            v_picked_scales[:].rearrange("p (g m t) -> p t g m", m=P, t=PACK),
+        )
+        gather_v(0, 1)
+        deal_v(0, 0)
+        gather_v(0, 2)
+        deal_v(0, 1)
+        nc.vector.tensor_copy(q_words[1][:], q_table[1][:].indirect(list2[:]))
+        deal_v(0, 2)
+        nc.vector.tensor_copy(q_scales[:], q_table_scales[:].indirect(list2[:]))
+        round_wc(nc.scalar.copy, 0, 0)
+        gather_v(1, 0)
+        quantize_wc(0, 0)
+        deal_v(1, 0)
+        round_wc(nc.scalar.copy, 1, 0)
+        score_matmuls(0)
+        relevance(0)
+        gather_v(1, 1)
+        deal_v(1, 1)
+        score_matmuls(1)
+        relevance(1)
+        gather_v(1, 2)
+        deal_v(1, 2)
+        woven["p", 0] = weave(nc.vector.tensor_copy, p_slices[0], "p_woven")
+        score_matmuls(2)
+        relevance(2)
+        p_q[0] = quantize(flat(woven["p", 0]), "p0")
+        woven["p", 1] = weave(nc.vector.tensor_copy, p_slices[1], "p_woven")
+        p_q[1] = quantize(flat(woven["p", 1]), "p1")
+        woven["p", 2] = weave(nc.vector.tensor_copy, p_slices[2], "p_woven")
+        p_q[2] = quantize(flat(woven["p", 2]), "p2")
+        deal_wd(0)
+        round_wc(nc.scalar.copy, 2, 0)
+        quantize_wc(1, 0)
+        quantize_wc(2, 0)
+        for t in range(PACK):
+            doc_pass(0, t, 0)
+        for t in range(PACK):
+            doc_pass(0, t, 1)
+        for t in range(PACK):
+            code_pass(0, t, 0)
+        for t in range(PACK):
+            code_pass(0, t, 1)
+        for t in range(PACK):
+            doc_pass(0, t, 2)
+        for t in range(PACK):
+            code_pass(0, t, 2)
+        round_wc(nc.scalar.copy, 0, 1)
+        round_wc(nc.scalar.copy, 1, 1)
         for t in range(PACK):
             gate(0, t)
         deal_wd(1)
-        for a in range(SP):
-            for t in range(PACK):
-                code_pass(0, t, a)
-        for a in range(SP):
-            round_wc(nc.scalar.copy, a, 1)
+        round_wc(nc.vector.tensor_copy, 2, 1)
         for t in range(PACK):
             gated(0, t)
+        quantize_wc(0, 1)
+        quantize_wc(1, 1)
+        quantize_wc(2, 1)
         for t in range(PACK):
             for a in range(SP):
                 doc_pass(1, t, a)
+        for t in range(PACK):
             gate(1, t)
-        for a in range(SP):
-            quantize_wc(a, 1)
-        woven = weave(nc.vector.tensor_copy, result[0], "y_woven")
-        planes(0, woven)
+        woven["y", 0] = weave(nc.scalar.copy, result[0], "y_woven")
+        planes(0, woven["y", 0])
         for t in range(PACK):
             for a in range(SP):
                 code_pass(1, t, a)
+        for t in range(PACK):
             gated(1, t)
-        woven = weave(nc.vector.tensor_copy, result[1], "y_woven")
-        planes(1, woven)
+        woven["y", 1] = weave(nc.vector.tensor_copy, result[1], "y_woven")
+        planes(1, woven["y", 1])

@@ -16,6 +16,7 @@ FP4X4 = mybir.dt.float4_e2m1fn_x4
 ADD = mybir.AluOpType.add
 MULT = mybir.AluOpType.mult
 SIGMOID = mybir.ActivationFunctionType.Sigmoid
+COPY = mybir.ActivationFunctionType.Copy
 
 P = 128
 PACK = 4
@@ -50,13 +51,16 @@ def tile_list_code_search_context_kernel(
         trust_sb = held([P, SP, PACK], F32, "trust_sb")
         score = [held([P, PACK, S2], F32, f"score{g}") for g in range(SP)]
 
+        warm = held([P, 2], F32, "warm")
+        nc.vector.memset(warm[:], 0.0)
+        nc.scalar.activation(warm[:, 1:2], warm[:, 0:1], SIGMOID)
         nc.vector.memset(v_table_scales[:].bitcast(I32), 0)
         nc.vector.memset(q_table_scales[:].bitcast(I32), 0)
         nc.vector.memset(wd_raw_scales[:].rearrange("p a n -> p (a n)").bitcast(I32), 0)
 
         def load_scales(sb, dram):
             for quad in range(4):
-                nc.gpsimd.dma_start(
+                nc.sync.dma_start(
                     sb[32 * quad : 32 * quad + 4 * KP, :].bitcast(I32),
                     dram[:, 4 * quad : 4 * quad + 4, :].bitcast(I32),
                 )
@@ -66,7 +70,7 @@ def tile_list_code_search_context_kernel(
 
         def load_wd_scales():
             for quad in range(4):
-                nc.gpsimd.dma_start(
+                nc.sync.dma_start(
                     wd_raw_scales[32 * quad : 32 * quad + 4, :, :].bitcast(I32),
                     wd_scales[:, 4 * quad : 4 * quad + 4, :].rearrange("a r n -> r a n").bitcast(I32),
                 )
@@ -84,45 +88,35 @@ def tile_list_code_search_context_kernel(
         def load_pathb(g):
             nc.sync.dma_start(score[g][:], pathb[g * GROUP : (g + 1) * GROUP, :].rearrange("(p t) j -> p t j", t=PACK))
 
-        load_scales(v_table_scales, tab_scales)
-        load_scales(q_table_scales, tab2_scales)
-        load_wd_scales()
-        nc.sync.dma_start(list2[:], offs2)
-        load_words(q_table[0], tab2_words[0])
         nc.sync.dma_start(list1[:], offs)
-        load_words(v_table[0], tab_words[0])
-        load_words(q_table[1], tab2_words[1])
-        load_wc(0, 0)
-        load_words(v_table[1], tab_words[1])
-        load_wc(1, 0)
+        nc.sync.dma_start(list2[:], offs2)
         nc.sync.dma_start(trust_sb[:], trust.rearrange("(g p t) -> p g t", p=P, t=PACK))
+        load_scales(v_table_scales, tab_scales)
+        load_words(v_table[0], tab_words[0])
+        load_scales(q_table_scales, tab2_scales)
+        load_words(v_table[1], tab_words[1])
+        load_words(q_table[0], tab2_words[0])
+        load_words(q_table[1], tab2_words[1])
         load_pathb(0)
         load_pathb(1)
         load_pathb(2)
+        load_wc(0, 0)
         nc.sync.dma_start(wd_raw[:].bitcast(I32), wd_words.rearrange("a p n -> p a n").bitcast(I32))
+        load_wd_scales()
+        load_wc(1, 0)
         load_wc(2, 0)
         load_wc(0, 1)
         load_wc(1, 1)
         load_wc(2, 1)
 
+        v_picked_scales = held([P, S], U8, "v_picked_scales")
         q_words = [held([P, S2], U32, f"q_words{a}") for a in range(KP)]
         q_scales = held([P, S2], U8, "q_scales")
-        v_picked_scales = held([P, S], U8, "v_picked_scales")
         v_scales = held([P, SP, PACK, P], U8, "v_scales")
-        v_words = {(a, g): held([P, PACK, P], U32, f"v_words{a}{g}") for a in range(KP) for g in range(SP)}
-        cols = GROUP // 16
+        v_words = [held([P, SP, PACK, P], U32, f"v_words{a}") for a in range(KP)]
 
-        picked = {}
-
-        def gather_v(a, g):
-            picked[a, g] = ring.tile([P, GROUP], U32, name="picked", align_bytes=64)
-            nc.vector.tensor_copy(picked[a, g][:], v_table[a][:].indirect(list1[:, g * cols : (g + 1) * cols]))
-
-        def deal_v(a, g):
-            nc.vector.tensor_copy(
-                v_words[a, g][:].rearrange("p t (c i) -> p c t i", i=4),
-                picked[a, g][:].rearrange("p (c i t) -> p c t i", i=4, t=PACK),
-            )
+        def gather_v(a):
+            nc.vector.tensor_copy(v_words[a][:].rearrange("p g t m -> p g m t"), v_table[a][:].indirect(list1[:]))
 
         banks = {}
 
@@ -136,7 +130,7 @@ def tile_list_code_search_context_kernel(
                 for a in range(KP):
                     nc.tensor.matmul_mx(
                         out=acc[:],
-                        lhsT=v_words[a, g][:, t, :].bitcast(FP8X4),
+                        lhsT=v_words[a][:, g, t, :].bitcast(FP8X4),
                         lhsT_scale=v_scales[4 * a : P, g, t, :],
                         rhs=q_words[a][:].bitcast(FP8X4),
                         rhs_scale=q_scales[4 * a : P, :],
@@ -153,11 +147,20 @@ def tile_list_code_search_context_kernel(
                 z = score[g][:, t, :]
                 nc.vector.tensor_tensor(z, banks[4 + t][:], z, ADD)
                 nc.scalar.activation(z, z, SIGMOID)
-                nc.gpsimd.tensor_scalar(rounded[:, t, :], z, trust_sb[:, g, t : t + 1], 0.0, MULT, ADD)
+                nc.scalar.activation(rounded[:, t, :], z, COPY, scale=trust_sb[:, g, t : t + 1])
 
         def weave(engine_copy, src, name):
             woven = ring.tile([P, S2, PACK], BF16, name=name, align_bytes=64)
             engine_copy(woven[:].rearrange("p (c i) t -> p c t i", i=4), src[:].rearrange("p t (c i) -> p c t i", i=4))
+            return woven
+
+        def weave_shared(src, name, cut):
+            woven = ring.tile([P, S2, PACK], BF16, name=name, align_bytes=64)
+            for engine_copy, cols in ((nc.vector.tensor_copy, slice(0, cut)), (nc.scalar.copy, slice(cut, S2))):
+                engine_copy(
+                    woven[:, cols, :].rearrange("p (c i) t -> p c t i", i=4),
+                    src[:, :, cols].rearrange("p t (c i) -> p c t i", i=4),
+                )
             return woven
 
         def quantize(woven, name):
@@ -243,43 +246,33 @@ def tile_list_code_search_context_kernel(
                 )
 
         woven = {}
-        nc.vector.tensor_copy(q_words[0][:], q_table[0][:].indirect(list2[:]))
         nc.vector.tensor_copy(v_picked_scales[:], v_table_scales[:].indirect(list1[:]))
-        gather_v(0, 0)
+        gather_v(0)
         nc.vector.tensor_copy(
             v_scales[:].rearrange("p g t m -> p t g m"),
             v_picked_scales[:].rearrange("p (g m t) -> p t g m", m=P, t=PACK),
         )
-        gather_v(0, 1)
-        deal_v(0, 0)
-        gather_v(0, 2)
-        deal_v(0, 1)
-        nc.vector.tensor_copy(q_words[1][:], q_table[1][:].indirect(list2[:]))
-        deal_v(0, 2)
         nc.vector.tensor_copy(q_scales[:], q_table_scales[:].indirect(list2[:]))
-        round_wc(nc.scalar.copy, 0, 0)
-        gather_v(1, 0)
-        quantize_wc(0, 0)
-        deal_v(1, 0)
-        round_wc(nc.scalar.copy, 1, 0)
+        gather_v(1)
+        nc.vector.tensor_copy(q_words[0][:], q_table[0][:].indirect(list2[:]))
+        nc.vector.tensor_copy(q_words[1][:], q_table[1][:].indirect(list2[:]))
         score_matmuls(0)
         relevance(0)
-        gather_v(1, 1)
-        deal_v(1, 1)
         score_matmuls(1)
         relevance(1)
-        gather_v(1, 2)
-        deal_v(1, 2)
         woven["p", 0] = weave(nc.vector.tensor_copy, p_slices[0], "p_woven")
         score_matmuls(2)
         relevance(2)
         p_q[0] = quantize(flat(woven["p", 0]), "p0")
         woven["p", 1] = weave(nc.vector.tensor_copy, p_slices[1], "p_woven")
         p_q[1] = quantize(flat(woven["p", 1]), "p1")
+        round_wc(nc.vector.tensor_copy, 0, 0)
         woven["p", 2] = weave(nc.vector.tensor_copy, p_slices[2], "p_woven")
         p_q[2] = quantize(flat(woven["p", 2]), "p2")
+        quantize_wc(0, 0)
         deal_wd(0)
-        round_wc(nc.scalar.copy, 2, 0)
+        round_wc(nc.scalar.copy, 1, 0)
+        round_wc(nc.vector.tensor_copy, 2, 0)
         quantize_wc(1, 0)
         quantize_wc(2, 0)
         for t in range(PACK):
@@ -310,12 +303,12 @@ def tile_list_code_search_context_kernel(
                 doc_pass(1, t, a)
         for t in range(PACK):
             gate(1, t)
-        woven["y", 0] = weave(nc.scalar.copy, result[0], "y_woven")
+        woven["y", 0] = weave(nc.vector.tensor_copy, result[0], "y_woven")
         planes(0, woven["y", 0])
         for t in range(PACK):
             for a in range(SP):
                 code_pass(1, t, a)
         for t in range(PACK):
             gated(1, t)
-        woven["y", 1] = weave(nc.vector.tensor_copy, result[1], "y_woven")
+        woven["y", 1] = weave_shared(result[1], "y_woven", 320)
         planes(1, woven["y", 1])

@@ -48,7 +48,8 @@ def tile_list_code_search_context_kernel(
         q_table_scales = held([P, T2], U8, "q_table_scales")
         wd_raw = held([P, SP, 2 * N], U8, "wd_raw")
         wd_raw_scales = held([P, SP, N], U8, "wd_raw_scales")
-        trust_sb = held([P, SP, PACK], F32, "trust_sb")
+        trust_sb = held([P, SP, 2 * PACK], F32, "trust_sb")
+        trust_rows = trust.rearrange("(g p t) -> p g t", p=P, t=PACK)
         score = [held([P, PACK, S2], F32, f"score{g}") for g in range(SP)]
 
         warm = held([P, 2], F32, "warm")
@@ -90,13 +91,14 @@ def tile_list_code_search_context_kernel(
 
         nc.sync.dma_start(list1[:], offs)
         nc.sync.dma_start(list2[:], offs2)
-        nc.sync.dma_start(trust_sb[:], trust.rearrange("(g p t) -> p g t", p=P, t=PACK))
+        nc.sync.dma_start(trust_sb[:, 0, 0:PACK], trust_rows[:, 0, :])
         load_scales(v_table_scales, tab_scales)
         load_words(v_table[0], tab_words[0])
         load_scales(q_table_scales, tab2_scales)
         load_words(v_table[1], tab_words[1])
         load_words(q_table[0], tab2_words[0])
         load_words(q_table[1], tab2_words[1])
+        nc.sync.dma_start(trust_sb[:, 1:, 0:PACK], trust_rows[:, 1:, :])
         load_pathb(0)
         load_pathb(1)
         load_pathb(2)
@@ -113,10 +115,22 @@ def tile_list_code_search_context_kernel(
         q_words = [held([P, S2], U32, f"q_words{a}") for a in range(KP)]
         q_scales = held([P, S2], U8, "q_scales")
         v_scales = held([P, SP, PACK, P], U8, "v_scales")
-        v_words = [held([P, SP, PACK, P], U32, f"v_words{a}") for a in range(KP)]
+        v_words = [held([P, PACK, S // PACK], U32, f"v_words{a}") for a in range(KP)]
+
+        picked = {}
 
         def gather_v(a):
-            nc.vector.tensor_copy(v_words[a][:].rearrange("p g t m -> p g m t"), v_table[a][:].indirect(list1[:]))
+            if a >= 0:
+                nc.vector.tensor_copy(v_words[a][:].rearrange("p t s -> p s t"), v_table[a][:].indirect(list1[:]))
+            else:
+                picked[a] = keep.tile([P, S], U32, name=f"picked{a}", tag="picked", align_bytes=64)
+                nc.vector.tensor_copy(picked[a][:], v_table[a][:].indirect(list1[:]))
+
+        def deal_v(a):
+            nc.vector.tensor_copy(
+                v_words[a][:].rearrange("p t (c i) -> p c t i", i=4),
+                picked[a][:].rearrange("p (c i t) -> p c t i", i=4, t=PACK),
+            )
 
         banks = {}
 
@@ -130,7 +144,7 @@ def tile_list_code_search_context_kernel(
                 for a in range(KP):
                     nc.tensor.matmul_mx(
                         out=acc[:],
-                        lhsT=v_words[a][:, g, t, :].bitcast(FP8X4),
+                        lhsT=v_words[a][:, t, g * P : (g + 1) * P].bitcast(FP8X4),
                         lhsT_scale=v_scales[4 * a : P, g, t, :],
                         rhs=q_words[a][:].bitcast(FP8X4),
                         rhs_scale=q_scales[4 * a : P, :],

@@ -42,95 +42,99 @@ def tile_list_code_search_context_kernel(
 
         list1 = keep.tile([P, S // 16], U16, name="list1")
         list2 = keep.tile([P, S2 // 16], U16, name="list2")
-        v_table = [held([P, T], U32, f"v_table{a}") for a in range(KP)]
+        v_table = {1: held([P, T], U32, "v_table1")}
+        staged = held([P, 2 * S + S2], U8, "staged")
         q_table = [held([P, T2], U32, f"q_table{a}") for a in range(KP)]
-        v_table_scales = held([P, T], U8, "v_table_scales")
-        q_table_scales = held([P, T2], U8, "q_table_scales")
-        wd_raw = held([P, SP, 2 * N], U8, "wd_raw")
-        wd_raw_scales = held([P, SP, N], U8, "wd_raw_scales")
-        trust_sb = held([P, SP, 2 * PACK], F32, "trust_sb")
+        trust_sb = held([P, 1, 2 * PACK], F32, "trust_sb")
         trust_rows = trust.rearrange("(g p t) -> p g t", p=P, t=PACK)
-        score = [held([P, PACK, S2], F32, f"score{g}") for g in range(SP)]
+        scale_planes = held([P, 2, 2 * S + S2], U8, "scale_planes")
+        q_words = [held([P, S2], U32, f"q_words{a}") for a in range(KP)]
+        v_words = [held([P, PACK, S // PACK], U32, f"v_words{a}") for a in range(KP)]
 
-        warm = held([P, 2], F32, "warm")
-        nc.vector.memset(warm[:], 0.0)
-        nc.scalar.activation(warm[:, 1:2], warm[:, 0:1], SIGMOID)
-        nc.vector.memset(v_table_scales[:].bitcast(I32), 0)
-        nc.vector.memset(q_table_scales[:].bitcast(I32), 0)
-        nc.vector.memset(wd_raw_scales[:].rearrange("p a n -> p (a n)").bitcast(I32), 0)
+        with tc.tile_pool(name="head", bufs=1) as head:
+            v_table_scales = head.tile([P, T], U8, name="v_table_scales", align_bytes=64)
+            q_table_scales = head.tile([P, T2], U8, name="q_table_scales", align_bytes=64)
+            wd_raw_scales = head.tile([P, SP, GROUP], U8, name="wd_raw_scales", align_bytes=64)
+            v_picked_scales = head.tile([P, S], U8, name="v_picked_scales", align_bytes=64)
+            q_picked_scales = head.tile([P, S2], U8, name="q_picked_scales", align_bytes=64)
+            v_table[0] = head.tile([P, T], U32, name="v_table0", align_bytes=64)
 
-        def load_scales(sb, dram):
-            for quad in range(4):
+            warm = held([P, 2], F32, "warm")
+            nc.vector.memset(warm[:], 0.0)
+            nc.scalar.activation(warm[:, 1:2], warm[:, 0:1], SIGMOID)
+            nc.vector.memset(v_table_scales[:].bitcast(I32), 0)
+            nc.vector.memset(q_table_scales[:].bitcast(I32), 0)
+            nc.vector.memset(wd_raw_scales[:].rearrange("p a n -> p (a n)").bitcast(I32), 0)
+            nc.vector.memset(scale_planes[:].rearrange("p h n -> p (h n)").bitcast(I32), 0)
+
+            def load_scales(sb, dram):
+                nc.sync.dma_start(sb[0:P:4, :].bitcast(I32), dram.rearrange("a q t -> q a t").bitcast(I32))
+
+            def load_words(sb, dram):
+                nc.sync.dma_start(sb[:].bitcast(I32), dram.rearrange("p n t -> p (n t)").bitcast(I32))
+
+            wc_raw = {}
+
+            def load_wc(a, g):
+                raw = late.tile([P, PACK, GROUP], F32, name=f"wc_raw{a}{g}", tag=f"wc_raw{a}{g}")
                 nc.sync.dma_start(
-                    sb[32 * quad : 32 * quad + 4 * KP, :].bitcast(I32),
-                    dram[:, 4 * quad : 4 * quad + 4, :].bitcast(I32),
+                    raw[:],
+                    wc[a * GROUP : (a + 1) * GROUP, g * GROUP : (g + 1) * GROUP].rearrange("(p j) n -> p j n", j=PACK),
                 )
+                wc_raw[a, g] = raw
 
-        def load_words(sb, dram):
-            nc.sync.dma_start(sb[:].bitcast(I32), dram.rearrange("p n t -> p (n t)").bitcast(I32))
+            def load_pathb(g):
+                nc.sync.dma_start(score[g][:], pathb[g * GROUP : (g + 1) * GROUP, :].rearrange("(p t) j -> p t j", t=PACK))
 
-        def load_wd_scales():
-            for quad in range(4):
-                nc.sync.dma_start(
-                    wd_raw_scales[32 * quad : 32 * quad + 4, :, :].bitcast(I32),
-                    wd_scales[:, 4 * quad : 4 * quad + 4, :].rearrange("a r n -> r a n").bitcast(I32),
-                )
-
-        wc_raw = {}
-
-        def load_wc(a, g):
-            raw = keep.tile([P, PACK, GROUP], F32, name=f"wc_raw{a}{g}", tag=f"wc_raw{a}{g}")
+            nc.sync.dma_start(list1[:], offs)
+            nc.sync.dma_start(list2[:], offs2)
+            nc.sync.dma_start(trust_sb[:, 0, 0:PACK], trust_rows[:, 0, :])
+            load_scales(v_table_scales, tab_scales)
+            load_scales(q_table_scales, tab2_scales)
             nc.sync.dma_start(
-                raw[:],
-                wc[a * GROUP : (a + 1) * GROUP, g * GROUP : (g + 1) * GROUP].rearrange("(p j) n -> p j n", j=PACK),
+                wd_raw_scales[0:P:4, :, :].bitcast(I32), wd_scales.rearrange("a q (g c) -> (q g) a c", g=NG).bitcast(I32)
             )
-            wc_raw[a, g] = raw
+            load_words(v_table[0], tab_words[0])
+            load_words(v_table[1], tab_words[1])
+            load_words(q_table[0], tab2_words[0])
+            load_words(q_table[1], tab2_words[1])
 
-        def load_pathb(g):
-            nc.sync.dma_start(score[g][:], pathb[g * GROUP : (g + 1) * GROUP, :].rearrange("(p t) j -> p t j", t=PACK))
+            nc.vector.tensor_copy(v_picked_scales[:], v_table_scales[:].indirect(list1[:]))
+            nc.vector.tensor_copy(q_picked_scales[:], q_table_scales[:].indirect(list2[:]))
+            nc.vector.tensor_copy(
+                staged[:, S + S2 :].rearrange("p (t a m) -> p t a m", t=PACK, a=SP),
+                wd_raw_scales[:].rearrange("p a (m t) -> p t a m", t=PACK),
+            )
+            nc.vector.tensor_copy(
+                staged[:, 0:S].rearrange("p (g t m) -> p t g m", g=SP, t=PACK),
+                v_picked_scales[:].rearrange("p (g m t) -> p t g m", m=P, t=PACK),
+            )
+            nc.vector.tensor_copy(staged[:, S : S + S2].bitcast(U32), q_picked_scales[:].bitcast(U32))
+            for quad in range(4):
+                nc.scalar.dma_start(
+                    scale_planes[32 * quad : 32 * quad + 4, :, :].bitcast(I32),
+                    staged[32 * quad : 32 * quad + 32 : 4, :].bitcast(I32),
+                )
+            nc.vector.tensor_copy(v_words[0][:].rearrange("p t s -> p s t"), v_table[0][:].indirect(list1[:]))
 
-        nc.sync.dma_start(list1[:], offs)
-        nc.sync.dma_start(list2[:], offs2)
-        nc.sync.dma_start(trust_sb[:, 0, 0:PACK], trust_rows[:, 0, :])
-        load_scales(v_table_scales, tab_scales)
-        load_words(v_table[0], tab_words[0])
-        load_scales(q_table_scales, tab2_scales)
-        load_words(v_table[1], tab_words[1])
-        load_words(q_table[0], tab2_words[0])
-        load_words(q_table[1], tab2_words[1])
-        nc.sync.dma_start(trust_sb[:, 1:, 0:PACK], trust_rows[:, 1:, :])
+        late = ctx.enter_context(tc.tile_pool(name="late", bufs=1))
+        score = [late.tile([P, PACK, S2], F32, name=f"score{g}", align_bytes=64) for g in range(SP)]
+        wd_raw = late.tile([P, SP, 2 * N], U8, name="wd_raw", align_bytes=64)
+        trust_late = late.tile([P, SP - 1, 2 * PACK], F32, name="trust_late", align_bytes=64)
+        nc.sync.dma_start(trust_late[:, :, 0:PACK], trust_rows[:, 1:, :])
         load_pathb(0)
         load_pathb(1)
         load_pathb(2)
         load_wc(0, 0)
         nc.sync.dma_start(wd_raw[:].bitcast(I32), wd_words.rearrange("a p n -> p a n").bitcast(I32))
-        load_wd_scales()
         load_wc(1, 0)
         load_wc(2, 0)
         load_wc(0, 1)
         load_wc(1, 1)
         load_wc(2, 1)
 
-        v_picked_scales = held([P, S], U8, "v_picked_scales")
-        q_words = [held([P, S2], U32, f"q_words{a}") for a in range(KP)]
-        q_scales = held([P, S2], U8, "q_scales")
-        v_scales = held([P, SP, PACK, P], U8, "v_scales")
-        v_words = [held([P, PACK, S // PACK], U32, f"v_words{a}") for a in range(KP)]
-
-        picked = {}
-
         def gather_v(a):
-            if a >= 0:
-                nc.vector.tensor_copy(v_words[a][:].rearrange("p t s -> p s t"), v_table[a][:].indirect(list1[:]))
-            else:
-                picked[a] = keep.tile([P, S], U32, name=f"picked{a}", tag="picked", align_bytes=64)
-                nc.vector.tensor_copy(picked[a][:], v_table[a][:].indirect(list1[:]))
-
-        def deal_v(a):
-            nc.vector.tensor_copy(
-                v_words[a][:].rearrange("p t (c i) -> p c t i", i=4),
-                picked[a][:].rearrange("p (c i t) -> p c t i", i=4, t=PACK),
-            )
+            nc.vector.tensor_copy(v_words[a][:].rearrange("p t s -> p s t"), v_table[a][:].indirect(list1[:]))
 
         banks = {}
 
@@ -145,9 +149,9 @@ def tile_list_code_search_context_kernel(
                     nc.tensor.matmul_mx(
                         out=acc[:],
                         lhsT=v_words[a][:, t, g * P : (g + 1) * P].bitcast(FP8X4),
-                        lhsT_scale=v_scales[4 * a : P, g, t, :],
+                        lhsT_scale=scale_planes[:, a, (g * PACK + t) * P : (g * PACK + t + 1) * P],
                         rhs=q_words[a][:].bitcast(FP8X4),
-                        rhs_scale=q_scales[4 * a : P, :],
+                        rhs_scale=scale_planes[:, a, S : S + S2],
                         start=(a == 0),
                         stop=(a == KP - 1),
                     )
@@ -161,7 +165,7 @@ def tile_list_code_search_context_kernel(
                 z = score[g][:, t, :]
                 nc.vector.tensor_tensor(z, banks[4 + t][:], z, ADD)
                 nc.scalar.activation(z, z, SIGMOID)
-                nc.scalar.activation(rounded[:, t, :], z, COPY, scale=trust_sb[:, g, t : t + 1])
+                nc.scalar.activation(rounded[:, t, :], z, COPY, scale=(trust_sb[:, 0, t : t + 1] if g == 0 else trust_late[:, g - 1, t : t + 1]))
 
         def weave(engine_copy, src, name):
             woven = ring.tile([P, S2, PACK], BF16, name=name, align_bytes=64)
@@ -199,16 +203,11 @@ def tile_list_code_search_context_kernel(
             wc_q[a, g] = quantize(wc_woven[a, g][:].rearrange("p t m j -> p (t m j)"), f"wc{a}{g}")
 
         wd_dealt = [held([P, PACK, SP, 2 * P], U8, f"wd_dealt{g}") for g in range(NG)]
-        wd_dealt_scales = [held([P, PACK, SP, P], U8, f"wd_dealt_scales{g}") for g in range(NG)]
 
         def deal_wd(g):
             nc.vector.tensor_copy(
                 wd_dealt[g][:].bitcast(U16),
                 wd_raw[:, :, 2 * g * GROUP : 2 * (g + 1) * GROUP].bitcast(U16).rearrange("p a (m t) -> p t a m", t=PACK),
-            )
-            nc.vector.tensor_copy(
-                wd_dealt_scales[g][:],
-                wd_raw_scales[:, :, g * GROUP : (g + 1) * GROUP].rearrange("p a (m t) -> p t a m", t=PACK),
             )
 
         def doc_pass(g, t, a):
@@ -216,7 +215,7 @@ def tile_list_code_search_context_kernel(
             nc.tensor.matmul_mx(
                 out=acc[:],
                 lhsT=wd_dealt[g][:, t, a, :].bitcast(FP4X4),
-                lhsT_scale=wd_dealt_scales[g][:, t, a, :],
+                lhsT_scale=scale_planes[:, g, S + S2 + (t * SP + a) * P : S + S2 + (t * SP + a + 1) * P],
                 rhs=p_q[a][0][:].bitcast(FP8X4),
                 rhs_scale=p_q[a][1][:],
                 start=(a == 0),
@@ -243,7 +242,7 @@ def tile_list_code_search_context_kernel(
 
         def gate(g, t):
             if t == 0:
-                result[g] = keep.tile([P, PACK, S2], F32, name=f"result{g}", tag=("wc_raw11", "wc_raw21")[g])
+                result[g] = late.tile([P, PACK, S2], F32, name=f"result{g}", tag=("wc_raw11", "wc_raw21")[g])
             nc.scalar.activation(result[g][:, t, :], banks[t][:], SIGMOID)
 
         def gated(g, t):
@@ -260,13 +259,6 @@ def tile_list_code_search_context_kernel(
                 )
 
         woven = {}
-        nc.vector.tensor_copy(v_picked_scales[:], v_table_scales[:].indirect(list1[:]))
-        gather_v(0)
-        nc.vector.tensor_copy(
-            v_scales[:].rearrange("p g t m -> p t g m"),
-            v_picked_scales[:].rearrange("p (g m t) -> p t g m", m=P, t=PACK),
-        )
-        nc.vector.tensor_copy(q_scales[:], q_table_scales[:].indirect(list2[:]))
         gather_v(1)
         nc.vector.tensor_copy(q_words[0][:], q_table[0][:].indirect(list2[:]))
         nc.vector.tensor_copy(q_words[1][:], q_table[1][:].indirect(list2[:]))

@@ -42,22 +42,22 @@ def tile_list_code_search_context_kernel(
 
         list1 = keep.tile([P, S // 16], U16, name="list1")
         list2 = keep.tile([P, S2 // 16], U16, name="list2")
-        v_table = {1: held([P, T], U32, "v_table1")}
+        v_table = [held([P, T], U32, f"v_table{a}") for a in range(KP)]
         staged = held([P, 2 * S + S2], U8, "staged")
-        q_table = [held([P, T2], U32, f"q_table{a}") for a in range(KP)]
+        q_table = {}
         trust_sb = held([P, 1, 2 * PACK], F32, "trust_sb")
         trust_rows = trust.rearrange("(g p t) -> p g t", p=P, t=PACK)
         scale_planes = held([P, 2, 2 * S + S2], U8, "scale_planes")
-        q_words = [held([P, S2], U32, f"q_words{a}") for a in range(KP)]
-        v_words = [held([P, PACK, S // PACK], U32, f"v_words{a}") for a in range(KP)]
+        q_words = {1: held([P, S2], U32, "q_words1")}
+        wd_raw_scales = keep.tile([P, SP, GROUP], U8, name="wd_raw_scales", tag="q_words0", align_bytes=64)
+        v_words = {}
 
         with tc.tile_pool(name="head", bufs=1) as head:
             v_table_scales = head.tile([P, T], U8, name="v_table_scales", align_bytes=64)
             q_table_scales = head.tile([P, T2], U8, name="q_table_scales", align_bytes=64)
-            wd_raw_scales = head.tile([P, SP, GROUP], U8, name="wd_raw_scales", align_bytes=64)
             v_picked_scales = head.tile([P, S], U8, name="v_picked_scales", align_bytes=64)
+            q_table[0] = head.tile([P, T2], U32, name="q_table0", align_bytes=64)
             q_picked_scales = head.tile([P, S2], U8, name="q_picked_scales", align_bytes=64)
-            v_table[0] = head.tile([P, T], U32, name="v_table0", align_bytes=64)
 
             warm = held([P, 2], F32, "warm")
             nc.vector.memset(warm[:], 0.0)
@@ -84,57 +84,70 @@ def tile_list_code_search_context_kernel(
                 wc_raw[a, g] = raw
 
             def load_pathb(g):
-                nc.sync.dma_start(score[g][:], pathb[g * GROUP : (g + 1) * GROUP, :].rearrange("(p t) j -> p t j", t=PACK))
+                nc.sync.dma_start(bias[g][:], pathb[g * GROUP : (g + 1) * GROUP, :].rearrange("(p t) j -> p t j", t=PACK))
 
             nc.sync.dma_start(list1[:], offs)
             nc.sync.dma_start(list2[:], offs2)
             nc.sync.dma_start(trust_sb[:, 0, 0:PACK], trust_rows[:, 0, :])
             load_scales(v_table_scales, tab_scales)
+            load_words(q_table[0], tab2_words[0])
             load_scales(q_table_scales, tab2_scales)
             nc.sync.dma_start(
                 wd_raw_scales[0:P:4, :, :].bitcast(I32), wd_scales.rearrange("a q (g c) -> (q g) a c", g=NG).bitcast(I32)
             )
             load_words(v_table[0], tab_words[0])
             load_words(v_table[1], tab_words[1])
-            load_words(q_table[0], tab2_words[0])
-            load_words(q_table[1], tab2_words[1])
 
             nc.vector.tensor_copy(v_picked_scales[:], v_table_scales[:].indirect(list1[:]))
-            nc.vector.tensor_copy(q_picked_scales[:], q_table_scales[:].indirect(list2[:]))
-            nc.vector.tensor_copy(
-                staged[:, S + S2 :].rearrange("p (t a m) -> p t a m", t=PACK, a=SP),
-                wd_raw_scales[:].rearrange("p a (m t) -> p t a m", t=PACK),
-            )
             nc.vector.tensor_copy(
                 staged[:, 0:S].rearrange("p (g t m) -> p t g m", g=SP, t=PACK),
                 v_picked_scales[:].rearrange("p (g m t) -> p t g m", m=P, t=PACK),
             )
+            nc.vector.tensor_copy(q_picked_scales[:], q_table_scales[:].indirect(list2[:]))
             nc.vector.tensor_copy(staged[:, S : S + S2].bitcast(U32), q_picked_scales[:].bitcast(U32))
+            nc.vector.tensor_copy(
+                staged[:, S + S2 :].rearrange("p (t a m) -> p t a m", t=PACK, a=SP),
+                wd_raw_scales[:].rearrange("p a (m t) -> p t a m", t=PACK),
+            )
             for quad in range(4):
                 nc.scalar.dma_start(
                     scale_planes[32 * quad : 32 * quad + 4, :, :].bitcast(I32),
                     staged[32 * quad : 32 * quad + 32 : 4, :].bitcast(I32),
                 )
-            nc.vector.tensor_copy(v_words[0][:].rearrange("p t s -> p s t"), v_table[0][:].indirect(list1[:]))
+            q_words[0] = keep.tile([P, S2], U32, name="q_words0", tag="q_words0", align_bytes=64)
+            nc.vector.tensor_copy(q_words[0][:], q_table[0][:].indirect(list2[:]))
 
         late = ctx.enter_context(tc.tile_pool(name="late", bufs=1))
-        score = [late.tile([P, PACK, S2], F32, name=f"score{g}", align_bytes=64) for g in range(SP)]
+        bias = {g: late.tile([P, PACK, S2], F32, name=f"bias{g}", tag=f"bias{g}", align_bytes=64) for g in (1, 2)}
+        bias0 = [late.tile([P, 2, S2], F32, name=f"bias0{h}", tag=f"bias0{h}", align_bytes=64) for h in range(2)]
+        score = [held([P, PACK, S2], F32, "score0"), bias[1], bias[2]]
         wd_raw = late.tile([P, SP, 2 * N], U8, name="wd_raw", align_bytes=64)
         trust_late = late.tile([P, SP - 1, 2 * PACK], F32, name="trust_late", align_bytes=64)
+        q_table[1] = late.tile([P, T2], U32, name="q_table1", tag="q_table1", align_bytes=64)
+        load_words(q_table[1], tab2_words[1])
         nc.sync.dma_start(trust_late[:, :, 0:PACK], trust_rows[:, 1:, :])
-        load_pathb(0)
+        for h in range(2):
+            nc.sync.dma_start(
+                bias0[h][:], pathb[0:GROUP, :].rearrange("(p t) j -> p t j", t=PACK)[:, 2 * h : 2 * h + 2, :]
+            )
         load_pathb(1)
         load_pathb(2)
         load_wc(0, 0)
         nc.sync.dma_start(wd_raw[:].bitcast(I32), wd_words.rearrange("a p n -> p a n").bitcast(I32))
         load_wc(1, 0)
+        load_wc(2, 1)
         load_wc(2, 0)
         load_wc(0, 1)
         load_wc(1, 1)
-        load_wc(2, 1)
 
-        def gather_v(a):
-            nc.vector.tensor_copy(v_words[a][:].rearrange("p t s -> p s t"), v_table[a][:].indirect(list1[:]))
+        def gather_v(a, g):
+            if (a, g) == (KP - 1, SP - 1):
+                v_words[a, g] = late.tile([P, PACK, P], U32, name="v_words_last", tag="bias01", align_bytes=64)
+            else:
+                v_words[a, g] = held([P, PACK, P], U32, f"v_words{a}{g}")
+            nc.vector.tensor_copy(
+                v_words[a, g][:].rearrange("p t s -> p s t"), v_table[a][:].indirect(list1[:, 32 * g : 32 * (g + 1)])
+            )
 
         banks = {}
 
@@ -142,13 +155,14 @@ def tile_list_code_search_context_kernel(
             banks[b] = psum.tile([P, S2], F32, name=f"bank{b}")
             return banks[b]
 
-        def score_matmuls(g):
+        def score_matmuls(g, a):
             for t in range(PACK):
-                acc = bank(4 + t)
-                for a in range(KP):
+                b = (4 * (g + 1) + t) % 8
+                acc = bank(b) if a == 0 else banks[b]
+                if True:
                     nc.tensor.matmul_mx(
                         out=acc[:],
-                        lhsT=v_words[a][:, t, g * P : (g + 1) * P].bitcast(FP8X4),
+                        lhsT=v_words[a, g][:, t, :].bitcast(FP8X4),
                         lhsT_scale=scale_planes[:, a, (g * PACK + t) * P : (g * PACK + t + 1) * P],
                         rhs=q_words[a][:].bitcast(FP8X4),
                         rhs_scale=scale_planes[:, a, S : S + S2],
@@ -163,7 +177,7 @@ def tile_list_code_search_context_kernel(
             p_slices[g] = rounded
             for t in range(PACK):
                 z = score[g][:, t, :]
-                nc.vector.tensor_tensor(z, banks[4 + t][:], z, ADD)
+                nc.vector.tensor_tensor(z, banks[(4 * (g + 1) + t) % 8][:], (bias[g][:, t, :] if g else bias0[t // 2][:, t % 2, :]), ADD)
                 nc.scalar.activation(z, z, SIGMOID)
                 nc.scalar.activation(rounded[:, t, :], z, COPY, scale=(trust_sb[:, 0, t : t + 1] if g == 0 else trust_late[:, g - 1, t : t + 1]))
 
@@ -192,7 +206,7 @@ def tile_list_code_search_context_kernel(
         p_q = {}
 
         def round_wc(engine_copy, a, g):
-            woven = wring.tile([P, PACK, P, PACK], BF16, name="wc_woven", align_bytes=64, bufs=3)
+            woven = wring.tile([P, PACK, P, PACK], BF16, name="wc_woven", align_bytes=64, bufs=4)
             engine_copy(
                 woven[:].rearrange("p t m j -> p m j t"),
                 wc_raw[a, g][:].rearrange("p j (m t) -> p m j t", t=PACK),
@@ -222,8 +236,8 @@ def tile_list_code_search_context_kernel(
                 stop=(a == SP - 1),
             )
 
-        def code_pass(g, t, a):
-            acc = bank(4 + t) if a == 0 else banks[4 + t]
+        def code_pass(g, t, a, first, last):
+            acc = bank(4 + t) if first else banks[4 + t]
             words, scales = wc_q[a, g]
             nc.tensor.matmul_mx(
                 out=acc[:],
@@ -231,8 +245,8 @@ def tile_list_code_search_context_kernel(
                 lhsT_scale=scales[:, t * P : (t + 1) * P],
                 rhs=p_q[a][0][:].bitcast(FP8X4),
                 rhs_scale=p_q[a][1][:],
-                start=(a == 0),
-                stop=(a == SP - 1),
+                start=first,
+                stop=last,
             )
 
         def flat(woven):
@@ -242,7 +256,7 @@ def tile_list_code_search_context_kernel(
 
         def gate(g, t):
             if t == 0:
-                result[g] = late.tile([P, PACK, S2], F32, name=f"result{g}", tag=("wc_raw11", "wc_raw21")[g])
+                result[g] = late.tile([P, PACK, S2], F32, name=f"result{g}", tag=("wc_raw20", "wc_raw11")[g])
             nc.scalar.activation(result[g][:, t, :], banks[t][:], SIGMOID)
 
         def gated(g, t):
@@ -259,61 +273,61 @@ def tile_list_code_search_context_kernel(
                 )
 
         woven = {}
-        gather_v(1)
-        nc.vector.tensor_copy(q_words[0][:], q_table[0][:].indirect(list2[:]))
+        for g in range(SP):
+            gather_v(0, g)
+        score_matmuls(0, 0)
+        score_matmuls(1, 0)
+        gather_v(1, 0)
+        gather_v(1, 1)
         nc.vector.tensor_copy(q_words[1][:], q_table[1][:].indirect(list2[:]))
-        score_matmuls(0)
+        score_matmuls(0, 1)
+        score_matmuls(1, 1)
         relevance(0)
-        score_matmuls(1)
+        gather_v(1, 2)
         relevance(1)
+        score_matmuls(2, 0)
+        score_matmuls(2, 1)
         woven["p", 0] = weave(nc.vector.tensor_copy, p_slices[0], "p_woven")
-        score_matmuls(2)
         relevance(2)
         p_q[0] = quantize(flat(woven["p", 0]), "p0")
         woven["p", 1] = weave(nc.vector.tensor_copy, p_slices[1], "p_woven")
         p_q[1] = quantize(flat(woven["p", 1]), "p1")
         round_wc(nc.vector.tensor_copy, 0, 0)
-        woven["p", 2] = weave(nc.vector.tensor_copy, p_slices[2], "p_woven")
-        p_q[2] = quantize(flat(woven["p", 2]), "p2")
-        quantize_wc(0, 0)
         deal_wd(0)
+        woven["p", 2] = weave(nc.vector.tensor_copy, p_slices[2], "p_woven")
+        quantize_wc(0, 0)
+        p_q[2] = quantize(flat(woven["p", 2]), "p2")
+        deal_wd(1)
         round_wc(nc.scalar.copy, 1, 0)
-        round_wc(nc.vector.tensor_copy, 2, 0)
+        round_wc(nc.scalar.copy, 2, 0)
+        round_wc(nc.vector.tensor_copy, 2, 1)
         quantize_wc(1, 0)
+        quantize_wc(2, 1)
         quantize_wc(2, 0)
+        for a in range(SP):
+            for t in range(PACK):
+                doc_pass(0, t, a)
+        for a in range(SP):
+            for t in range(PACK):
+                code_pass(0, t, a, a == 0, a == SP - 1)
         for t in range(PACK):
-            doc_pass(0, t, 0)
-        for t in range(PACK):
-            doc_pass(0, t, 1)
-        for t in range(PACK):
-            code_pass(0, t, 0)
-        for t in range(PACK):
-            code_pass(0, t, 1)
-        for t in range(PACK):
-            doc_pass(0, t, 2)
-        for t in range(PACK):
-            code_pass(0, t, 2)
+            gate(0, t)
         round_wc(nc.scalar.copy, 0, 1)
         round_wc(nc.scalar.copy, 1, 1)
         for t in range(PACK):
-            gate(0, t)
-        deal_wd(1)
-        round_wc(nc.vector.tensor_copy, 2, 1)
-        for t in range(PACK):
             gated(0, t)
-        quantize_wc(0, 1)
-        quantize_wc(1, 1)
-        quantize_wc(2, 1)
         for t in range(PACK):
             for a in range(SP):
                 doc_pass(1, t, a)
+        woven["y", 0] = weave(nc.vector.tensor_copy, result[0], "y_woven")
+        quantize_wc(0, 1)
+        planes(0, woven["y", 0])
+        quantize_wc(1, 1)
+        for a in (2, 0, 1):
+            for t in range(PACK):
+                code_pass(1, t, a, a == 2, a == 1)
         for t in range(PACK):
             gate(1, t)
-        woven["y", 0] = weave(nc.vector.tensor_copy, result[0], "y_woven")
-        planes(0, woven["y", 0])
-        for t in range(PACK):
-            for a in range(SP):
-                code_pass(1, t, a)
         for t in range(PACK):
             gated(1, t)
         woven["y", 1] = weave_shared(result[1], "y_woven", 320)

@@ -24,6 +24,7 @@ GROUP = P * PACK
 KP = K // GROUP
 SP = S // GROUP
 NG = N // GROUP
+HALF = S2 // 2
 
 
 def tile_list_code_search_context_kernel(
@@ -43,21 +44,22 @@ def tile_list_code_search_context_kernel(
         list1 = keep.tile([P, S // 16], U16, name="list1")
         list2 = keep.tile([P, S2 // 16], U16, name="list2")
         v_table = [held([P, T], U32, f"v_table{a}") for a in range(KP)]
-        staged = held([P, 2 * S + S2], U8, "staged")
+        staged = held([P, S + S2], U8, "staged")
         q_table = {}
         trust_sb = held([P, 1, 2 * PACK], F32, "trust_sb")
         trust_rows = trust.rearrange("(g p t) -> p g t", p=P, t=PACK)
-        scale_planes = held([P, 2, 2 * S + S2], U8, "scale_planes")
+        scale_planes = held([P, 2, S + S2], U8, "scale_planes")
+        wd_planes = held([P, NG, S], U8, "wd_planes")
+        wd_raw_scales = held([P, SP, GROUP], U8, "wd_raw_scales")
         q_words = {1: held([P, S2], U32, "q_words1")}
-        wd_raw_scales = keep.tile([P, SP, GROUP], U8, name="wd_raw_scales", tag="q_words0", align_bytes=64)
+        q_picked_scales = keep.tile([P, S2], U8, name="q_picked_scales", tag="q_words0", align_bytes=64)
         v_words = {}
 
         with tc.tile_pool(name="head", bufs=1) as head:
             v_table_scales = head.tile([P, T], U8, name="v_table_scales", align_bytes=64)
             q_table_scales = head.tile([P, T2], U8, name="q_table_scales", align_bytes=64)
-            v_picked_scales = head.tile([P, S], U8, name="v_picked_scales", align_bytes=64)
             q_table[0] = head.tile([P, T2], U32, name="q_table0", align_bytes=64)
-            q_picked_scales = head.tile([P, S2], U8, name="q_picked_scales", align_bytes=64)
+            v_picked_scales = head.tile([P, S], U8, name="v_picked_scales", align_bytes=64)
 
             warm = held([P, 2], F32, "warm")
             nc.vector.memset(warm[:], 0.0)
@@ -66,6 +68,7 @@ def tile_list_code_search_context_kernel(
             nc.vector.memset(q_table_scales[:].bitcast(I32), 0)
             nc.vector.memset(wd_raw_scales[:].rearrange("p a n -> p (a n)").bitcast(I32), 0)
             nc.vector.memset(scale_planes[:].rearrange("p h n -> p (h n)").bitcast(I32), 0)
+            nc.vector.memset(wd_planes[:].rearrange("p h n -> p (h n)").bitcast(I32), 0)
 
             def load_scales(sb, dram):
                 nc.sync.dma_start(sb[0:P:4, :].bitcast(I32), dram.rearrange("a q t -> q a t").bitcast(I32))
@@ -90,26 +93,22 @@ def tile_list_code_search_context_kernel(
             nc.sync.dma_start(list2[:], offs2)
             nc.sync.dma_start(trust_sb[:, 0, 0:PACK], trust_rows[:, 0, :])
             load_scales(v_table_scales, tab_scales)
-            load_words(q_table[0], tab2_words[0])
             load_scales(q_table_scales, tab2_scales)
+            load_words(q_table[0], tab2_words[0])
+            load_words(v_table[0], tab_words[0])
+            load_words(v_table[1], tab_words[1])
             nc.sync.dma_start(
                 wd_raw_scales[0:P:4, :, :].bitcast(I32), wd_scales.rearrange("a q (g c) -> (q g) a c", g=NG).bitcast(I32)
             )
-            load_words(v_table[0], tab_words[0])
-            load_words(v_table[1], tab_words[1])
 
             nc.vector.tensor_copy(v_picked_scales[:], v_table_scales[:].indirect(list1[:]))
+            nc.vector.tensor_copy(q_picked_scales[:], q_table_scales[:].indirect(list2[:]))
             nc.vector.tensor_copy(
                 staged[:, 0:S].rearrange("p (g t m) -> p t g m", g=SP, t=PACK),
                 v_picked_scales[:].rearrange("p (g m t) -> p t g m", m=P, t=PACK),
             )
-            nc.vector.tensor_copy(q_picked_scales[:], q_table_scales[:].indirect(list2[:]))
             nc.vector.tensor_copy(staged[:, S : S + S2].bitcast(U32), q_picked_scales[:].bitcast(U32))
-            nc.vector.tensor_copy(
-                staged[:, S + S2 :].rearrange("p (t a m) -> p t a m", t=PACK, a=SP),
-                wd_raw_scales[:].rearrange("p a (m t) -> p t a m", t=PACK),
-            )
-            for quad in range(4):
+            for quad in (0, 2, 1, 3):
                 nc.scalar.dma_start(
                     scale_planes[32 * quad : 32 * quad + 4, :, :].bitcast(I32),
                     staged[32 * quad : 32 * quad + 32 : 4, :].bitcast(I32),
@@ -132,13 +131,6 @@ def tile_list_code_search_context_kernel(
             )
         load_pathb(1)
         load_pathb(2)
-        load_wc(0, 0)
-        nc.sync.dma_start(wd_raw[:].bitcast(I32), wd_words.rearrange("a p n -> p a n").bitcast(I32))
-        load_wc(1, 0)
-        load_wc(2, 1)
-        load_wc(2, 0)
-        load_wc(0, 1)
-        load_wc(1, 1)
 
         def gather_v(a, g):
             if (a, g) == (KP - 1, SP - 1):
@@ -175,46 +167,71 @@ def tile_list_code_search_context_kernel(
         def relevance(g):
             rounded = ring.tile([P, PACK, S2], BF16, name="p_slices", align_bytes=64, bufs=3)
             p_slices[g] = rounded
-            for t in range(PACK):
-                z = score[g][:, t, :]
-                nc.vector.tensor_tensor(z, banks[(4 * (g + 1) + t) % 8][:], (bias[g][:, t, :] if g else bias0[t // 2][:, t % 2, :]), ADD)
+            for h in range(2):
+                for t in (2 * h, 2 * h + 1):
+                    nc.vector.tensor_tensor(
+                        score[g][:, t, :],
+                        banks[(4 * (g + 1) + t) % 8][:],
+                        (bias[g][:, t, :] if g else bias0[h][:, t % 2, :]),
+                        ADD,
+                    )
+                z = score[g][:, 2 * h : 2 * h + 2, :]
                 nc.scalar.activation(z, z, SIGMOID)
-                nc.scalar.activation(rounded[:, t, :], z, COPY, scale=(trust_sb[:, 0, t : t + 1] if g == 0 else trust_late[:, g - 1, t : t + 1]))
+            for t in range(PACK):
+                nc.scalar.activation(
+                    rounded[:, t, :],
+                    score[g][:, t, :],
+                    COPY,
+                    scale=(trust_sb[:, 0, t : t + 1] if g == 0 else trust_late[:, g - 1, t : t + 1]),
+                )
 
-        def weave(engine_copy, src, name):
+        def weave_cols(engine_copy, woven, src, cols):
+            engine_copy(
+                woven[:, cols, :].rearrange("p (c i) t -> p c t i", i=4),
+                src[:, :, cols].rearrange("p t (c i) -> p c t i", i=4),
+            )
+
+        def weave(src, name):
             woven = ring.tile([P, S2, PACK], BF16, name=name, align_bytes=64)
-            engine_copy(woven[:].rearrange("p (c i) t -> p c t i", i=4), src[:].rearrange("p t (c i) -> p c t i", i=4))
+            for h in range(2):
+                weave_cols(nc.vector.tensor_copy, woven, src, slice(h * HALF, (h + 1) * HALF))
             return woven
 
         def weave_shared(src, name, cut):
             woven = ring.tile([P, S2, PACK], BF16, name=name, align_bytes=64)
-            for engine_copy, cols in ((nc.vector.tensor_copy, slice(0, cut)), (nc.scalar.copy, slice(cut, S2))):
-                engine_copy(
-                    woven[:, cols, :].rearrange("p (c i) t -> p c t i", i=4),
-                    src[:, :, cols].rearrange("p t (c i) -> p c t i", i=4),
-                )
+            weave_cols(nc.vector.tensor_copy, woven, src, slice(0, HALF))
+            weave_cols(nc.vector.tensor_copy, woven, src, slice(HALF, cut))
+            weave_cols(nc.scalar.copy, woven, src, slice(cut, S2))
             return woven
 
-        def quantize(woven, name):
+        def quantize(woven, name, parts):
             words = held([P, GROUP], U32, name + "_words")
             scales = held([P, GROUP], U8, name + "_scales")
-            nc.vector.quantize_mx(out=words[:].bitcast(FP8X4), scales=scales[:], in_=woven)
+            width = GROUP // parts
+            for h in range(parts):
+                nc.vector.quantize_mx(
+                    out=words[:, h * width : (h + 1) * width].bitcast(FP8X4),
+                    scales=scales[:, h * width : (h + 1) * width],
+                    in_=woven[:, PACK * h * width : PACK * (h + 1) * width],
+                )
             return words, scales
 
         wc_woven = {}
         wc_q = {}
         p_q = {}
 
-        def round_wc(engine_copy, a, g):
+        def round_wc(engine_copy, a, g, parts):
             woven = wring.tile([P, PACK, P, PACK], BF16, name="wc_woven", align_bytes=64, bufs=4)
-            engine_copy(
-                woven[:].rearrange("p t m j -> p m j t"),
-                wc_raw[a, g][:].rearrange("p j (m t) -> p m j t", t=PACK),
-            )
+            for h in range(parts):
+                slots = slice(h * PACK // parts, (h + 1) * PACK // parts)
+                engine_copy(
+                    woven[:, slots, :, :].rearrange("p t m j -> p m j t"),
+                    wc_raw[a, g][:].rearrange("p j (m t) -> p m j t", t=PACK)[:, :, :, slots],
+                )
             wc_woven[a, g] = woven
 
-        def quantize_wc(a, g):
-            wc_q[a, g] = quantize(wc_woven[a, g][:].rearrange("p t m j -> p (t m j)"), f"wc{a}{g}")
+        def quantize_wc(a, g, parts):
+            wc_q[a, g] = quantize(wc_woven[a, g][:].rearrange("p t m j -> p (t m j)"), f"wc{a}{g}", parts)
 
         wd_dealt = [held([P, PACK, SP, 2 * P], U8, f"wd_dealt{g}") for g in range(NG)]
 
@@ -229,7 +246,7 @@ def tile_list_code_search_context_kernel(
             nc.tensor.matmul_mx(
                 out=acc[:],
                 lhsT=wd_dealt[g][:, t, a, :].bitcast(FP4X4),
-                lhsT_scale=scale_planes[:, g, S + S2 + (t * SP + a) * P : S + S2 + (t * SP + a + 1) * P],
+                lhsT_scale=wd_planes[:, g, (t * SP + a) * P : (t * SP + a + 1) * P],
                 rhs=p_q[a][0][:].bitcast(FP8X4),
                 rhs_scale=p_q[a][1][:],
                 start=(a == 0),
@@ -265,7 +282,7 @@ def tile_list_code_search_context_kernel(
             nc.sync.dma_start(out_0[g * GROUP : (g + 1) * GROUP, :].rearrange("(p t) j -> p t j", t=PACK)[:, t, :], y)
 
         def planes(g, woven):
-            words, scales = quantize(flat(woven), f"y{g}")
+            words, scales = quantize(flat(woven), f"y{g}", 2)
             nc.sync.dma_start(out_1[g].rearrange("p m t -> p (m t)").bitcast(I32), words[:].bitcast(I32))
             for quad in range(4):
                 nc.sync.dma_start(
@@ -275,6 +292,24 @@ def tile_list_code_search_context_kernel(
         woven = {}
         for g in range(SP):
             gather_v(0, g)
+        wd_staged = keep.tile([P, S], U8, name="wd_staged", tag="v_table0", align_bytes=64)
+        nc.vector.tensor_copy(
+            wd_staged[:].rearrange("p (t a m) -> p t a m", t=PACK, a=SP),
+            wd_raw_scales[:].rearrange("p a (m t) -> p t a m", t=PACK),
+        )
+        for quad in (0, 2, 1, 3):
+            nc.sync.dma_start(
+                wd_planes[32 * quad : 32 * quad + 4, :, :].bitcast(I32),
+                wd_staged[32 * quad : 32 * quad + 32 : 4, :].bitcast(I32),
+            )
+        load_wc(0, 0)
+        nc.sync.dma_start(wd_raw[:].bitcast(I32), wd_words.rearrange("a p n -> p a n").bitcast(I32))
+        load_wc(1, 0)
+        load_wc(2, 1)
+        load_wc(2, 0)
+        load_wc(0, 1)
+        load_wc(1, 1)
+
         score_matmuls(0, 0)
         score_matmuls(1, 0)
         gather_v(1, 0)
@@ -287,23 +322,23 @@ def tile_list_code_search_context_kernel(
         relevance(1)
         score_matmuls(2, 0)
         score_matmuls(2, 1)
-        woven["p", 0] = weave(nc.vector.tensor_copy, p_slices[0], "p_woven")
+        woven["p", 0] = weave(p_slices[0], "p_woven")
         relevance(2)
-        p_q[0] = quantize(flat(woven["p", 0]), "p0")
-        woven["p", 1] = weave(nc.vector.tensor_copy, p_slices[1], "p_woven")
-        p_q[1] = quantize(flat(woven["p", 1]), "p1")
-        round_wc(nc.vector.tensor_copy, 0, 0)
+        p_q[0] = quantize(flat(woven["p", 0]), "p0", 2)
+        woven["p", 1] = weave(p_slices[1], "p_woven")
+        p_q[1] = quantize(flat(woven["p", 1]), "p1", 2)
+        round_wc(nc.vector.tensor_copy, 0, 0, 2)
         deal_wd(0)
-        woven["p", 2] = weave(nc.vector.tensor_copy, p_slices[2], "p_woven")
-        quantize_wc(0, 0)
-        p_q[2] = quantize(flat(woven["p", 2]), "p2")
+        woven["p", 2] = weave(p_slices[2], "p_woven")
+        quantize_wc(0, 0, 2)
+        p_q[2] = quantize(flat(woven["p", 2]), "p2", 2)
         deal_wd(1)
-        round_wc(nc.scalar.copy, 1, 0)
-        round_wc(nc.scalar.copy, 2, 0)
-        round_wc(nc.vector.tensor_copy, 2, 1)
-        quantize_wc(1, 0)
-        quantize_wc(2, 1)
-        quantize_wc(2, 0)
+        round_wc(nc.scalar.copy, 1, 0, 1)
+        round_wc(nc.scalar.copy, 2, 0, 1)
+        round_wc(nc.vector.tensor_copy, 2, 1, 2)
+        quantize_wc(1, 0, 1)
+        quantize_wc(2, 1, 2)
+        quantize_wc(2, 0, 1)
         for a in range(SP):
             for t in range(PACK):
                 doc_pass(0, t, a)
@@ -312,17 +347,17 @@ def tile_list_code_search_context_kernel(
                 code_pass(0, t, a, a == 0, a == SP - 1)
         for t in range(PACK):
             gate(0, t)
-        round_wc(nc.scalar.copy, 0, 1)
-        round_wc(nc.scalar.copy, 1, 1)
+        round_wc(nc.scalar.copy, 0, 1, 1)
+        round_wc(nc.scalar.copy, 1, 1, 1)
         for t in range(PACK):
             gated(0, t)
         for t in range(PACK):
             for a in range(SP):
                 doc_pass(1, t, a)
-        woven["y", 0] = weave(nc.vector.tensor_copy, result[0], "y_woven")
-        quantize_wc(0, 1)
+        woven["y", 0] = weave(result[0], "y_woven")
+        quantize_wc(0, 1, 1)
         planes(0, woven["y", 0])
-        quantize_wc(1, 1)
+        quantize_wc(1, 1, 1)
         for a in (2, 0, 1):
             for t in range(PACK):
                 code_pass(1, t, a, a == 2, a == 1)

@@ -273,7 +273,7 @@ def tile_list_code_search_context_kernel(
 
         def gate(g, t):
             if t == 0:
-                result[g] = late.tile([P, PACK, S2], F32, name=f"result{g}", tag=("wc_raw20", "wc_raw11")[g])
+                result[g] = late.tile([P, PACK, S2], F32, name=f"result{g}", tag=("wc_raw20", "wc_raw01")[g])
             nc.scalar.activation(result[g][:, t, :], banks[t][:], SIGMOID)
 
         def gated(g, t):
@@ -285,7 +285,7 @@ def tile_list_code_search_context_kernel(
             words, scales = quantize(flat(woven), f"y{g}", 2)
             nc.sync.dma_start(out_1[g].rearrange("p m t -> p (m t)").bitcast(I32), words[:].bitcast(I32))
             for quad in range(4):
-                nc.sync.dma_start(
+                (nc.sync if quad < 2 or g == 0 else nc.scalar).dma_start(
                     out_2[g, 4 * quad : 4 * quad + 4, :].bitcast(I32), scales[32 * quad : 32 * quad + 4, :].bitcast(I32)
                 )
 
@@ -307,8 +307,8 @@ def tile_list_code_search_context_kernel(
         load_wc(1, 0)
         load_wc(2, 1)
         load_wc(2, 0)
-        load_wc(0, 1)
         load_wc(1, 1)
+        load_wc(0, 1)
 
         score_matmuls(0, 0)
         score_matmuls(1, 0)
@@ -348,19 +348,19 @@ def tile_list_code_search_context_kernel(
         for t in range(PACK):
             gate(0, t)
         round_wc(nc.scalar.copy, 0, 1, 1)
-        round_wc(nc.scalar.copy, 1, 1, 1)
         for t in range(PACK):
             gated(0, t)
+        round_wc(nc.vector.tensor_copy, 1, 1, 2)
         for t in range(PACK):
             for a in range(SP):
                 doc_pass(1, t, a)
-        woven["y", 0] = weave(result[0], "y_woven")
+        quantize_wc(1, 1, 2)
         quantize_wc(0, 1, 1)
+        woven["y", 0] = weave(result[0], "y_woven")
         planes(0, woven["y", 0])
-        quantize_wc(1, 1, 1)
-        for a in (2, 0, 1):
+        for a in (2, 1, 0):
             for t in range(PACK):
-                code_pass(1, t, a, a == 2, a == 1)
+                code_pass(1, t, a, a == 2, a == 0)
         for t in range(PACK):
             gate(1, t)
         for t in range(PACK):

@@ -35,7 +35,6 @@ def tile_list_code_search_context_kernel(
     with ExitStack() as ctx:
         keep = ctx.enter_context(tc.tile_pool(name="keep", bufs=1))
         ring = ctx.enter_context(tc.tile_pool(name="ring", bufs=2))
-        wring = ctx.enter_context(tc.tile_pool(name="wring", bufs=4))
         psum = ctx.enter_context(tc.psum_pool(name="psum", bufs=1))
 
         def held(shape, dtype, name):
@@ -79,7 +78,7 @@ def tile_list_code_search_context_kernel(
             wc_raw = {}
 
             def load_wc(a, g):
-                raw = late.tile([P, PACK, GROUP], F32, name=f"wc_raw{a}{g}", tag=f"wc_raw{a}{g}")
+                raw = late.tile([P, PACK, GROUP], F32, name=f"wc_raw{a}{g}", tag=f"wc_raw{a}{g}", align_bytes=64)
                 nc.sync.dma_start(
                     raw[:],
                     wc[a * GROUP : (a + 1) * GROUP, g * GROUP : (g + 1) * GROUP].rearrange("(p j) n -> p j n", j=PACK),
@@ -87,7 +86,12 @@ def tile_list_code_search_context_kernel(
                 wc_raw[a, g] = raw
 
             def load_pathb(g):
-                nc.sync.dma_start(bias[g][:], pathb[g * GROUP : (g + 1) * GROUP, :].rearrange("(p t) j -> p t j", t=PACK))
+                rows = pathb[g * GROUP : (g + 1) * GROUP, :].rearrange("(p t) j -> p t j", t=PACK)
+                if g == 1:
+                    nc.sync.dma_start(score[g][:], rows)
+                else:
+                    for h in range(2):
+                        nc.sync.dma_start(bias[g, h][:], rows[:, 2 * h : 2 * h + 2, :])
 
             nc.sync.dma_start(list1[:], offs)
             nc.sync.dma_start(list2[:], offs2)
@@ -117,20 +121,21 @@ def tile_list_code_search_context_kernel(
             nc.vector.tensor_copy(q_words[0][:], q_table[0][:].indirect(list2[:]))
 
         late = ctx.enter_context(tc.tile_pool(name="late", bufs=1))
-        bias = {g: late.tile([P, PACK, S2], F32, name=f"bias{g}", tag=f"bias{g}", align_bytes=64) for g in (1, 2)}
-        bias0 = [late.tile([P, 2, S2], F32, name=f"bias0{h}", tag=f"bias0{h}", align_bytes=64) for h in range(2)]
-        score = [held([P, PACK, S2], F32, "score0"), bias[1], bias[2]]
+        bias = {
+            (g, h): late.tile([P, 2, S2], F32, name=f"bias{g}{h}", tag=f"bias{g}{h}", align_bytes=64)
+            for g in (0, 2)
+            for h in range(2)
+        }
+        score = [held([P, PACK, S2], F32, "score0"), late.tile([P, PACK, S2], F32, name="score1"), held([P, PACK, S2], F32, "score2")]
+        for h in range(2):
+            bias[1, h] = score[1][:, 2 * h : 2 * h + 2, :]
         wd_raw = late.tile([P, SP, 2 * N], U8, name="wd_raw", align_bytes=64)
         trust_late = late.tile([P, SP - 1, 2 * PACK], F32, name="trust_late", align_bytes=64)
         q_table[1] = late.tile([P, T2], U32, name="q_table1", tag="q_table1", align_bytes=64)
         load_words(q_table[1], tab2_words[1])
         nc.sync.dma_start(trust_late[:, :, 0:PACK], trust_rows[:, 1:, :])
-        for h in range(2):
-            nc.sync.dma_start(
-                bias0[h][:], pathb[0:GROUP, :].rearrange("(p t) j -> p t j", t=PACK)[:, 2 * h : 2 * h + 2, :]
-            )
+        load_pathb(0)
         load_pathb(1)
-        load_pathb(2)
 
         def gather_v(a, g):
             if (a, g) == (KP - 1, SP - 1):
@@ -172,7 +177,7 @@ def tile_list_code_search_context_kernel(
                     nc.vector.tensor_tensor(
                         score[g][:, t, :],
                         banks[(4 * (g + 1) + t) % 8][:],
-                        (bias[g][:, t, :] if g else bias0[h][:, t % 2, :]),
+                        bias[g, h][:, t % 2, :],
                         ADD,
                     )
                 z = score[g][:, 2 * h : 2 * h + 2, :]
@@ -191,8 +196,8 @@ def tile_list_code_search_context_kernel(
                 src[:, :, cols].rearrange("p t (c i) -> p c t i", i=4),
             )
 
-        def weave(src, name):
-            woven = ring.tile([P, S2, PACK], BF16, name=name, align_bytes=64)
+        def weave(src, name, tag):
+            woven = late.tile([P, S2, PACK], BF16, name=name, tag=tag, align_bytes=64)
             for h in range(2):
                 weave_cols(nc.vector.tensor_copy, woven, src, slice(h * HALF, (h + 1) * HALF))
             return woven
@@ -221,7 +226,7 @@ def tile_list_code_search_context_kernel(
         p_q = {}
 
         def round_wc(engine_copy, a, g, parts):
-            woven = wring.tile([P, PACK, P, PACK], BF16, name="wc_woven", align_bytes=64, bufs=4)
+            woven = late.tile([P, PACK, P, PACK], BF16, name=f"wc_woven{a}{g}", tag=f"wc_woven{(a + SP * g) % 4}", align_bytes=64)
             for h in range(parts):
                 slots = slice(h * PACK // parts, (h + 1) * PACK // parts)
                 engine_copy(
@@ -273,7 +278,7 @@ def tile_list_code_search_context_kernel(
 
         def gate(g, t):
             if t == 0:
-                result[g] = late.tile([P, PACK, S2], F32, name=f"result{g}", tag=("wc_raw20", "wc_raw01")[g])
+                result[g] = late.tile([P, PACK, S2], F32, name=f"result{g}", tag=("wc_raw10", "wc_raw11")[g], align_bytes=64)
             nc.scalar.activation(result[g][:, t, :], banks[t][:], SIGMOID)
 
         def gated(g, t):
@@ -302,14 +307,14 @@ def tile_list_code_search_context_kernel(
                 wd_planes[32 * quad : 32 * quad + 4, :, :].bitcast(I32),
                 wd_staged[32 * quad : 32 * quad + 32 : 4, :].bitcast(I32),
             )
-        load_wc(0, 0)
         nc.sync.dma_start(wd_raw[:].bitcast(I32), wd_words.rearrange("a p n -> p a n").bitcast(I32))
+        load_pathb(2)
+        load_wc(0, 0)
         load_wc(1, 0)
-        load_wc(2, 1)
         load_wc(2, 0)
-        load_wc(1, 1)
+        load_wc(2, 1)
         load_wc(0, 1)
-
+        load_wc(1, 1)
         score_matmuls(0, 0)
         score_matmuls(1, 0)
         gather_v(1, 0)
@@ -322,45 +327,51 @@ def tile_list_code_search_context_kernel(
         relevance(1)
         score_matmuls(2, 0)
         score_matmuls(2, 1)
-        woven["p", 0] = weave(p_slices[0], "p_woven")
-        relevance(2)
-        p_q[0] = quantize(flat(woven["p", 0]), "p0", 2)
-        woven["p", 1] = weave(p_slices[1], "p_woven")
-        p_q[1] = quantize(flat(woven["p", 1]), "p1", 2)
-        round_wc(nc.vector.tensor_copy, 0, 0, 2)
         deal_wd(0)
-        woven["p", 2] = weave(p_slices[2], "p_woven")
-        quantize_wc(0, 0, 2)
-        p_q[2] = quantize(flat(woven["p", 2]), "p2", 2)
         deal_wd(1)
+        relevance(2)
+        woven["p", 0] = weave(p_slices[0], "p_woven0", "bias20")
+        p_q[0] = quantize(flat(woven["p", 0]), "p0", 2)
+        for t in range(PACK):
+            doc_pass(0, t, 0)
+        woven["p", 1] = weave(p_slices[1], "p_woven1", "bias21")
+        p_q[1] = quantize(flat(woven["p", 1]), "p1", 2)
+        for t in range(PACK):
+            doc_pass(0, t, 1)
+        round_wc(nc.vector.tensor_copy, 0, 0, 2)
+        quantize_wc(0, 0, 2)
+        for t in range(PACK):
+            code_pass(0, t, 0, True, False)
+        woven["p", 2] = weave(p_slices[2], "p_woven2", "bias20")
+        p_q[2] = quantize(flat(woven["p", 2]), "p2", 2)
+        for t in range(PACK):
+            doc_pass(0, t, 2)
         round_wc(nc.scalar.copy, 1, 0, 1)
-        round_wc(nc.scalar.copy, 2, 0, 1)
-        round_wc(nc.vector.tensor_copy, 2, 1, 2)
+        round_wc(nc.vector.tensor_copy, 2, 0, 2)
         quantize_wc(1, 0, 1)
-        quantize_wc(2, 1, 2)
-        quantize_wc(2, 0, 1)
-        for a in range(SP):
-            for t in range(PACK):
-                doc_pass(0, t, a)
-        for a in range(SP):
-            for t in range(PACK):
-                code_pass(0, t, a, a == 0, a == SP - 1)
+        for t in range(PACK):
+            code_pass(0, t, 1, False, False)
         for t in range(PACK):
             gate(0, t)
-        round_wc(nc.scalar.copy, 0, 1, 1)
+        quantize_wc(2, 0, 2)
         for t in range(PACK):
-            gated(0, t)
-        round_wc(nc.vector.tensor_copy, 1, 1, 2)
+            code_pass(0, t, 2, False, True)
         for t in range(PACK):
             for a in range(SP):
                 doc_pass(1, t, a)
-        quantize_wc(1, 1, 2)
+        round_wc(nc.vector.tensor_copy, 2, 1, 2)
+        quantize_wc(2, 1, 2)
+        round_wc(nc.scalar.copy, 0, 1, 1)
+        round_wc(nc.scalar.copy, 1, 1, 1)
+        for t in range(PACK):
+            gated(0, t)
         quantize_wc(0, 1, 1)
-        woven["y", 0] = weave(result[0], "y_woven")
+        woven["y", 0] = weave(result[0], "y_woven0", "wc_raw01")
+        quantize_wc(1, 1, 1)
         planes(0, woven["y", 0])
-        for a in (2, 1, 0):
+        for a in (2, 0, 1):
             for t in range(PACK):
-                code_pass(1, t, a, a == 2, a == 0)
+                code_pass(1, t, a, a == 2, a == 1)
         for t in range(PACK):
             gate(1, t)
         for t in range(PACK):

@@ -21,10 +21,18 @@ COPY = mybir.ActivationFunctionType.Copy
 P = 128
 PACK = 4
 GROUP = P * PACK
-KP = K // GROUP
-SP = S // GROUP
-NG = N // GROUP
+K_GROUPS = K // GROUP
+I_GROUPS = S // GROUP
+N_GROUPS = N // GROUP
 HALF = S2 // 2
+LIST_COLUMNS = GROUP // 16
+QUADRANT = 32
+TABLE_ROWS = 16 * K_GROUPS
+TABLE_ROW0 = P - TABLE_ROWS
+WD_ROWS = 16 * N_GROUPS * I_GROUPS
+QUADRANT_ORDER = (0, 2, 1, 3)
+LAST_WEAVE_VECTOR_COLUMNS = 320
+WC_WOVEN_PLACES = 4
 
 
 def tile_list_code_search_context_kernel(
@@ -40,174 +48,164 @@ def tile_list_code_search_context_kernel(
         def held(shape, dtype, name):
             return keep.tile(shape, dtype, name=name, align_bytes=64)
 
+        def load_words(sb, dram):
+            nc.sync.dma_start(sb[:].bitcast(I32), dram.rearrange("p n t -> p (n t)").bitcast(I32))
+
         list1 = keep.tile([P, S // 16], U16, name="list1")
         list2 = keep.tile([P, S2 // 16], U16, name="list2")
-        v_table = [held([P, T], U32, f"v_table{a}") for a in range(KP)]
-        staged = held([P, S + S2], U8, "staged")
+        v_table = [held([P, T], U32, f"v_table{a}") for a in range(K_GROUPS)]
         q_table = {}
-        trust_sb = held([P, 1, 2 * PACK], F32, "trust_sb")
-        trust_rows = trust.rearrange("(g p t) -> p g t", p=P, t=PACK)
-        scale_planes = held([P, 2, S + S2], U8, "scale_planes")
-        wd_planes = held([P, NG, S], U8, "wd_planes")
-        wd_raw_scales = held([P, SP, GROUP], U8, "wd_raw_scales")
+        staged = held([P, S + S2], U8, "staged")
+        score_planes = held([P, K_GROUPS, S2 + S], U8, "score_planes")
+        wd_planes = held([P, N_GROUPS * I_GROUPS, GROUP], U8, "wd_planes")
+        wd_raw_scales = held([P, GROUP], U8, "wd_raw_scales")
         q_words = {1: held([P, S2], U32, "q_words1")}
-        q_picked_scales = keep.tile([P, S2], U8, name="q_picked_scales", tag="q_words0", align_bytes=64)
-        v_words = {}
+        v_picked_scales = keep.tile([P, S], U8, name="v_picked_scales", tag="q_words0", align_bytes=64)
 
         with tc.tile_pool(name="head", bufs=1) as head:
             v_table_scales = head.tile([P, T], U8, name="v_table_scales", align_bytes=64)
             q_table_scales = head.tile([P, T2], U8, name="q_table_scales", align_bytes=64)
             q_table[0] = head.tile([P, T2], U32, name="q_table0", align_bytes=64)
-            v_picked_scales = head.tile([P, S], U8, name="v_picked_scales", align_bytes=64)
+            q_picked_scales = head.tile([P, S2], U8, name="q_picked_scales", align_bytes=64)
 
             warm = held([P, 2], F32, "warm")
             nc.vector.memset(warm[:], 0.0)
             nc.scalar.activation(warm[:, 1:2], warm[:, 0:1], SIGMOID)
-            nc.vector.memset(v_table_scales[:].bitcast(I32), 0)
-            nc.vector.memset(q_table_scales[:].bitcast(I32), 0)
-            nc.vector.memset(wd_raw_scales[:].rearrange("p a n -> p (a n)").bitcast(I32), 0)
-            nc.vector.memset(scale_planes[:].rearrange("p h n -> p (h n)").bitcast(I32), 0)
-            nc.vector.memset(wd_planes[:].rearrange("p h n -> p (h n)").bitcast(I32), 0)
 
-            def load_scales(sb, dram):
-                nc.sync.dma_start(sb[0:P:4, :].bitcast(I32), dram.rearrange("a q t -> q a t").bitcast(I32))
+            for window in (v_table_scales, q_table_scales):
+                nc.vector.memset(window[0:TABLE_ROW0, :].bitcast(I32), 0)
+            nc.vector.memset(wd_raw_scales[WD_ROWS:P, :].bitcast(I32), 0)
+            for planes in (score_planes, wd_planes):
+                nc.vector.memset(planes[:].rearrange("p c n -> p (c n)").bitcast(I32), 0)
 
-            def load_words(sb, dram):
-                nc.sync.dma_start(sb[:].bitcast(I32), dram.rearrange("p n t -> p (n t)").bitcast(I32))
-
-            wc_raw = {}
-
-            def load_wc(a, g):
-                raw = late.tile([P, PACK, GROUP], F32, name=f"wc_raw{a}{g}", tag=f"wc_raw{a}{g}", align_bytes=64)
-                nc.sync.dma_start(
-                    raw[:],
-                    wc[a * GROUP : (a + 1) * GROUP, g * GROUP : (g + 1) * GROUP].rearrange("(p j) n -> p j n", j=PACK),
-                )
-                wc_raw[a, g] = raw
-
-            def load_pathb(g):
-                rows = pathb[g * GROUP : (g + 1) * GROUP, :].rearrange("(p t) j -> p t j", t=PACK)
-                if g == 1:
-                    nc.sync.dma_start(score[g][:], rows)
-                else:
-                    for h in range(2):
-                        nc.sync.dma_start(bias[g, h][:], rows[:, 2 * h : 2 * h + 2, :])
+            def load_table_scales(sb, dram):
+                nc.sync.dma_start(sb[TABLE_ROW0:P, :].bitcast(I32), dram.rearrange("a q t -> q a t").bitcast(I32))
 
             nc.sync.dma_start(list1[:], offs)
+            load_table_scales(v_table_scales, tab_scales)
             nc.sync.dma_start(list2[:], offs2)
-            nc.sync.dma_start(trust_sb[:, 0, 0:PACK], trust_rows[:, 0, :])
-            load_scales(v_table_scales, tab_scales)
-            load_scales(q_table_scales, tab2_scales)
+            load_table_scales(q_table_scales, tab2_scales)
             load_words(q_table[0], tab2_words[0])
             load_words(v_table[0], tab_words[0])
             load_words(v_table[1], tab_words[1])
             nc.sync.dma_start(
-                wd_raw_scales[0:P:4, :, :].bitcast(I32), wd_scales.rearrange("a q (g c) -> (q g) a c", g=NG).bitcast(I32)
+                wd_raw_scales[0:WD_ROWS, :].bitcast(I32),
+                wd_scales.rearrange("b q (g c) -> (q g) b c", g=N_GROUPS).bitcast(I32),
             )
 
             nc.vector.tensor_copy(v_picked_scales[:], v_table_scales[:].indirect(list1[:]))
             nc.vector.tensor_copy(q_picked_scales[:], q_table_scales[:].indirect(list2[:]))
             nc.vector.tensor_copy(
-                staged[:, 0:S].rearrange("p (g t m) -> p t g m", g=SP, t=PACK),
-                v_picked_scales[:].rearrange("p (g m t) -> p t g m", m=P, t=PACK),
+                staged[:, S2:].rearrange("p (b t m) -> p t b m", b=I_GROUPS, t=PACK),
+                v_picked_scales[:].rearrange("p (b m t) -> p t b m", m=P, t=PACK),
             )
-            nc.vector.tensor_copy(staged[:, S : S + S2].bitcast(U32), q_picked_scales[:].bitcast(U32))
-            for quad in (0, 2, 1, 3):
+            nc.vector.tensor_copy(staged[:, 0:S2].bitcast(U32), q_picked_scales[:].bitcast(U32))
+            rows = TABLE_ROWS // 4
+            for quad in QUADRANT_ORDER:
                 nc.scalar.dma_start(
-                    scale_planes[32 * quad : 32 * quad + 4, :, :].bitcast(I32),
-                    staged[32 * quad : 32 * quad + 32 : 4, :].bitcast(I32),
+                    score_planes[QUADRANT * quad : QUADRANT * quad + 4, :, :].bitcast(I32),
+                    staged[TABLE_ROW0 + rows * quad : TABLE_ROW0 + rows * (quad + 1), :].bitcast(I32),
                 )
             q_words[0] = keep.tile([P, S2], U32, name="q_words0", tag="q_words0", align_bytes=64)
             nc.vector.tensor_copy(q_words[0][:], q_table[0][:].indirect(list2[:]))
 
         late = ctx.enter_context(tc.tile_pool(name="late", bufs=1))
-        bias = {
-            (g, h): late.tile([P, 2, S2], F32, name=f"bias{g}{h}", tag=f"bias{g}{h}", align_bytes=64)
-            for g in (0, 2)
-            for h in range(2)
-        }
-        score = [held([P, PACK, S2], F32, "score0"), late.tile([P, PACK, S2], F32, name="score1"), held([P, PACK, S2], F32, "score2")]
+
+        def placed(shape, dtype, name, tag):
+            return late.tile(shape, dtype, name=name, tag=tag, align_bytes=64)
+
+        bias = {(b, h): placed([P, 2, S2], F32, f"bias{b}{h}", f"bias{b}{h}") for b in (0, 2) for h in range(2)}
+        score = [
+            held([P, PACK, S2], F32, "score0"),
+            late.tile([P, PACK, S2], F32, name="score1"),
+            held([P, PACK, S2], F32, "score2"),
+        ]
         for h in range(2):
             bias[1, h] = score[1][:, 2 * h : 2 * h + 2, :]
-        wd_raw = late.tile([P, SP, 2 * N], U8, name="wd_raw", align_bytes=64)
-        trust_late = late.tile([P, SP - 1, 2 * PACK], F32, name="trust_late", align_bytes=64)
-        q_table[1] = late.tile([P, T2], U32, name="q_table1", tag="q_table1", align_bytes=64)
+        wd_raw = late.tile([P, I_GROUPS, 2 * N], U8, name="wd_raw", align_bytes=64)
+        trust_sb = late.tile([P, I_GROUPS, 2 * PACK], F32, name="trust_sb", align_bytes=64)
+        q_table[1] = placed([P, T2], U32, "q_table1", "q_table1")
+
+        def load_pathb(b):
+            dram = pathb[b * GROUP : (b + 1) * GROUP, :].rearrange("(p t) j -> p t j", t=PACK)
+            if b == 1:
+                nc.sync.dma_start(score[b][:], dram)
+            else:
+                for h in range(2):
+                    nc.sync.dma_start(bias[b, h][:], dram[:, 2 * h : 2 * h + 2, :])
+
+        wc_raw = {}
+
+        def load_wc(b, g):
+            wc_raw[b, g] = placed([P, PACK, GROUP], F32, f"wc_raw{b}{g}", f"wc_raw{b}{g}")
+            nc.sync.dma_start(
+                wc_raw[b, g][:],
+                wc[b * GROUP : (b + 1) * GROUP, g * GROUP : (g + 1) * GROUP].rearrange("(p t) n -> p t n", t=PACK),
+            )
+
         load_words(q_table[1], tab2_words[1])
-        nc.sync.dma_start(trust_late[:, :, 0:PACK], trust_rows[:, 1:, :])
         load_pathb(0)
+        nc.sync.dma_start(trust_sb[:, :, 0:PACK], trust.rearrange("(b p t) -> p b t", p=P, t=PACK))
         load_pathb(1)
 
-        def gather_v(a, g):
-            if (a, g) == (KP - 1, SP - 1):
-                v_words[a, g] = late.tile([P, PACK, P], U32, name="v_words_last", tag="bias01", align_bytes=64)
-            else:
-                v_words[a, g] = held([P, PACK, P], U32, f"v_words{a}{g}")
+        v_words = {}
+
+        def gather_v(a, b, tile):
+            v_words[a, b] = tile
             nc.vector.tensor_copy(
-                v_words[a, g][:].rearrange("p t s -> p s t"), v_table[a][:].indirect(list1[:, 32 * g : 32 * (g + 1)])
+                v_words[a, b][:].rearrange("p t m -> p m t"),
+                v_table[a][:].indirect(list1[:, LIST_COLUMNS * b : LIST_COLUMNS * (b + 1)]),
             )
+
+        def v_tile(a, b):
+            return held([P, PACK, P], U32, f"v_words{a}{b}")
 
         banks = {}
 
-        def bank(b):
-            banks[b] = psum.tile([P, S2], F32, name=f"bank{b}")
-            return banks[b]
+        def accumulator(index, first):
+            if first:
+                banks[index] = psum.tile([P, S2], F32, name=f"bank{index}")
+            return banks[index]
 
-        def score_matmuls(g, a):
+        def score_bank(b, t):
+            return PACK * ((b + 1) % 2) + t
+
+        def score_passes(b, a):
+            v_plane = score_planes[:, a, S2 + b * GROUP : S2 + (b + 1) * GROUP]
             for t in range(PACK):
-                b = (4 * (g + 1) + t) % 8
-                acc = bank(b) if a == 0 else banks[b]
-                if True:
-                    nc.tensor.matmul_mx(
-                        out=acc[:],
-                        lhsT=v_words[a, g][:, t, :].bitcast(FP8X4),
-                        lhsT_scale=scale_planes[:, a, (g * PACK + t) * P : (g * PACK + t + 1) * P],
-                        rhs=q_words[a][:].bitcast(FP8X4),
-                        rhs_scale=scale_planes[:, a, S : S + S2],
-                        start=(a == 0),
-                        stop=(a == KP - 1),
-                    )
+                nc.tensor.matmul_mx(
+                    out=accumulator(score_bank(b, t), a == 0)[:],
+                    lhsT=v_words[a, b][:, t, :].bitcast(FP8X4),
+                    lhsT_scale=v_plane[:, t * P : (t + 1) * P],
+                    rhs=q_words[a][:].bitcast(FP8X4),
+                    rhs_scale=score_planes[:, a, 0:S2],
+                    start=(a == 0),
+                    stop=(a == K_GROUPS - 1),
+                )
 
         p_slices = {}
 
-        def relevance(g):
-            rounded = ring.tile([P, PACK, S2], BF16, name="p_slices", align_bytes=64, bufs=3)
-            p_slices[g] = rounded
+        def relevance(b):
+            p_slices[b] = ring.tile([P, PACK, S2], BF16, name="p_slices", align_bytes=64, bufs=I_GROUPS)
             for h in range(2):
                 for t in (2 * h, 2 * h + 1):
-                    nc.vector.tensor_tensor(
-                        score[g][:, t, :],
-                        banks[(4 * (g + 1) + t) % 8][:],
-                        bias[g, h][:, t % 2, :],
-                        ADD,
-                    )
-                z = score[g][:, 2 * h : 2 * h + 2, :]
-                nc.scalar.activation(z, z, SIGMOID)
+                    nc.vector.tensor_tensor(score[b][:, t, :], banks[score_bank(b, t)][:], bias[b, h][:, t % 2, :], ADD)
+                pair = score[b][:, 2 * h : 2 * h + 2, :]
+                nc.scalar.activation(pair, pair, SIGMOID)
             for t in range(PACK):
-                nc.scalar.activation(
-                    rounded[:, t, :],
-                    score[g][:, t, :],
-                    COPY,
-                    scale=(trust_sb[:, 0, t : t + 1] if g == 0 else trust_late[:, g - 1, t : t + 1]),
-                )
+                nc.scalar.activation(p_slices[b][:, t, :], score[b][:, t, :], COPY, scale=trust_sb[:, b, t : t + 1])
 
-        def weave_cols(engine_copy, woven, src, cols):
+        def weave_columns(engine_copy, woven, slices, cols):
             engine_copy(
-                woven[:, cols, :].rearrange("p (c i) t -> p c t i", i=4),
-                src[:, :, cols].rearrange("p t (c i) -> p c t i", i=4),
+                woven[:, cols, :].rearrange("p (c e) t -> p c t e", e=4),
+                slices[:, :, cols].rearrange("p t (c e) -> p c t e", e=4),
             )
 
-        def weave(src, name, tag):
-            woven = late.tile([P, S2, PACK], BF16, name=name, tag=tag, align_bytes=64)
+        def weave(slices, name, tag):
+            woven = placed([P, S2, PACK], BF16, name, tag)
             for h in range(2):
-                weave_cols(nc.vector.tensor_copy, woven, src, slice(h * HALF, (h + 1) * HALF))
-            return woven
-
-        def weave_shared(src, name, cut):
-            woven = ring.tile([P, S2, PACK], BF16, name=name, align_bytes=64)
-            weave_cols(nc.vector.tensor_copy, woven, src, slice(0, HALF))
-            weave_cols(nc.vector.tensor_copy, woven, src, slice(HALF, cut))
-            weave_cols(nc.scalar.copy, woven, src, slice(cut, S2))
-            return woven
+                weave_columns(nc.vector.tensor_copy, woven, slices, slice(h * HALF, (h + 1) * HALF))
+            return woven[:].rearrange("p j t -> p (j t)")
 
         def quantize(woven, name, parts):
             words = held([P, GROUP], U32, name + "_words")
@@ -221,160 +219,156 @@ def tile_list_code_search_context_kernel(
                 )
             return words, scales
 
-        wc_woven = {}
-        wc_q = {}
         p_q = {}
 
-        def round_wc(engine_copy, a, g, parts):
-            woven = late.tile([P, PACK, P, PACK], BF16, name=f"wc_woven{a}{g}", tag=f"wc_woven{(a + SP * g) % 4}", align_bytes=64)
-            for h in range(parts):
-                slots = slice(h * PACK // parts, (h + 1) * PACK // parts)
+        def quantize_p(b, tag):
+            woven = weave(p_slices[b], f"p_woven{b}", tag)
+            p_q[b] = quantize(woven, f"p{b}", 2)
+
+        wc_woven = {}
+        wc_q = {}
+
+        def round_wc(engine_copies, b, g):
+            place = (b + I_GROUPS * g) % WC_WOVEN_PLACES
+            wc_woven[b, g] = placed([P, PACK, P, PACK], BF16, f"wc_woven{b}{g}", f"wc_woven{place}")
+            share = PACK // len(engine_copies)
+            for h, engine_copy in enumerate(engine_copies):
+                slots = slice(h * share, (h + 1) * share)
                 engine_copy(
-                    woven[:, slots, :, :].rearrange("p t m j -> p m j t"),
-                    wc_raw[a, g][:].rearrange("p j (m t) -> p m j t", t=PACK)[:, :, :, slots],
+                    wc_woven[b, g][:, slots, :, :].rearrange("p s m t -> p m t s"),
+                    wc_raw[b, g][:].rearrange("p t (m s) -> p m t s", s=PACK)[:, :, :, slots],
                 )
-            wc_woven[a, g] = woven
 
-        def quantize_wc(a, g, parts):
-            wc_q[a, g] = quantize(wc_woven[a, g][:].rearrange("p t m j -> p (t m j)"), f"wc{a}{g}", parts)
+        def quantize_wc(b, g, parts=1):
+            woven = wc_woven[b, g][:].rearrange("p s m t -> p (s m t)")
+            wc_q[b, g] = quantize(woven, f"wc{b}{g}", parts)
 
-        wd_dealt = [held([P, PACK, SP, 2 * P], U8, f"wd_dealt{g}") for g in range(NG)]
+        wd_dealt = [held([P, PACK, I_GROUPS, 2 * P], U8, f"wd_dealt{g}") for g in range(N_GROUPS)]
 
         def deal_wd(g):
             nc.vector.tensor_copy(
                 wd_dealt[g][:].bitcast(U16),
-                wd_raw[:, :, 2 * g * GROUP : 2 * (g + 1) * GROUP].bitcast(U16).rearrange("p a (m t) -> p t a m", t=PACK),
+                wd_raw[:, :, 2 * g * GROUP : 2 * (g + 1) * GROUP].bitcast(U16).rearrange("p b (m t) -> p t b m", t=PACK),
             )
 
-        def doc_pass(g, t, a):
-            acc = bank(t) if a == 0 else banks[t]
+        def doc_pass(g, t, b):
             nc.tensor.matmul_mx(
-                out=acc[:],
-                lhsT=wd_dealt[g][:, t, a, :].bitcast(FP4X4),
-                lhsT_scale=wd_planes[:, g, (t * SP + a) * P : (t * SP + a + 1) * P],
-                rhs=p_q[a][0][:].bitcast(FP8X4),
-                rhs_scale=p_q[a][1][:],
-                start=(a == 0),
-                stop=(a == SP - 1),
+                out=accumulator(t, b == 0)[:],
+                lhsT=wd_dealt[g][:, t, b, :].bitcast(FP4X4),
+                lhsT_scale=wd_planes[:, g * I_GROUPS + b, t * P : (t + 1) * P],
+                rhs=p_q[b][0][:].bitcast(FP8X4),
+                rhs_scale=p_q[b][1][:],
+                start=(b == 0),
+                stop=(b == I_GROUPS - 1),
             )
 
-        def code_pass(g, t, a, first, last):
-            acc = bank(4 + t) if first else banks[4 + t]
-            words, scales = wc_q[a, g]
-            nc.tensor.matmul_mx(
-                out=acc[:],
-                lhsT=words[:, t * P : (t + 1) * P].bitcast(FP8X4),
-                lhsT_scale=scales[:, t * P : (t + 1) * P],
-                rhs=p_q[a][0][:].bitcast(FP8X4),
-                rhs_scale=p_q[a][1][:],
-                start=first,
-                stop=last,
-            )
-
-        def flat(woven):
-            return woven[:].rearrange("p j t -> p (j t)")
-
-        result = {}
-
-        def gate(g, t):
-            if t == 0:
-                result[g] = late.tile([P, PACK, S2], F32, name=f"result{g}", tag=("wc_raw10", "wc_raw11")[g], align_bytes=64)
-            nc.scalar.activation(result[g][:, t, :], banks[t][:], SIGMOID)
-
-        def gated(g, t):
-            y = result[g][:, t, :]
-            nc.vector.tensor_tensor(y, banks[4 + t][:], y, MULT)
-            nc.sync.dma_start(out_0[g * GROUP : (g + 1) * GROUP, :].rearrange("(p t) j -> p t j", t=PACK)[:, t, :], y)
-
-        def planes(g, woven):
-            words, scales = quantize(flat(woven), f"y{g}", 2)
-            nc.sync.dma_start(out_1[g].rearrange("p m t -> p (m t)").bitcast(I32), words[:].bitcast(I32))
-            for quad in range(4):
-                (nc.sync if quad < 2 or g == 0 else nc.scalar).dma_start(
-                    out_2[g, 4 * quad : 4 * quad + 4, :].bitcast(I32), scales[32 * quad : 32 * quad + 4, :].bitcast(I32)
+        def code_passes(g, b, first, last):
+            words, scales = wc_q[b, g]
+            for t in range(PACK):
+                nc.tensor.matmul_mx(
+                    out=accumulator(PACK + t, first)[:],
+                    lhsT=words[:, t * P : (t + 1) * P].bitcast(FP8X4),
+                    lhsT_scale=scales[:, t * P : (t + 1) * P],
+                    rhs=p_q[b][0][:].bitcast(FP8X4),
+                    rhs_scale=p_q[b][1][:],
+                    start=first,
+                    stop=last,
                 )
 
-        woven = {}
-        for g in range(SP):
-            gather_v(0, g)
-        wd_staged = keep.tile([P, S], U8, name="wd_staged", tag="v_table0", align_bytes=64)
-        nc.vector.tensor_copy(
-            wd_staged[:].rearrange("p (t a m) -> p t a m", t=PACK, a=SP),
-            wd_raw_scales[:].rearrange("p a (m t) -> p t a m", t=PACK),
-        )
-        for quad in (0, 2, 1, 3):
+        def gates(gate):
+            for t in range(PACK):
+                nc.scalar.activation(gate[:, t, :], banks[t][:], SIGMOID)
+
+        def products(g, y):
+            dram = out_0[g * GROUP : (g + 1) * GROUP, :].rearrange("(p t) j -> p t j", t=PACK)
+            for t in range(PACK):
+                nc.vector.tensor_tensor(y[:, t, :], banks[PACK + t][:], y[:, t, :], MULT)
+                nc.sync.dma_start(dram[:, t, :], y[:, t, :])
+
+        def store_planes(g, woven, word_stores, scale_queues):
+            words, scales = quantize(woven, f"y{g}", 2)
+            width = S2 // word_stores
+            for h in range(word_stores):
+                cols = slice(h * width, (h + 1) * width)
+                nc.sync.dma_start(
+                    out_1[g].rearrange("p m t -> p (m t)").bitcast(I32)[:, cols], words[:, cols].bitcast(I32)
+                )
+            for quad, queue in enumerate(scale_queues):
+                queue.dma_start(
+                    out_2[g, 4 * quad : 4 * quad + 4, :].bitcast(I32),
+                    scales[QUADRANT * quad : QUADRANT * quad + 4, :].bitcast(I32),
+                )
+
+        for b in range(I_GROUPS):
+            gather_v(0, b, v_tile(0, b))
+        wd_staged = keep.tile([P, PACK, P], U8, name="wd_staged", tag="v_table0", align_bytes=64)
+        nc.vector.tensor_copy(wd_staged[:], wd_raw_scales[:].rearrange("p (m t) -> p t m", t=PACK))
+        rows = WD_ROWS // 4
+        for quad in QUADRANT_ORDER:
             nc.sync.dma_start(
-                wd_planes[32 * quad : 32 * quad + 4, :, :].bitcast(I32),
-                wd_staged[32 * quad : 32 * quad + 32 : 4, :].bitcast(I32),
+                wd_planes[QUADRANT * quad : QUADRANT * quad + 4, :, :].bitcast(I32),
+                wd_staged[rows * quad : rows * (quad + 1), :, :].rearrange("p t m -> p (t m)").bitcast(I32),
             )
-        nc.sync.dma_start(wd_raw[:].bitcast(I32), wd_words.rearrange("a p n -> p a n").bitcast(I32))
+        nc.sync.dma_start(wd_raw[:].bitcast(I32), wd_words.rearrange("b p n -> p b n").bitcast(I32))
         load_pathb(2)
-        load_wc(0, 0)
-        load_wc(1, 0)
-        load_wc(2, 0)
-        load_wc(2, 1)
-        load_wc(0, 1)
-        load_wc(1, 1)
-        score_matmuls(0, 0)
-        score_matmuls(1, 0)
-        gather_v(1, 0)
-        gather_v(1, 1)
+        for b, g in ((0, 0), (1, 0), (2, 0), (2, 1), (0, 1), (1, 1)):
+            load_wc(b, g)
+
+        score_passes(0, 0)
+        for b in range(2):
+            gather_v(1, b, v_tile(1, b))
         nc.vector.tensor_copy(q_words[1][:], q_table[1][:].indirect(list2[:]))
-        score_matmuls(0, 1)
-        score_matmuls(1, 1)
+        score_passes(0, 1)
+        score_passes(1, 0)
+        score_passes(1, 1)
         relevance(0)
-        gather_v(1, 2)
+        gather_v(1, 2, placed([P, PACK, P], U32, "v_words12", "bias01"))
         relevance(1)
-        score_matmuls(2, 0)
-        score_matmuls(2, 1)
+        score_passes(2, 0)
+        score_passes(2, 1)
         deal_wd(0)
         deal_wd(1)
         relevance(2)
-        woven["p", 0] = weave(p_slices[0], "p_woven0", "bias20")
-        p_q[0] = quantize(flat(woven["p", 0]), "p0", 2)
-        for t in range(PACK):
-            doc_pass(0, t, 0)
-        woven["p", 1] = weave(p_slices[1], "p_woven1", "bias21")
-        p_q[1] = quantize(flat(woven["p", 1]), "p1", 2)
-        for t in range(PACK):
-            doc_pass(0, t, 1)
-        round_wc(nc.vector.tensor_copy, 0, 0, 2)
-        quantize_wc(0, 0, 2)
-        for t in range(PACK):
-            code_pass(0, t, 0, True, False)
-        woven["p", 2] = weave(p_slices[2], "p_woven2", "bias20")
-        p_q[2] = quantize(flat(woven["p", 2]), "p2", 2)
+
+        for b in range(2):
+            quantize_p(b, f"bias2{b}")
+            for t in range(PACK):
+                doc_pass(0, t, b)
+        round_wc([nc.vector.tensor_copy] * 2, 0, 0)
+        quantize_wc(0, 0, parts=2)
+        code_passes(0, 0, True, False)
+        quantize_p(2, "bias20")
         for t in range(PACK):
             doc_pass(0, t, 2)
-        round_wc(nc.scalar.copy, 1, 0, 1)
-        round_wc(nc.vector.tensor_copy, 2, 0, 2)
-        quantize_wc(1, 0, 1)
+        round_wc([nc.scalar.copy], 1, 0)
+        round_wc([nc.vector.tensor_copy] * 2, 2, 0)
+        quantize_wc(1, 0)
+        code_passes(0, 1, False, False)
+        y0 = placed([P, PACK, S2], F32, "y0", "wc_raw10")
+        gates(y0)
+        quantize_wc(2, 0, parts=2)
+        code_passes(0, 2, False, True)
+
         for t in range(PACK):
-            code_pass(0, t, 1, False, False)
-        for t in range(PACK):
-            gate(0, t)
-        quantize_wc(2, 0, 2)
-        for t in range(PACK):
-            code_pass(0, t, 2, False, True)
-        for t in range(PACK):
-            for a in range(SP):
-                doc_pass(1, t, a)
-        round_wc(nc.vector.tensor_copy, 2, 1, 2)
-        quantize_wc(2, 1, 2)
-        round_wc(nc.scalar.copy, 0, 1, 1)
-        round_wc(nc.scalar.copy, 1, 1, 1)
-        for t in range(PACK):
-            gated(0, t)
-        quantize_wc(0, 1, 1)
-        woven["y", 0] = weave(result[0], "y_woven0", "wc_raw01")
-        quantize_wc(1, 1, 1)
-        planes(0, woven["y", 0])
-        for a in (2, 0, 1):
-            for t in range(PACK):
-                code_pass(1, t, a, a == 2, a == 1)
-        for t in range(PACK):
-            gate(1, t)
-        for t in range(PACK):
-            gated(1, t)
-        woven["y", 1] = weave_shared(result[1], "y_woven", 320)
-        planes(1, woven["y", 1])
+            for b in range(I_GROUPS):
+                doc_pass(1, t, b)
+        round_wc([nc.vector.tensor_copy] * 2, 2, 1)
+        quantize_wc(2, 1, parts=2)
+        round_wc([nc.scalar.copy], 0, 1)
+        round_wc([nc.scalar.copy], 1, 1)
+        products(0, y0)
+        quantize_wc(0, 1)
+        y0_woven = weave(y0, "y0_woven", "wc_raw01")
+        quantize_wc(1, 1)
+        store_planes(0, y0_woven, 1, [nc.sync] * 4)
+        code_passes(1, 2, True, False)
+        code_passes(1, 0, False, False)
+        code_passes(1, 1, False, True)
+        y1 = placed([P, PACK, S2], F32, "y1", "wc_raw11")
+        gates(y1)
+        products(1, y1)
+        y1_woven = ring.tile([P, S2, PACK], BF16, name="y1_woven", align_bytes=64)
+        weave_columns(nc.vector.tensor_copy, y1_woven, y1, slice(0, HALF))
+        weave_columns(nc.vector.tensor_copy, y1_woven, y1, slice(HALF, LAST_WEAVE_VECTOR_COLUMNS))
+        weave_columns(nc.scalar.copy, y1_woven, y1, slice(LAST_WEAVE_VECTOR_COLUMNS, S2))
+        store_planes(1, y1_woven[:].rearrange("p j t -> p (j t)"), 2, [nc.sync, nc.sync, nc.scalar, nc.scalar])

@@ -54,60 +54,66 @@ def tile_list_code_search_context_kernel(
         list1 = keep.tile([P, S // 16], U16, name="list1")
         list2 = keep.tile([P, S2 // 16], U16, name="list2")
         v_table = [held([P, T], U32, f"v_table{a}") for a in range(K_GROUPS)]
-        q_table = {}
+        q_table = {0: held([P, T2], U32, "q_table0")}
         staged = held([P, S + S2], U8, "staged")
         score_planes = held([P, K_GROUPS, S2 + S], U8, "score_planes")
         wd_planes = held([P, N_GROUPS * I_GROUPS, GROUP], U8, "wd_planes")
+        q_words = [held([P, S2], U32, f"q_words{a}") for a in range(K_GROUPS)]
         wd_raw_scales = held([P, GROUP], U8, "wd_raw_scales")
-        q_words = {1: held([P, S2], U32, "q_words1")}
-        v_picked_scales = keep.tile([P, S], U8, name="v_picked_scales", tag="q_words0", align_bytes=64)
+        v_words = {}
+
+        def gather_v(a, b, tag=None, pool=keep):
+            name = f"v_words{a}{b}"
+            v_words[a, b] = pool.tile([P, PACK, P], U32, name=name, tag=tag or name, align_bytes=64)
+            nc.vector.tensor_copy(
+                v_words[a, b][:].rearrange("p t m -> p m t"),
+                v_table[a][:].indirect(list1[:, LIST_COLUMNS * b : LIST_COLUMNS * (b + 1)]),
+            )
 
         with tc.tile_pool(name="head", bufs=1) as head:
             v_table_scales = head.tile([P, T], U8, name="v_table_scales", align_bytes=64)
             q_table_scales = head.tile([P, T2], U8, name="q_table_scales", align_bytes=64)
-            q_table[0] = head.tile([P, T2], U32, name="q_table0", align_bytes=64)
+            v_picked_scales = head.tile([P, S], U8, name="v_picked_scales", align_bytes=64)
             q_picked_scales = head.tile([P, S2], U8, name="q_picked_scales", align_bytes=64)
 
             warm = held([P, 2], F32, "warm")
             nc.vector.memset(warm[:], 0.0)
             nc.scalar.activation(warm[:, 1:2], warm[:, 0:1], SIGMOID)
 
-            for window in (v_table_scales, q_table_scales):
+            for window in (q_table_scales, v_table_scales):
                 nc.vector.memset(window[0:TABLE_ROW0, :].bitcast(I32), 0)
             nc.vector.memset(wd_raw_scales[WD_ROWS:P, :].bitcast(I32), 0)
             for planes in (score_planes, wd_planes):
-                nc.vector.memset(planes[:].rearrange("p c n -> p (c n)").bitcast(I32), 0)
+                nc.gpsimd.memset(planes[:].rearrange("p c n -> p (c n)").bitcast(I32), 0)
 
             def load_table_scales(sb, dram):
                 nc.sync.dma_start(sb[TABLE_ROW0:P, :].bitcast(I32), dram.rearrange("a q t -> q a t").bitcast(I32))
 
-            nc.sync.dma_start(list1[:], offs)
-            load_table_scales(v_table_scales, tab_scales)
             nc.sync.dma_start(list2[:], offs2)
             load_table_scales(q_table_scales, tab2_scales)
-            load_words(q_table[0], tab2_words[0])
+            nc.sync.dma_start(list1[:], offs)
+            load_table_scales(v_table_scales, tab_scales)
             load_words(v_table[0], tab_words[0])
             load_words(v_table[1], tab_words[1])
+            load_words(q_table[0], tab2_words[0])
             nc.sync.dma_start(
                 wd_raw_scales[0:WD_ROWS, :].bitcast(I32),
                 wd_scales.rearrange("b q (g c) -> (q g) b c", g=N_GROUPS).bitcast(I32),
             )
 
-            nc.vector.tensor_copy(v_picked_scales[:], v_table_scales[:].indirect(list1[:]))
             nc.vector.tensor_copy(q_picked_scales[:], q_table_scales[:].indirect(list2[:]))
+            nc.vector.tensor_copy(v_picked_scales[:], v_table_scales[:].indirect(list1[:]))
+            nc.vector.tensor_copy(staged[:, 0:S2].bitcast(U32), q_picked_scales[:].bitcast(U32))
             nc.vector.tensor_copy(
                 staged[:, S2:].rearrange("p (b t m) -> p t b m", b=I_GROUPS, t=PACK),
                 v_picked_scales[:].rearrange("p (b m t) -> p t b m", m=P, t=PACK),
             )
-            nc.vector.tensor_copy(staged[:, 0:S2].bitcast(U32), q_picked_scales[:].bitcast(U32))
             rows = TABLE_ROWS // 4
             for quad in QUADRANT_ORDER:
-                nc.scalar.dma_start(
+                nc.sync.dma_start(
                     score_planes[QUADRANT * quad : QUADRANT * quad + 4, :, :].bitcast(I32),
                     staged[TABLE_ROW0 + rows * quad : TABLE_ROW0 + rows * (quad + 1), :].bitcast(I32),
                 )
-            q_words[0] = keep.tile([P, S2], U32, name="q_words0", tag="q_words0", align_bytes=64)
-            nc.vector.tensor_copy(q_words[0][:], q_table[0][:].indirect(list2[:]))
 
         late = ctx.enter_context(tc.tile_pool(name="late", bufs=1))
 
@@ -148,18 +154,6 @@ def tile_list_code_search_context_kernel(
         nc.sync.dma_start(trust_sb[:, :, 0:PACK], trust.rearrange("(b p t) -> p b t", p=P, t=PACK))
         load_pathb(1)
 
-        v_words = {}
-
-        def gather_v(a, b, tile):
-            v_words[a, b] = tile
-            nc.vector.tensor_copy(
-                v_words[a, b][:].rearrange("p t m -> p m t"),
-                v_table[a][:].indirect(list1[:, LIST_COLUMNS * b : LIST_COLUMNS * (b + 1)]),
-            )
-
-        def v_tile(a, b):
-            return held([P, PACK, P], U32, f"v_words{a}{b}")
-
         banks = {}
 
         def accumulator(index, first):
@@ -170,17 +164,17 @@ def tile_list_code_search_context_kernel(
         def score_bank(b, t):
             return PACK * ((b + 1) % 2) + t
 
-        def score_passes(b, a):
+        def score_passes(b, a, first):
             v_plane = score_planes[:, a, S2 + b * GROUP : S2 + (b + 1) * GROUP]
             for t in range(PACK):
                 nc.tensor.matmul_mx(
-                    out=accumulator(score_bank(b, t), a == 0)[:],
+                    out=accumulator(score_bank(b, t), first)[:],
                     lhsT=v_words[a, b][:, t, :].bitcast(FP8X4),
                     lhsT_scale=v_plane[:, t * P : (t + 1) * P],
                     rhs=q_words[a][:].bitcast(FP8X4),
                     rhs_scale=score_planes[:, a, 0:S2],
-                    start=(a == 0),
-                    stop=(a == K_GROUPS - 1),
+                    start=first,
+                    stop=not first,
                 )
 
         p_slices = {}
@@ -300,7 +294,7 @@ def tile_list_code_search_context_kernel(
                 )
 
         for b in range(I_GROUPS):
-            gather_v(0, b, v_tile(0, b))
+            gather_v(0, b)
         wd_staged = keep.tile([P, PACK, P], U8, name="wd_staged", tag="v_table0", align_bytes=64)
         nc.vector.tensor_copy(wd_staged[:], wd_raw_scales[:].rearrange("p (m t) -> p t m", t=PACK))
         rows = WD_ROWS // 4
@@ -314,18 +308,19 @@ def tile_list_code_search_context_kernel(
         for b, g in ((0, 0), (1, 0), (2, 0), (2, 1), (0, 1), (1, 1)):
             load_wc(b, g)
 
-        score_passes(0, 0)
-        for b in range(2):
-            gather_v(1, b, v_tile(1, b))
+        gather_v(1, 0)
+        nc.vector.tensor_copy(q_words[0][:], q_table[0][:].indirect(list2[:]))
+        gather_v(1, 1, "q_table0")
         nc.vector.tensor_copy(q_words[1][:], q_table[1][:].indirect(list2[:]))
-        score_passes(0, 1)
-        score_passes(1, 0)
-        score_passes(1, 1)
+        score_passes(0, 0, True)
+        score_passes(0, 1, False)
+        score_passes(1, 1, True)
+        score_passes(1, 0, False)
         relevance(0)
-        gather_v(1, 2, placed([P, PACK, P], U32, "v_words12", "bias01"))
+        gather_v(1, 2, "bias01", late)
         relevance(1)
-        score_passes(2, 0)
-        score_passes(2, 1)
+        score_passes(2, 0, True)
+        score_passes(2, 1, False)
         deal_wd(0)
         deal_wd(1)
         relevance(2)

@@ -42,7 +42,6 @@ def tile_list_code_search_context_kernel(
     nc = tc.nc
     with ExitStack() as ctx:
         keep = ctx.enter_context(tc.tile_pool(name="keep", bufs=1))
-        ring = ctx.enter_context(tc.tile_pool(name="ring", bufs=2))
         psum = ctx.enter_context(tc.psum_pool(name="psum", bufs=1))
 
         def held(shape, dtype, name):
@@ -180,14 +179,25 @@ def tile_list_code_search_context_kernel(
         p_slices = {}
 
         def relevance(b):
-            p_slices[b] = ring.tile([P, PACK, S2], BF16, name="p_slices", align_bytes=64, bufs=I_GROUPS)
             for h in range(2):
                 for t in (2 * h, 2 * h + 1):
                     nc.vector.tensor_tensor(score[b][:, t, :], banks[score_bank(b, t)][:], bias[b, h][:, t % 2, :], ADD)
                 pair = score[b][:, 2 * h : 2 * h + 2, :]
                 nc.scalar.activation(pair, pair, SIGMOID)
-            for t in range(PACK):
-                nc.scalar.activation(p_slices[b][:, t, :], score[b][:, t, :], COPY, scale=trust_sb[:, b, t : t + 1])
+
+        def on_scalar(out, in_, factor):
+            nc.scalar.activation(out, in_, COPY, scale=factor)
+
+        def on_gpsimd(out, in_, factor):
+            nc.gpsimd.tensor_scalar(out, in_, factor, 0.0, MULT, ADD)
+
+        def on_vector(out, in_, factor):
+            nc.vector.tensor_scalar(out, in_, factor, None, MULT)
+
+        def trust_products(b, engines, tile):
+            p_slices[b] = tile
+            for t, product in enumerate(engines):
+                product(tile[:, t, :], score[b][:, t, :], trust_sb[:, b, t : t + 1])
 
         def weave_columns(engine_copy, woven, slices, cols):
             engine_copy(
@@ -222,9 +232,8 @@ def tile_list_code_search_context_kernel(
         wc_woven = {}
         wc_q = {}
 
-        def round_wc(engine_copies, b, g):
-            place = (b + I_GROUPS * g) % WC_WOVEN_PLACES
-            wc_woven[b, g] = placed([P, PACK, P, PACK], BF16, f"wc_woven{b}{g}", f"wc_woven{place}")
+        def round_wc(engine_copies, b, g, tag):
+            wc_woven[b, g] = placed([P, PACK, P, PACK], BF16, f"wc_woven{b}{g}", tag)
             share = PACK // len(engine_copies)
             for h, engine_copy in enumerate(engine_copies):
                 slots = slice(h * share, (h + 1) * share)
@@ -237,9 +246,10 @@ def tile_list_code_search_context_kernel(
             woven = wc_woven[b, g][:].rearrange("p s m t -> p (s m t)")
             wc_q[b, g] = quantize(woven, f"wc{b}{g}", parts)
 
-        wd_dealt = [held([P, PACK, I_GROUPS, 2 * P], U8, f"wd_dealt{g}") for g in range(N_GROUPS)]
+        wd_dealt = {}
 
-        def deal_wd(g):
+        def deal_wd(g, tile):
+            wd_dealt[g] = tile
             nc.vector.tensor_copy(
                 wd_dealt[g][:].bitcast(U16),
                 wd_raw[:, :, 2 * g * GROUP : 2 * (g + 1) * GROUP].bitcast(U16).rearrange("p b (m t) -> p t b m", t=PACK),
@@ -273,10 +283,10 @@ def tile_list_code_search_context_kernel(
             for t in range(PACK):
                 nc.scalar.activation(gate[:, t, :], banks[t][:], SIGMOID)
 
-        def products(g, y):
+        def products(g, y, gate):
             dram = out_0[g * GROUP : (g + 1) * GROUP, :].rearrange("(p t) j -> p t j", t=PACK)
             for t in range(PACK):
-                nc.vector.tensor_tensor(y[:, t, :], banks[PACK + t][:], y[:, t, :], MULT)
+                nc.vector.tensor_tensor(y[:, t, :], banks[PACK + t][:], gate[:, t, :], MULT)
                 nc.sync.dma_start(dram[:, t, :], y[:, t, :])
 
         def store_planes(g, woven, word_stores, scale_queues):
@@ -297,6 +307,7 @@ def tile_list_code_search_context_kernel(
             gather_v(0, b)
         wd_staged = keep.tile([P, PACK, P], U8, name="wd_staged", tag="v_table0", align_bytes=64)
         nc.vector.tensor_copy(wd_staged[:], wd_raw_scales[:].rearrange("p (m t) -> p t m", t=PACK))
+        load_pathb(2)
         rows = WD_ROWS // 4
         for quad in QUADRANT_ORDER:
             nc.sync.dma_start(
@@ -304,65 +315,63 @@ def tile_list_code_search_context_kernel(
                 wd_staged[rows * quad : rows * (quad + 1), :, :].rearrange("p t m -> p (t m)").bitcast(I32),
             )
         nc.sync.dma_start(wd_raw[:].bitcast(I32), wd_words.rearrange("b p n -> p b n").bitcast(I32))
-        load_pathb(2)
-        for b, g in ((0, 0), (1, 0), (2, 0), (2, 1), (0, 1), (1, 1)):
-            load_wc(b, g)
+        for g in range(N_GROUPS):
+            for b in range(I_GROUPS):
+                load_wc(b, g)
 
         gather_v(1, 0)
         nc.vector.tensor_copy(q_words[0][:], q_table[0][:].indirect(list2[:]))
         gather_v(1, 1, "q_table0")
         nc.vector.tensor_copy(q_words[1][:], q_table[1][:].indirect(list2[:]))
+        gather_v(1, 2, "q_table1", late)
         score_passes(0, 0, True)
         score_passes(0, 1, False)
         score_passes(1, 1, True)
         score_passes(1, 0, False)
         relevance(0)
-        gather_v(1, 2, "bias01", late)
+        trust_products(0, [on_gpsimd] * 4, held([P, PACK, S2], BF16, "p_slices0"))
         relevance(1)
         score_passes(2, 0, True)
         score_passes(2, 1, False)
-        deal_wd(0)
-        deal_wd(1)
         relevance(2)
+        trust_products(1, [on_gpsimd] * 4, held([P, PACK, S2], BF16, "p_slices1"))
 
-        for b in range(2):
-            quantize_p(b, f"bias2{b}")
-            for t in range(PACK):
-                doc_pass(0, t, b)
-        round_wc([nc.vector.tensor_copy] * 2, 0, 0)
-        quantize_wc(0, 0, parts=2)
-        code_passes(0, 0, True, False)
-        quantize_p(2, "bias20")
+        deal_wd(0, held([P, PACK, I_GROUPS, 2 * P], U8, "wd_dealt0"))
+        quantize_p(0, "bias20")
         for t in range(PACK):
-            doc_pass(0, t, 2)
-        round_wc([nc.scalar.copy], 1, 0)
-        round_wc([nc.vector.tensor_copy] * 2, 2, 0)
-        quantize_wc(1, 0)
-        code_passes(0, 1, False, False)
-        y0 = placed([P, PACK, S2], F32, "y0", "wc_raw10")
-        gates(y0)
-        quantize_wc(2, 0, parts=2)
-        code_passes(0, 2, False, True)
+            doc_pass(0, t, 0)
+        trust_products(2, [on_vector] * 4, held([P, PACK, S2], BF16, "p_slices2"))
+        for b in range(I_GROUPS):
+            round_wc([nc.scalar.copy], b, 0, f"woven{b}")
+            quantize_wc(b, 0)
+            code_passes(0, b, b == 0, b == I_GROUPS - 1)
+            if b + 1 < I_GROUPS:
+                quantize_p(b + 1, f"woven{b}")
+                for t in range(PACK):
+                    doc_pass(0, t, b + 1)
+        deal_wd(1, placed([P, PACK, I_GROUPS, 2 * P], U8, "wd_dealt1", "woven2"))
+        round_wc([nc.scalar.copy], 0, 1, "woven0")
+        gate0 = placed([P, PACK, S2], F32, "gate0", "wc_raw01")
+        gates(gate0)
 
         for t in range(PACK):
             for b in range(I_GROUPS):
                 doc_pass(1, t, b)
-        round_wc([nc.vector.tensor_copy] * 2, 2, 1)
-        quantize_wc(2, 1, parts=2)
-        round_wc([nc.scalar.copy], 0, 1)
-        round_wc([nc.scalar.copy], 1, 1)
-        products(0, y0)
         quantize_wc(0, 1)
-        y0_woven = weave(y0, "y0_woven", "wc_raw01")
-        quantize_wc(1, 1)
+        round_wc([nc.vector.tensor_copy] * 2, 1, 1, "woven3")
+        quantize_wc(1, 1, parts=2)
+        round_wc([nc.scalar.copy], 2, 1, "woven1")
+        y0 = placed([P, PACK, S2], F32, "y0", "wc_raw11")
+        products(0, y0, gate0)
+        quantize_wc(2, 1)
+        y0_woven = weave(y0, "y0_woven", "woven1")
         store_planes(0, y0_woven, 1, [nc.sync] * 4)
-        code_passes(1, 2, True, False)
-        code_passes(1, 0, False, False)
-        code_passes(1, 1, False, True)
-        y1 = placed([P, PACK, S2], F32, "y1", "wc_raw11")
+        for b in range(I_GROUPS):
+            code_passes(1, b, b == 0, b == I_GROUPS - 1)
+        y1 = placed([P, PACK, S2], F32, "y1", "wc_raw21")
         gates(y1)
-        products(1, y1)
-        y1_woven = ring.tile([P, S2, PACK], BF16, name="y1_woven", align_bytes=64)
+        products(1, y1, y1)
+        y1_woven = held([P, S2, PACK], BF16, "y1_woven")
         weave_columns(nc.vector.tensor_copy, y1_woven, y1, slice(0, HALF))
         weave_columns(nc.vector.tensor_copy, y1_woven, y1, slice(HALF, LAST_WEAVE_VECTOR_COLUMNS))
         weave_columns(nc.scalar.copy, y1_woven, y1, slice(LAST_WEAVE_VECTOR_COLUMNS, S2))

@@ -32,7 +32,7 @@ TABLE_ROW0 = P - TABLE_ROWS
 WD_ROWS = 16 * N_GROUPS * I_GROUPS
 QUADRANT_ORDER = (0, 2, 1, 3)
 LAST_WEAVE_VECTOR_COLUMNS = 320
-WC_WOVEN_PLACES = 4
+LAST_ROUNDING_VECTOR_COLUMNS = 88
 
 
 def tile_list_code_search_context_kernel(
@@ -232,15 +232,16 @@ def tile_list_code_search_context_kernel(
         wc_woven = {}
         wc_q = {}
 
-        def round_wc(engine_copies, b, g, tag):
+        def round_wc(b, g, tag, on_vector):
             wc_woven[b, g] = placed([P, PACK, P, PACK], BF16, f"wc_woven{b}{g}", tag)
-            share = PACK // len(engine_copies)
-            for h, engine_copy in enumerate(engine_copies):
-                slots = slice(h * share, (h + 1) * share)
-                engine_copy(
-                    wc_woven[b, g][:, slots, :, :].rearrange("p s m t -> p m t s"),
-                    wc_raw[b, g][:].rearrange("p t (m s) -> p m t s", s=PACK)[:, :, :, slots],
-                )
+            woven = wc_woven[b, g][:].rearrange("p s m t -> p m t s")
+            raw = wc_raw[b, g][:].rearrange("p t (m s) -> p m t s", s=PACK)
+            if on_vector < P:
+                nc.scalar.copy(woven[:, on_vector:, :, :], raw[:, on_vector:, :, :])
+            if on_vector > 0:
+                for h in range(2):
+                    slots = slice(2 * h, 2 * h + 2)
+                    nc.vector.tensor_copy(woven[:, :on_vector, :, slots], raw[:, :on_vector, :, slots])
 
         def quantize_wc(b, g, parts=1):
             woven = wc_woven[b, g][:].rearrange("p s m t -> p (s m t)")
@@ -334,37 +335,45 @@ def tile_list_code_search_context_kernel(
         score_passes(2, 0, True)
         score_passes(2, 1, False)
         relevance(2)
-        trust_products(1, [on_gpsimd] * 4, held([P, PACK, S2], BF16, "p_slices1"))
+        for b in (1, 2):
+            trust_products(b, [on_scalar] * 4, placed([P, PACK, S2], BF16, f"p_slices{b}", f"p_slices{b}"))
+
+        def doc_passes(g, b):
+            for t in range(PACK):
+                doc_pass(g, t, b)
 
         deal_wd(0, held([P, PACK, I_GROUPS, 2 * P], U8, "wd_dealt0"))
         quantize_p(0, "bias20")
-        for t in range(PACK):
-            doc_pass(0, t, 0)
-        trust_products(2, [on_vector] * 4, held([P, PACK, S2], BF16, "p_slices2"))
-        for b in range(I_GROUPS):
-            round_wc([nc.scalar.copy], b, 0, f"woven{b}")
-            quantize_wc(b, 0)
-            code_passes(0, b, b == 0, b == I_GROUPS - 1)
-            if b + 1 < I_GROUPS:
-                quantize_p(b + 1, f"woven{b}")
-                for t in range(PACK):
-                    doc_pass(0, t, b + 1)
-        deal_wd(1, placed([P, PACK, I_GROUPS, 2 * P], U8, "wd_dealt1", "woven2"))
-        round_wc([nc.scalar.copy], 0, 1, "woven0")
-        gate0 = placed([P, PACK, S2], F32, "gate0", "wc_raw01")
+        doc_passes(0, 0)
+        round_wc(0, 0, "woven0", on_vector=P)
+        quantize_wc(0, 0, parts=2)
+        code_passes(0, 0, True, False)
+        quantize_p(1, "woven0")
+        doc_passes(0, 1)
+        quantize_p(2, "p_slices1")
+        doc_passes(0, 2)
+        round_wc(1, 0, "woven1", on_vector=0)
+        quantize_wc(1, 0)
+        code_passes(0, 1, False, False)
+        deal_wd(1, placed([P, PACK, I_GROUPS, 2 * P], U8, "wd_dealt1", "woven1"))
+        round_wc(2, 0, "woven2", on_vector=0)
+        gate0 = placed([P, PACK, S2], F32, "gate0", "wc_raw20")
         gates(gate0)
+        round_wc(0, 1, "woven0", on_vector=P)
+        quantize_wc(2, 0)
+        code_passes(0, 2, False, True)
+        quantize_wc(0, 1, parts=2)
 
         for t in range(PACK):
             for b in range(I_GROUPS):
                 doc_pass(1, t, b)
-        quantize_wc(0, 1)
-        round_wc([nc.vector.tensor_copy] * 2, 1, 1, "woven3")
-        quantize_wc(1, 1, parts=2)
-        round_wc([nc.scalar.copy], 2, 1, "woven1")
-        y0 = placed([P, PACK, S2], F32, "y0", "wc_raw11")
+        round_wc(1, 1, "woven3", on_vector=0)
+        y0 = placed([P, PACK, S2], F32, "y0", "wc_raw01")
         products(0, y0, gate0)
-        quantize_wc(2, 1)
-        y0_woven = weave(y0, "y0_woven", "woven1")
+        round_wc(2, 1, "woven2", on_vector=LAST_ROUNDING_VECTOR_COLUMNS)
+        quantize_wc(1, 1)
+        quantize_wc(2, 1, parts=2)
+        y0_woven = weave(y0, "y0_woven", "woven2")
         store_planes(0, y0_woven, 1, [nc.sync] * 4)
         for b in range(I_GROUPS):
             code_passes(1, b, b == 0, b == I_GROUPS - 1)

@@ -75,10 +75,6 @@ def tile_list_code_search_context_kernel(
             v_picked_scales = head.tile([P, S], U8, name="v_picked_scales", align_bytes=64)
             q_picked_scales = head.tile([P, S2], U8, name="q_picked_scales", align_bytes=64)
 
-            warm = held([P, 2], F32, "warm")
-            nc.vector.memset(warm[:], 0.0)
-            nc.scalar.activation(warm[:, 1:2], warm[:, 0:1], SIGMOID)
-
             for window in (q_table_scales, v_table_scales):
                 nc.vector.memset(window[0:TABLE_ROW0, :].bitcast(I32), 0)
             nc.vector.memset(wd_raw_scales[WD_ROWS:P, :].bitcast(I32), 0)
@@ -127,7 +123,7 @@ def tile_list_code_search_context_kernel(
         ]
         for h in range(2):
             bias[1, h] = score[1][:, 2 * h : 2 * h + 2, :]
-        wd_raw = late.tile([P, I_GROUPS, 2 * N], U8, name="wd_raw", align_bytes=64)
+        wd_raw = placed([P, I_GROUPS, 2 * N], U8, "wd_raw", "wd_raw")
         trust_sb = late.tile([P, I_GROUPS, 2 * PACK], F32, name="trust_sb", align_bytes=64)
         q_table[1] = placed([P, T2], U32, "q_table1", "q_table1")
 
@@ -249,17 +245,18 @@ def tile_list_code_search_context_kernel(
 
         wd_dealt = {}
 
-        def deal_wd(g, tile):
-            wd_dealt[g] = tile
+        def deal_wd():
+            dealt = placed([P, N_GROUPS, PACK, I_GROUPS, 2 * P], U8, "wd_dealt", "p_slices0")
             nc.vector.tensor_copy(
-                wd_dealt[g][:].bitcast(U16),
-                wd_raw[:, :, 2 * g * GROUP : 2 * (g + 1) * GROUP].bitcast(U16).rearrange("p b (m t) -> p t b m", t=PACK),
+                dealt[:].bitcast(U16),
+                wd_raw[:].bitcast(U16).rearrange("p b (g m t) -> p g t b m", g=N_GROUPS, t=PACK),
             )
+            wd_dealt[0] = dealt
 
         def doc_pass(g, t, b):
             nc.tensor.matmul_mx(
-                out=accumulator(t, b == 0)[:],
-                lhsT=wd_dealt[g][:, t, b, :].bitcast(FP4X4),
+                out=accumulator(PACK * g + t, b == 0)[:],
+                lhsT=wd_dealt[0][:, g, t, b, :].bitcast(FP4X4),
                 lhsT_scale=wd_planes[:, g * I_GROUPS + b, t * P : (t + 1) * P],
                 rhs=p_q[b][0][:].bitcast(FP8X4),
                 rhs_scale=p_q[b][1][:],
@@ -271,7 +268,7 @@ def tile_list_code_search_context_kernel(
             words, scales = wc_q[b, g]
             for t in range(PACK):
                 nc.tensor.matmul_mx(
-                    out=accumulator(PACK + t, first)[:],
+                    out=accumulator(PACK * (1 - g) + t, first)[:],
                     lhsT=words[:, t * P : (t + 1) * P].bitcast(FP8X4),
                     lhsT_scale=scales[:, t * P : (t + 1) * P],
                     rhs=p_q[b][0][:].bitcast(FP8X4),
@@ -280,14 +277,14 @@ def tile_list_code_search_context_kernel(
                     stop=last,
                 )
 
-        def gates(gate):
+        def gates(g, gate):
             for t in range(PACK):
-                nc.scalar.activation(gate[:, t, :], banks[t][:], SIGMOID)
+                nc.scalar.activation(gate[:, t, :], banks[PACK * g + t][:], SIGMOID)
 
         def products(g, y, gate):
             dram = out_0[g * GROUP : (g + 1) * GROUP, :].rearrange("(p t) j -> p t j", t=PACK)
             for t in range(PACK):
-                nc.vector.tensor_tensor(y[:, t, :], banks[PACK + t][:], gate[:, t, :], MULT)
+                nc.vector.tensor_tensor(y[:, t, :], banks[PACK * (1 - g) + t][:], gate[:, t, :], MULT)
                 nc.sync.dma_start(dram[:, t, :], y[:, t, :])
 
         def store_planes(g, woven, word_stores, scale_queues):
@@ -330,55 +327,48 @@ def tile_list_code_search_context_kernel(
         score_passes(1, 1, True)
         score_passes(1, 0, False)
         relevance(0)
-        trust_products(0, [on_gpsimd] * 4, held([P, PACK, S2], BF16, "p_slices0"))
+        trust_products(0, [on_gpsimd] * 4, placed([P, PACK, S2], BF16, "p_slices0", "p_slices0"))
         relevance(1)
         score_passes(2, 0, True)
         score_passes(2, 1, False)
         relevance(2)
-        for b in (1, 2):
-            trust_products(b, [on_scalar] * 4, placed([P, PACK, S2], BF16, f"p_slices{b}", f"p_slices{b}"))
+        trust_products(1, [on_gpsimd] * 4, placed([P, PACK, S2], BF16, "p_slices1", "p_slices1"))
+        trust_products(2, [on_scalar] * 4, held([P, PACK, S2], BF16, "p_slices2"))
 
         def doc_passes(g, b):
             for t in range(PACK):
                 doc_pass(g, t, b)
 
-        deal_wd(0, held([P, PACK, I_GROUPS, 2 * P], U8, "wd_dealt0"))
         quantize_p(0, "bias20")
+        deal_wd()
         doc_passes(0, 0)
-        round_wc(0, 0, "woven0", on_vector=P)
-        quantize_wc(0, 0, parts=2)
-        code_passes(0, 0, True, False)
-        quantize_p(1, "woven0")
+        quantize_p(1, "wd_raw")
         doc_passes(0, 1)
         quantize_p(2, "p_slices1")
         doc_passes(0, 2)
-        round_wc(1, 0, "woven1", on_vector=0)
-        quantize_wc(1, 0)
-        code_passes(0, 1, False, False)
-        deal_wd(1, placed([P, PACK, I_GROUPS, 2 * P], U8, "wd_dealt1", "woven1"))
-        round_wc(2, 0, "woven2", on_vector=0)
-        gate0 = placed([P, PACK, S2], F32, "gate0", "wc_raw20")
-        gates(gate0)
-        round_wc(0, 1, "woven0", on_vector=P)
-        quantize_wc(2, 0)
-        code_passes(0, 2, False, True)
-        quantize_wc(0, 1, parts=2)
+        for b in range(I_GROUPS):
+            round_wc(b, 0, f"woven{b}", on_vector=P if b == 2 else 0)
+            quantize_wc(b, 0, parts=2 if b == 2 else 1)
+            code_passes(0, b, b == 0, b == I_GROUPS - 1)
+        y0 = placed([P, PACK, S2], F32, "y0", "wc_raw10")
+        gates(0, y0)
+        products(0, y0, y0)
 
         for t in range(PACK):
             for b in range(I_GROUPS):
                 doc_pass(1, t, b)
-        round_wc(1, 1, "woven3", on_vector=0)
-        y0 = placed([P, PACK, S2], F32, "y0", "wc_raw01")
-        products(0, y0, gate0)
-        round_wc(2, 1, "woven2", on_vector=LAST_ROUNDING_VECTOR_COLUMNS)
-        quantize_wc(1, 1)
-        quantize_wc(2, 1, parts=2)
+        round_wc(0, 1, "woven0", on_vector=0)
+        quantize_wc(0, 1)
         y0_woven = weave(y0, "y0_woven", "woven2")
         store_planes(0, y0_woven, 1, [nc.sync] * 4)
+        round_wc(1, 1, "woven1", on_vector=0)
+        round_wc(2, 1, "woven3", on_vector=LAST_ROUNDING_VECTOR_COLUMNS)
+        quantize_wc(1, 1)
+        quantize_wc(2, 1, parts=2)
         for b in range(I_GROUPS):
             code_passes(1, b, b == 0, b == I_GROUPS - 1)
         y1 = placed([P, PACK, S2], F32, "y1", "wc_raw21")
-        gates(y1)
+        gates(1, y1)
         products(1, y1, y1)
         y1_woven = held([P, S2, PACK], BF16, "y1_woven")
         weave_columns(nc.vector.tensor_copy, y1_woven, y1, slice(0, HALF))

@@ -123,7 +123,7 @@ def tile_list_code_search_context_kernel(
         ]
         for h in range(2):
             bias[1, h] = score[1][:, 2 * h : 2 * h + 2, :]
-        wd_raw = placed([P, I_GROUPS, 2 * N], U8, "wd_raw", "wd_raw")
+        wd_raw = [placed([P, I_GROUPS, 2 * GROUP], U8, f"wd_raw{g}", f"wd_raw{g}") for g in range(N_GROUPS)]
         trust_sb = late.tile([P, I_GROUPS, 2 * PACK], F32, name="trust_sb", align_bytes=64)
         q_table[1] = placed([P, T2], U32, "q_table1", "q_table1")
 
@@ -178,8 +178,10 @@ def tile_list_code_search_context_kernel(
             for h in range(2):
                 for t in (2 * h, 2 * h + 1):
                     nc.vector.tensor_tensor(score[b][:, t, :], banks[score_bank(b, t)][:], bias[b, h][:, t % 2, :], ADD)
-                pair = score[b][:, 2 * h : 2 * h + 2, :]
-                nc.scalar.activation(pair, pair, SIGMOID)
+                width = 1 if (b, h) == (0, 0) else 2
+                for t in range(2 * h, 2 * h + 2, width):
+                    part = score[b][:, t : t + width, :]
+                    nc.scalar.activation(part, part, SIGMOID)
 
         def on_scalar(out, in_, factor):
             nc.scalar.activation(out, in_, COPY, scale=factor)
@@ -207,8 +209,8 @@ def tile_list_code_search_context_kernel(
                 weave_columns(nc.vector.tensor_copy, woven, slices, slice(h * HALF, (h + 1) * HALF))
             return woven[:].rearrange("p j t -> p (j t)")
 
-        def quantize(woven, name, parts):
-            words = held([P, GROUP], U32, name + "_words")
+        def quantize(woven, name, parts, tag=None):
+            words = placed([P, GROUP], U32, name + "_words", tag) if tag else held([P, GROUP], U32, name + "_words")
             scales = held([P, GROUP], U8, name + "_scales")
             width = GROUP // parts
             for h in range(parts):
@@ -245,18 +247,16 @@ def tile_list_code_search_context_kernel(
 
         wd_dealt = {}
 
-        def deal_wd():
-            dealt = placed([P, N_GROUPS, PACK, I_GROUPS, 2 * P], U8, "wd_dealt", "p_slices0")
+        def deal_wd(g, tag):
+            wd_dealt[g] = placed([P, PACK, I_GROUPS, 2 * P], U8, f"wd_dealt{g}", tag)
             nc.vector.tensor_copy(
-                dealt[:].bitcast(U16),
-                wd_raw[:].bitcast(U16).rearrange("p b (g m t) -> p g t b m", g=N_GROUPS, t=PACK),
+                wd_dealt[g][:].bitcast(U16), wd_raw[g][:].bitcast(U16).rearrange("p b (m t) -> p t b m", t=PACK)
             )
-            wd_dealt[0] = dealt
 
         def doc_pass(g, t, b):
             nc.tensor.matmul_mx(
-                out=accumulator(PACK * g + t, b == 0)[:],
-                lhsT=wd_dealt[0][:, g, t, b, :].bitcast(FP4X4),
+                out=accumulator(t, b == 0)[:],
+                lhsT=wd_dealt[g][:, t, b, :].bitcast(FP4X4),
                 lhsT_scale=wd_planes[:, g * I_GROUPS + b, t * P : (t + 1) * P],
                 rhs=p_q[b][0][:].bitcast(FP8X4),
                 rhs_scale=p_q[b][1][:],
@@ -268,7 +268,7 @@ def tile_list_code_search_context_kernel(
             words, scales = wc_q[b, g]
             for t in range(PACK):
                 nc.tensor.matmul_mx(
-                    out=accumulator(PACK * (1 - g) + t, first)[:],
+                    out=accumulator(PACK + t, first)[:],
                     lhsT=words[:, t * P : (t + 1) * P].bitcast(FP8X4),
                     lhsT_scale=scales[:, t * P : (t + 1) * P],
                     rhs=p_q[b][0][:].bitcast(FP8X4),
@@ -279,16 +279,16 @@ def tile_list_code_search_context_kernel(
 
         def gates(g, gate):
             for t in range(PACK):
-                nc.scalar.activation(gate[:, t, :], banks[PACK * g + t][:], SIGMOID)
+                nc.scalar.activation(gate[:, t, :], banks[t][:], SIGMOID)
 
         def products(g, y, gate):
             dram = out_0[g * GROUP : (g + 1) * GROUP, :].rearrange("(p t) j -> p t j", t=PACK)
             for t in range(PACK):
-                nc.vector.tensor_tensor(y[:, t, :], banks[PACK * (1 - g) + t][:], gate[:, t, :], MULT)
+                nc.vector.tensor_tensor(y[:, t, :], banks[PACK + t][:], gate[:, t, :], MULT)
                 nc.sync.dma_start(dram[:, t, :], y[:, t, :])
 
-        def store_planes(g, woven, word_stores, scale_queues):
-            words, scales = quantize(woven, f"y{g}", 2)
+        def store_planes(g, woven, word_stores, scale_queues, tag=None):
+            words, scales = quantize(woven, f"y{g}", 2, tag)
             width = S2 // word_stores
             for h in range(word_stores):
                 cols = slice(h * width, (h + 1) * width)
@@ -312,8 +312,9 @@ def tile_list_code_search_context_kernel(
                 wd_planes[QUADRANT * quad : QUADRANT * quad + 4, :, :].bitcast(I32),
                 wd_staged[rows * quad : rows * (quad + 1), :, :].rearrange("p t m -> p (t m)").bitcast(I32),
             )
-        nc.sync.dma_start(wd_raw[:].bitcast(I32), wd_words.rearrange("b p n -> p b n").bitcast(I32))
         for g in range(N_GROUPS):
+            wd_dram = wd_words[:, :, 2 * g * GROUP : 2 * (g + 1) * GROUP].rearrange("b p n -> p b n")
+            nc.sync.dma_start(wd_raw[g][:].bitcast(I32), wd_dram.bitcast(I32))
             for b in range(I_GROUPS):
                 load_wc(b, g)
 
@@ -332,7 +333,7 @@ def tile_list_code_search_context_kernel(
         score_passes(2, 0, True)
         score_passes(2, 1, False)
         relevance(2)
-        trust_products(1, [on_gpsimd] * 4, placed([P, PACK, S2], BF16, "p_slices1", "p_slices1"))
+        trust_products(1, [on_gpsimd] * 2 + [on_scalar] * 2, placed([P, PACK, S2], BF16, "p_slices1", "p_slices1"))
         trust_products(2, [on_scalar] * 4, held([P, PACK, S2], BF16, "p_slices2"))
 
         def doc_passes(g, b):
@@ -340,16 +341,17 @@ def tile_list_code_search_context_kernel(
                 doc_pass(g, t, b)
 
         quantize_p(0, "bias20")
-        deal_wd()
+        deal_wd(0, "p_slices0")
         doc_passes(0, 0)
-        quantize_p(1, "wd_raw")
+        quantize_p(1, "wd_raw0")
         doc_passes(0, 1)
         quantize_p(2, "p_slices1")
         doc_passes(0, 2)
-        for b in range(I_GROUPS):
-            round_wc(b, 0, f"woven{b}", on_vector=P if b == 2 else 0)
-            quantize_wc(b, 0, parts=2 if b == 2 else 1)
+        for b, on_vector in enumerate((P // 2, 0, P)):
+            round_wc(b, 0, f"woven{b}", on_vector)
+            quantize_wc(b, 0, parts=2 if on_vector else 1)
             code_passes(0, b, b == 0, b == I_GROUPS - 1)
+        deal_wd(1, "woven2")
         y0 = placed([P, PACK, S2], F32, "y0", "wc_raw10")
         gates(0, y0)
         products(0, y0, y0)
@@ -359,12 +361,12 @@ def tile_list_code_search_context_kernel(
                 doc_pass(1, t, b)
         round_wc(0, 1, "woven0", on_vector=0)
         quantize_wc(0, 1)
-        y0_woven = weave(y0, "y0_woven", "woven2")
-        store_planes(0, y0_woven, 1, [nc.sync] * 4)
+        y0_woven = weave(y0, "y0_woven", "bias20")
         round_wc(1, 1, "woven1", on_vector=0)
-        round_wc(2, 1, "woven3", on_vector=LAST_ROUNDING_VECTOR_COLUMNS)
         quantize_wc(1, 1)
+        round_wc(2, 1, "woven3", on_vector=LAST_ROUNDING_VECTOR_COLUMNS)
         quantize_wc(2, 1, parts=2)
+        store_planes(0, y0_woven, 1, [nc.sync] * 4, "woven3")
         for b in range(I_GROUPS):
             code_passes(1, b, b == 0, b == I_GROUPS - 1)
         y1 = placed([P, PACK, S2], F32, "y1", "wc_raw21")

@@ -84,6 +84,10 @@ def tile_list_code_search_context_kernel(
             def load_table_scales(sb, dram):
                 nc.sync.dma_start(sb[TABLE_ROW0:P, :].bitcast(I32), dram.rearrange("a q t -> q a t").bitcast(I32))
 
+            warm = held([P, 1], F32, "warm")
+            nc.gpsimd.memset(warm[:], 0.0)
+            nc.scalar.activation(warm[:], warm[:], SIGMOID)
+
             nc.sync.dma_start(list2[:], offs2)
             load_table_scales(q_table_scales, tab2_scales)
             nc.sync.dma_start(list1[:], offs)
@@ -123,17 +127,15 @@ def tile_list_code_search_context_kernel(
         ]
         for h in range(2):
             bias[1, h] = score[1][:, 2 * h : 2 * h + 2, :]
-        wd_raw = [placed([P, I_GROUPS, 2 * GROUP], U8, f"wd_raw{g}", f"wd_raw{g}") for g in range(N_GROUPS)]
+        wd_early = placed([P, I_GROUPS - 1, 2 * N], U8, "wd_early", "wd_early")
+        wd_last = placed([P, 2 * N], U8, "wd_last", "wd_last")
         trust_sb = late.tile([P, I_GROUPS, 2 * PACK], F32, name="trust_sb", align_bytes=64)
         q_table[1] = placed([P, T2], U32, "q_table1", "q_table1")
 
         def load_pathb(b):
             dram = pathb[b * GROUP : (b + 1) * GROUP, :].rearrange("(p t) j -> p t j", t=PACK)
-            if b == 1:
-                nc.sync.dma_start(score[b][:], dram)
-            else:
-                for h in range(2):
-                    nc.sync.dma_start(bias[b, h][:], dram[:, 2 * h : 2 * h + 2, :])
+            for h in range(2):
+                nc.sync.dma_start(bias[b, h][:], dram[:, 2 * h : 2 * h + 2, :])
 
         wc_raw = {}
 
@@ -144,7 +146,16 @@ def tile_list_code_search_context_kernel(
                 wc[b * GROUP : (b + 1) * GROUP, g * GROUP : (g + 1) * GROUP].rearrange("(p t) n -> p t n", t=PACK),
             )
 
+        wd_dealt = {}
+
+        def deal_wd(engine_copy, b, raw, dealt):
+            wd_dealt[b] = dealt
+            engine_copy(dealt[:].bitcast(U16), raw.bitcast(U16).rearrange("p (g m t) -> p g t m", g=N_GROUPS, t=PACK))
+
         load_words(q_table[1], tab2_words[1])
+        nc.sync.dma_start(wd_early[:].bitcast(I32), wd_words[0 : I_GROUPS - 1].rearrange("b p n -> p b n").bitcast(I32))
+        for b in range(I_GROUPS - 1):
+            deal_wd(nc.scalar.copy, b, wd_early[:, b, :], held([P, N_GROUPS, PACK, 2 * P], U8, f"wd_dealt{b}"))
         load_pathb(0)
         nc.sync.dma_start(trust_sb[:, :, 0:PACK], trust.rearrange("(b p t) -> p b t", p=P, t=PACK))
         load_pathb(1)
@@ -245,18 +256,10 @@ def tile_list_code_search_context_kernel(
             woven = wc_woven[b, g][:].rearrange("p s m t -> p (s m t)")
             wc_q[b, g] = quantize(woven, f"wc{b}{g}", parts)
 
-        wd_dealt = {}
-
-        def deal_wd(g, tag):
-            wd_dealt[g] = placed([P, PACK, I_GROUPS, 2 * P], U8, f"wd_dealt{g}", tag)
-            nc.vector.tensor_copy(
-                wd_dealt[g][:].bitcast(U16), wd_raw[g][:].bitcast(U16).rearrange("p b (m t) -> p t b m", t=PACK)
-            )
-
         def doc_pass(g, t, b):
             nc.tensor.matmul_mx(
                 out=accumulator(t, b == 0)[:],
-                lhsT=wd_dealt[g][:, t, b, :].bitcast(FP4X4),
+                lhsT=wd_dealt[b][:, g, t, :].bitcast(FP4X4),
                 lhsT_scale=wd_planes[:, g * I_GROUPS + b, t * P : (t + 1) * P],
                 rhs=p_q[b][0][:].bitcast(FP8X4),
                 rhs_scale=p_q[b][1][:],
@@ -281,11 +284,13 @@ def tile_list_code_search_context_kernel(
             for t in range(PACK):
                 nc.scalar.activation(gate[:, t, :], banks[t][:], SIGMOID)
 
-        def products(g, y, gate):
+        def products(g, y, slices_a_store):
             dram = out_0[g * GROUP : (g + 1) * GROUP, :].rearrange("(p t) j -> p t j", t=PACK)
             for t in range(PACK):
-                nc.vector.tensor_tensor(y[:, t, :], banks[PACK + t][:], gate[:, t, :], MULT)
-                nc.sync.dma_start(dram[:, t, :], y[:, t, :])
+                nc.vector.tensor_tensor(y[:, t, :], banks[PACK + t][:], y[:, t, :], MULT)
+                if (t + 1) % slices_a_store == 0:
+                    done = slice(t + 1 - slices_a_store, t + 1)
+                    nc.sync.dma_start(dram[:, done, :], y[:, done, :])
 
         def store_planes(g, woven, word_stores, scale_queues, tag=None):
             words, scales = quantize(woven, f"y{g}", 2, tag)
@@ -306,6 +311,7 @@ def tile_list_code_search_context_kernel(
         wd_staged = keep.tile([P, PACK, P], U8, name="wd_staged", tag="v_table0", align_bytes=64)
         nc.vector.tensor_copy(wd_staged[:], wd_raw_scales[:].rearrange("p (m t) -> p t m", t=PACK))
         load_pathb(2)
+        nc.sync.dma_start(wd_last[:].bitcast(I32), wd_words[I_GROUPS - 1].bitcast(I32))
         rows = WD_ROWS // 4
         for quad in QUADRANT_ORDER:
             nc.sync.dma_start(
@@ -313,8 +319,6 @@ def tile_list_code_search_context_kernel(
                 wd_staged[rows * quad : rows * (quad + 1), :, :].rearrange("p t m -> p (t m)").bitcast(I32),
             )
         for g in range(N_GROUPS):
-            wd_dram = wd_words[:, :, 2 * g * GROUP : 2 * (g + 1) * GROUP].rearrange("b p n -> p b n")
-            nc.sync.dma_start(wd_raw[g][:].bitcast(I32), wd_dram.bitcast(I32))
             for b in range(I_GROUPS):
                 load_wc(b, g)
 
@@ -341,9 +345,10 @@ def tile_list_code_search_context_kernel(
                 doc_pass(g, t, b)
 
         quantize_p(0, "bias20")
-        deal_wd(0, "p_slices0")
+        last_dealt = placed([P, N_GROUPS, PACK, 2 * P], U8, "wd_dealt_last", "p_slices0")
+        deal_wd(nc.vector.tensor_copy, I_GROUPS - 1, wd_last[:], last_dealt)
         doc_passes(0, 0)
-        quantize_p(1, "wd_raw0")
+        quantize_p(1, "wd_last")
         doc_passes(0, 1)
         quantize_p(2, "p_slices1")
         doc_passes(0, 2)
@@ -351,10 +356,9 @@ def tile_list_code_search_context_kernel(
             round_wc(b, 0, f"woven{b}", on_vector)
             quantize_wc(b, 0, parts=2 if on_vector else 1)
             code_passes(0, b, b == 0, b == I_GROUPS - 1)
-        deal_wd(1, "woven2")
         y0 = placed([P, PACK, S2], F32, "y0", "wc_raw10")
         gates(0, y0)
-        products(0, y0, y0)
+        products(0, y0, PACK)
 
         for t in range(PACK):
             for b in range(I_GROUPS):
@@ -371,7 +375,7 @@ def tile_list_code_search_context_kernel(
             code_passes(1, b, b == 0, b == I_GROUPS - 1)
         y1 = placed([P, PACK, S2], F32, "y1", "wc_raw21")
         gates(1, y1)
-        products(1, y1, y1)
+        products(1, y1, 1)
         y1_woven = held([P, S2, PACK], BF16, "y1_woven")
         weave_columns(nc.vector.tensor_copy, y1_woven, y1, slice(0, HALF))
         weave_columns(nc.vector.tensor_copy, y1_woven, y1, slice(HALF, LAST_WEAVE_VECTOR_COLUMNS))

@@ -32,6 +32,7 @@ TABLE_ROW0 = P - TABLE_ROWS
 WD_ROWS = 16 * N_GROUPS * I_GROUPS
 QUADRANT_ORDER = (0, 2, 1, 3)
 LAST_WEAVE_VECTOR_COLUMNS = 320
+PAIRED_GROUPS = (0,)
 LAST_ROUNDING_VECTOR_COLUMNS = 88
 
 
@@ -206,7 +207,8 @@ def tile_list_code_search_context_kernel(
         def trust_products(b, engines, tile):
             p_slices[b] = tile
             for t, product in enumerate(engines):
-                product(tile[:, t, :], score[b][:, t, :], trust_sb[:, b, t : t + 1])
+                out = tile[:, t // 2, :, t % 2] if b in PAIRED_GROUPS else tile[:, t, :]
+                product(out, score[b][:, t, :], trust_sb[:, b, t : t + 1])
 
         def weave_columns(engine_copy, woven, slices, cols):
             engine_copy(
@@ -234,8 +236,17 @@ def tile_list_code_search_context_kernel(
 
         p_q = {}
 
+        def weave_pairs(pairs, name, tag):
+            woven = placed([P, S2, PACK], BF16, name, tag)
+            words = pairs[:].rearrange("p u j e -> p (u j e)").bitcast(I32).rearrange("p (u j) -> p j u", u=2)
+            flat = woven[:].rearrange("p j t -> p (j t)")
+            for h in range(2):
+                cols = slice(h * HALF, (h + 1) * HALF)
+                nc.vector.tensor_copy(flat.bitcast(I32).rearrange("p (j u) -> p j u", u=2)[:, cols, :], words[:, cols, :])
+            return flat
+
         def quantize_p(b, tag):
-            woven = weave(p_slices[b], f"p_woven{b}", tag)
+            woven = (weave_pairs if b in PAIRED_GROUPS else weave)(p_slices[b], f"p_woven{b}", tag)
             p_q[b] = quantize(woven, f"p{b}", 2)
 
         wc_woven = {}
@@ -332,13 +343,13 @@ def tile_list_code_search_context_kernel(
         score_passes(1, 1, True)
         score_passes(1, 0, False)
         relevance(0)
-        trust_products(0, [on_gpsimd] * 4, placed([P, PACK, S2], BF16, "p_slices0", "p_slices0"))
+        trust_products(0, [on_gpsimd] * 4, placed([P, 2, S2, 2], BF16, "p_slices0", "p_slices0"))
         relevance(1)
         score_passes(2, 0, True)
         score_passes(2, 1, False)
         relevance(2)
         trust_products(1, [on_gpsimd] * 2 + [on_scalar] * 2, placed([P, PACK, S2], BF16, "p_slices1", "p_slices1"))
-        trust_products(2, [on_scalar] * 4, held([P, PACK, S2], BF16, "p_slices2"))
+        trust_products(2, [on_scalar] * 2 + [on_vector] * 2, held([P, PACK, S2], BF16, "p_slices2"))
 
         def doc_passes(g, b):
             for t in range(PACK):

@@ -31,9 +31,11 @@ TABLE_ROWS = 16 * K_GROUPS
 TABLE_ROW0 = P - TABLE_ROWS
 WD_ROWS = 16 * N_GROUPS * I_GROUPS
 QUADRANT_ORDER = (0, 2, 1, 3)
-LAST_WEAVE_VECTOR_COLUMNS = 320
+SECOND_ROUNDING_SCALAR = 88
+GPSIMD_ROUNDING = 64
+GPSIMD_WEAVE = 288
 PAIRED_GROUPS = (0,)
-LAST_ROUNDING_VECTOR_COLUMNS = 88
+LAST_ROUNDING_VECTOR_COLUMNS = 64
 
 
 def tile_list_code_search_context_kernel(
@@ -252,16 +254,25 @@ def tile_list_code_search_context_kernel(
         wc_woven = {}
         wc_q = {}
 
-        def round_wc(b, g, tag, on_vector):
-            wc_woven[b, g] = placed([P, PACK, P, PACK], BF16, f"wc_woven{b}{g}", tag)
-            woven = wc_woven[b, g][:].rearrange("p s m t -> p m t s")
-            raw = wc_raw[b, g][:].rearrange("p t (m s) -> p m t s", s=PACK)
-            if on_vector < P:
-                nc.scalar.copy(woven[:, on_vector:, :, :], raw[:, on_vector:, :, :])
-            if on_vector > 0:
-                for h in range(2):
-                    slots = slice(2 * h, 2 * h + 2)
-                    nc.vector.tensor_copy(woven[:, :on_vector, :, slots], raw[:, :on_vector, :, slots])
+        def round_wc(b, g, tag, engine_columns, cols):
+            if (b, g) not in wc_woven:
+                wc_woven[b, g] = placed([P, PACK, P, PACK], BF16, f"wc_woven{b}{g}", tag)
+            raw = wc_raw[b, g][:].rearrange("p t (m s) -> p t m s", s=PACK)
+            engine_columns(wc_woven[b, g][:, :, cols, :], raw[:, :, cols, :])
+
+        def on_scalar_columns(woven, raw):
+            nc.scalar.copy(woven.rearrange("p s m t -> p m t s"), raw.rearrange("p t m s -> p m t s"))
+
+        def on_vector_columns(woven, raw):
+            for slots in (slice(0, 2), slice(2, 4)):
+                nc.vector.tensor_copy(
+                    woven[:, slots].rearrange("p s m t -> p m t s"), raw[:, :, :, slots].rearrange("p t m s -> p m t s")
+                )
+
+        def on_gpsimd_columns(woven, raw):
+            nc.gpsimd.tensor_scalar(
+                woven.rearrange("p s m t -> p m s t"), raw.rearrange("p t m s -> p m s t"), 1.0, -0.0, MULT, ADD
+            )
 
         def quantize_wc(b, g, parts=1):
             woven = wc_woven[b, g][:].rearrange("p s m t -> p (s m t)")
@@ -269,7 +280,7 @@ def tile_list_code_search_context_kernel(
 
         def doc_pass(g, t, b):
             nc.tensor.matmul_mx(
-                out=accumulator(t, b == 0)[:],
+                out=accumulator(PACK * g + t, b == 0)[:],
                 lhsT=wd_dealt[b][:, g, t, :].bitcast(FP4X4),
                 lhsT_scale=wd_planes[:, g * I_GROUPS + b, t * P : (t + 1) * P],
                 rhs=p_q[b][0][:].bitcast(FP8X4),
@@ -282,7 +293,7 @@ def tile_list_code_search_context_kernel(
             words, scales = wc_q[b, g]
             for t in range(PACK):
                 nc.tensor.matmul_mx(
-                    out=accumulator(PACK + t, first)[:],
+                    out=accumulator(t, first)[:],
                     lhsT=words[:, t * P : (t + 1) * P].bitcast(FP8X4),
                     lhsT_scale=scales[:, t * P : (t + 1) * P],
                     rhs=p_q[b][0][:].bitcast(FP8X4),
@@ -293,29 +304,15 @@ def tile_list_code_search_context_kernel(
 
         def gates(g, gate):
             for t in range(PACK):
-                nc.scalar.activation(gate[:, t, :], banks[t][:], SIGMOID)
+                nc.scalar.activation(gate[:, t, :], banks[PACK * g + t][:], SIGMOID)
 
-        def products(g, y, slices_a_store):
+        def products(g, y, gate, slices_a_store):
             dram = out_0[g * GROUP : (g + 1) * GROUP, :].rearrange("(p t) j -> p t j", t=PACK)
             for t in range(PACK):
-                nc.vector.tensor_tensor(y[:, t, :], banks[PACK + t][:], y[:, t, :], MULT)
+                nc.vector.tensor_tensor(y[:, t, :], banks[t][:], gate[:, t, :], MULT)
                 if (t + 1) % slices_a_store == 0:
                     done = slice(t + 1 - slices_a_store, t + 1)
                     nc.sync.dma_start(dram[:, done, :], y[:, done, :])
-
-        def store_planes(g, woven, word_stores, scale_queues, tag=None):
-            words, scales = quantize(woven, f"y{g}", 2, tag)
-            width = S2 // word_stores
-            for h in range(word_stores):
-                cols = slice(h * width, (h + 1) * width)
-                nc.sync.dma_start(
-                    out_1[g].rearrange("p m t -> p (m t)").bitcast(I32)[:, cols], words[:, cols].bitcast(I32)
-                )
-            for quad, queue in enumerate(scale_queues):
-                queue.dma_start(
-                    out_2[g, 4 * quad : 4 * quad + 4, :].bitcast(I32),
-                    scales[QUADRANT * quad : QUADRANT * quad + 4, :].bitcast(I32),
-                )
 
         for b in range(I_GROUPS):
             gather_v(0, b)
@@ -355,40 +352,67 @@ def tile_list_code_search_context_kernel(
             for t in range(PACK):
                 doc_pass(g, t, b)
 
-        quantize_p(0, "bias20")
-        last_dealt = placed([P, N_GROUPS, PACK, 2 * P], U8, "wd_dealt_last", "p_slices0")
-        deal_wd(nc.vector.tensor_copy, I_GROUPS - 1, wd_last[:], last_dealt)
-        doc_passes(0, 0)
-        quantize_p(1, "wd_last")
-        doc_passes(0, 1)
-        quantize_p(2, "p_slices1")
-        doc_passes(0, 2)
-        for b, on_vector in enumerate((P // 2, 0, P)):
-            round_wc(b, 0, f"woven{b}", on_vector)
-            quantize_wc(b, 0, parts=2 if on_vector else 1)
-            code_passes(0, b, b == 0, b == I_GROUPS - 1)
-        y0 = placed([P, PACK, S2], F32, "y0", "wc_raw10")
-        gates(0, y0)
-        products(0, y0, PACK)
+        for b, tag in enumerate(("bias20", "wd_last", "p_slices1")):
+            quantize_p(b, tag)
+            if b == 0:
+                last_dealt = placed([P, N_GROUPS, PACK, 2 * P], U8, "wd_dealt_last", "p_slices0")
+                deal_wd(nc.vector.tensor_copy, I_GROUPS - 1, wd_last[:], last_dealt)
+            for g in range(N_GROUPS):
+                doc_passes(g, b)
 
-        for t in range(PACK):
-            for b in range(I_GROUPS):
-                doc_pass(1, t, b)
-        round_wc(0, 1, "woven0", on_vector=0)
-        quantize_wc(0, 1)
-        y0_woven = weave(y0, "y0_woven", "bias20")
-        round_wc(1, 1, "woven1", on_vector=0)
+        round_wc(0, 0, "woven0", on_scalar_columns, slice(0, P))
+        round_wc(1, 0, "woven1", on_scalar_columns, slice(0, SECOND_ROUNDING_SCALAR))
+        round_wc(1, 0, "woven1", on_vector_columns, slice(SECOND_ROUNDING_SCALAR, P))
+        quantize_wc(0, 0)
+        gate0 = placed([P, PACK, S2], F32, "gate0", "wc_raw10")
+        gates(0, gate0)
+        round_wc(2, 0, "woven2", on_vector_columns, slice(0, P))
+        round_wc(0, 1, "woven0", on_scalar_columns, slice(0, P // 2))
+        quantize_wc(1, 0)
+        quantize_wc(2, 0)
+        round_wc(0, 1, "woven0", on_vector_columns, slice(P // 2, P))
+        quantize_wc(0, 1, parts=2)
+        results = placed([P, N_GROUPS, PACK, S2], F32, "results", "wc_raw01")
+        y0, y1 = results[:, 0], results[:, 1]
+        for b in range(I_GROUPS):
+            code_passes(0, b, b == 0, b == I_GROUPS - 1)
+        round_wc(1, 1, "woven0", on_gpsimd_columns, slice(0, GPSIMD_ROUNDING))
+        products(0, y0, gate0, PACK)
+
+        round_wc(1, 1, "woven0", on_scalar_columns, slice(GPSIMD_ROUNDING, P))
+        gates(1, y1)
+        round_wc(2, 1, "woven3", on_scalar_columns, slice(LAST_ROUNDING_VECTOR_COLUMNS, P))
         quantize_wc(1, 1)
-        round_wc(2, 1, "woven3", on_vector=LAST_ROUNDING_VECTOR_COLUMNS)
+        round_wc(2, 1, "woven3", on_vector_columns, slice(0, LAST_ROUNDING_VECTOR_COLUMNS))
         quantize_wc(2, 1, parts=2)
-        store_planes(0, y0_woven, 1, [nc.sync] * 4, "woven3")
         for b in range(I_GROUPS):
             code_passes(1, b, b == 0, b == I_GROUPS - 1)
-        y1 = placed([P, PACK, S2], F32, "y1", "wc_raw21")
-        gates(1, y1)
-        products(1, y1, 1)
+        y0_woven = placed([P, S2, PACK], BF16, "y0_woven", "woven3")
+        first = slice(0, GPSIMD_WEAVE)
+        nc.gpsimd.tensor_scalar(y0_woven[:, first, :], y0[:, :, first].rearrange("p t j -> p j t"), 1.0, -0.0, MULT, ADD)
+        weave_columns(nc.scalar.copy, y0_woven, y0, slice(GPSIMD_WEAVE, S2))
+        products(1, y1, y1, 1)
         y1_woven = held([P, S2, PACK], BF16, "y1_woven")
+        weave_columns(nc.scalar.copy, y1_woven, y1, slice(HALF, S2))
+        y_words = [held([P, S2], U32, f"y_words{g}") for g in range(N_GROUPS)]
+        y_scales = held([P, N_GROUPS, S2], U8, "y_scales")
+
+        def quantize_y(g, woven, cols):
+            nc.vector.quantize_mx(
+                out=y_words[g][:, cols].bitcast(FP8X4),
+                scales=y_scales[:, g, cols],
+                in_=woven[:, cols, :].rearrange("p j t -> p (j t)"),
+            )
+            nc.sync.dma_start(
+                out_1[g].rearrange("p m t -> p (m t)").bitcast(I32)[:, cols], y_words[g][:, cols].bitcast(I32)
+            )
+
+        quantize_y(0, y0_woven, slice(0, S2))
         weave_columns(nc.vector.tensor_copy, y1_woven, y1, slice(0, HALF))
-        weave_columns(nc.vector.tensor_copy, y1_woven, y1, slice(HALF, LAST_WEAVE_VECTOR_COLUMNS))
-        weave_columns(nc.scalar.copy, y1_woven, y1, slice(LAST_WEAVE_VECTOR_COLUMNS, S2))
-        store_planes(1, y1_woven[:].rearrange("p j t -> p (j t)"), 2, [nc.sync, nc.sync, nc.scalar, nc.scalar])
+        for h in range(2):
+            quantize_y(1, y1_woven, slice(h * HALF, (h + 1) * HALF))
+        for quad, queue in enumerate([nc.sync, nc.sync, nc.scalar, nc.scalar]):
+            queue.dma_start(
+                out_2[:, 4 * quad : 4 * quad + 4, :].rearrange("g r m -> r g m").bitcast(I32),
+                y_scales[QUADRANT * quad : QUADRANT * quad + 4, :, :].bitcast(I32),
+            )

@@ -31,11 +31,11 @@ TABLE_ROWS = 16 * K_GROUPS
 TABLE_ROW0 = P - TABLE_ROWS
 WD_ROWS = 16 * N_GROUPS * I_GROUPS
 QUADRANT_ORDER = (0, 2, 1, 3)
-SECOND_ROUNDING_SCALAR = 88
-GPSIMD_ROUNDING = 64
+VECTOR_ROUNDING = {(1, 0): 40, (0, 1): 88, (2, 1): 88}
+EARLY_GATES = 2
+GPSIMD_ROUNDING = 48
 GPSIMD_WEAVE = 288
 PAIRED_GROUPS = (0,)
-LAST_ROUNDING_VECTOR_COLUMNS = 64
 
 
 def tile_list_code_search_context_kernel(
@@ -302,14 +302,14 @@ def tile_list_code_search_context_kernel(
                     stop=last,
                 )
 
-        def gates(g, gate):
-            for t in range(PACK):
-                nc.scalar.activation(gate[:, t, :], banks[PACK * g + t][:], SIGMOID)
+        def gates(g, gate, slices):
+            for t in slices:
+                nc.scalar.activation(gate[t], banks[PACK * g + t][:], SIGMOID)
 
         def products(g, y, gate, slices_a_store):
             dram = out_0[g * GROUP : (g + 1) * GROUP, :].rearrange("(p t) j -> p t j", t=PACK)
             for t in range(PACK):
-                nc.vector.tensor_tensor(y[:, t, :], banks[t][:], gate[:, t, :], MULT)
+                nc.vector.tensor_tensor(y[:, t, :], banks[t][:], gate[t], MULT)
                 if (t + 1) % slices_a_store == 0:
                     done = slice(t + 1 - slices_a_store, t + 1)
                     nc.sync.dma_start(dram[:, done, :], y[:, done, :])
@@ -360,38 +360,43 @@ def tile_list_code_search_context_kernel(
             for g in range(N_GROUPS):
                 doc_passes(g, b)
 
-        round_wc(0, 0, "woven0", on_scalar_columns, slice(0, P))
-        round_wc(1, 0, "woven1", on_scalar_columns, slice(0, SECOND_ROUNDING_SCALAR))
-        round_wc(1, 0, "woven1", on_vector_columns, slice(SECOND_ROUNDING_SCALAR, P))
+        def round_shared(b, g, tag, first, columns):
+            round_wc(b, g, tag, on_scalar_columns, slice(columns, P))
+            round_wc(b, g, tag, first, slice(0, columns))
+
+        round_wc(0, 0, "bias21", on_scalar_columns, slice(0, P))
+        round_shared(1, 0, "wd_last", on_vector_columns, VECTOR_ROUNDING[1, 0])
         quantize_wc(0, 0)
         gate0 = placed([P, PACK, S2], F32, "gate0", "wc_raw10")
-        gates(0, gate0)
-        round_wc(2, 0, "woven2", on_vector_columns, slice(0, P))
-        round_wc(0, 1, "woven0", on_scalar_columns, slice(0, P // 2))
+        gate0 = [gate0[:, t, :] for t in range(PACK)]
+        gates(0, gate0, range(PACK))
         quantize_wc(1, 0)
-        quantize_wc(2, 0)
-        round_wc(0, 1, "woven0", on_vector_columns, slice(P // 2, P))
+        round_wc(2, 0, "bias21", on_vector_columns, slice(0, P))
+        quantize_wc(2, 0, parts=2)
+        round_shared(0, 1, "wd_last", on_vector_columns, VECTOR_ROUNDING[0, 1])
         quantize_wc(0, 1, parts=2)
         results = placed([P, N_GROUPS, PACK, S2], F32, "results", "wc_raw01")
         y0, y1 = results[:, 0], results[:, 1]
+        gate1 = [y1[:, t, :] for t in range(EARLY_GATES)]
+        gates(1, gate1, range(EARLY_GATES))
         for b in range(I_GROUPS):
             code_passes(0, b, b == 0, b == I_GROUPS - 1)
-        round_wc(1, 1, "woven0", on_gpsimd_columns, slice(0, GPSIMD_ROUNDING))
+        round_shared(1, 1, "wd_last", on_gpsimd_columns, GPSIMD_ROUNDING)
         products(0, y0, gate0, PACK)
 
-        round_wc(1, 1, "woven0", on_scalar_columns, slice(GPSIMD_ROUNDING, P))
-        gates(1, y1)
-        round_wc(2, 1, "woven3", on_scalar_columns, slice(LAST_ROUNDING_VECTOR_COLUMNS, P))
         quantize_wc(1, 1)
-        round_wc(2, 1, "woven3", on_vector_columns, slice(0, LAST_ROUNDING_VECTOR_COLUMNS))
+        round_shared(2, 1, "wc_raw10", on_vector_columns, VECTOR_ROUNDING[2, 1])
+        last_gates = placed([P, PACK - EARLY_GATES, S2], F32, "last_gates", "wc_raw21")
+        gate1 = gate1 + [last_gates[:, e, :] for e in range(PACK - EARLY_GATES)]
+        gates(1, gate1, range(EARLY_GATES, PACK))
         quantize_wc(2, 1, parts=2)
         for b in range(I_GROUPS):
             code_passes(1, b, b == 0, b == I_GROUPS - 1)
-        y0_woven = placed([P, S2, PACK], BF16, "y0_woven", "woven3")
+        y0_woven = placed([P, S2, PACK], BF16, "y0_woven", "wc_raw10")
         first = slice(0, GPSIMD_WEAVE)
         nc.gpsimd.tensor_scalar(y0_woven[:, first, :], y0[:, :, first].rearrange("p t j -> p j t"), 1.0, -0.0, MULT, ADD)
         weave_columns(nc.scalar.copy, y0_woven, y0, slice(GPSIMD_WEAVE, S2))
-        products(1, y1, y1, 1)
+        products(1, y1, gate1, 1)
         y1_woven = held([P, S2, PACK], BF16, "y1_woven")
         weave_columns(nc.scalar.copy, y1_woven, y1, slice(HALF, S2))
         y_words = [held([P, S2], U32, f"y_words{g}") for g in range(N_GROUPS)]
@@ -407,8 +412,8 @@ def tile_list_code_search_context_kernel(
                 out_1[g].rearrange("p m t -> p (m t)").bitcast(I32)[:, cols], y_words[g][:, cols].bitcast(I32)
             )
 
-        quantize_y(0, y0_woven, slice(0, S2))
         weave_columns(nc.vector.tensor_copy, y1_woven, y1, slice(0, HALF))
+        quantize_y(0, y0_woven, slice(0, S2))
         for h in range(2):
             quantize_y(1, y1_woven, slice(h * HALF, (h + 1) * HALF))
         for quad, queue in enumerate([nc.sync, nc.sync, nc.scalar, nc.scalar]):

@@ -33,6 +33,7 @@ WD_ROWS = 16 * N_GROUPS * I_GROUPS
 QUADRANT_ORDER = (0, 2, 1, 3)
 VECTOR_ROUNDING = {(1, 0): 40, (0, 1): 88, (2, 1): 88}
 EARLY_GATES = 2
+CODE_ORDER = {(0, 0): (0, 1, 2), (0, 1): (2, 0, 1), (1, 0): (0, 1, 2), (1, 1): (0, 2, 1)}
 GPSIMD_ROUNDING = 48
 GPSIMD_WEAVE = 288
 PAIRED_GROUPS = (0,)
@@ -289,9 +290,10 @@ def tile_list_code_search_context_kernel(
                 stop=(b == I_GROUPS - 1),
             )
 
-        def code_passes(g, b, first, last):
-            words, scales = wc_q[b, g]
-            for t in range(PACK):
+        def code_passes(g, t, order):
+            for b in order:
+                words, scales = wc_q[b, g]
+                first, last = b == CODE_ORDER[g, t // 2][0], b == CODE_ORDER[g, t // 2][-1]
                 nc.tensor.matmul_mx(
                     out=accumulator(t, first)[:],
                     lhsT=words[:, t * P : (t + 1) * P].bitcast(FP8X4),
@@ -380,7 +382,10 @@ def tile_list_code_search_context_kernel(
         gate1 = [y1[:, t, :] for t in range(EARLY_GATES)]
         gates(1, gate1, range(EARLY_GATES))
         for b in range(I_GROUPS):
-            code_passes(0, b, b == 0, b == I_GROUPS - 1)
+            for t in range(2):
+                code_passes(0, t, [b])
+        for t in range(2, PACK):
+            code_passes(0, t, CODE_ORDER[0, 1])
         round_shared(1, 1, "wd_last", on_gpsimd_columns, GPSIMD_ROUNDING)
         products(0, y0, gate0, PACK)
 
@@ -390,13 +395,18 @@ def tile_list_code_search_context_kernel(
         gate1 = gate1 + [last_gates[:, e, :] for e in range(PACK - EARLY_GATES)]
         gates(1, gate1, range(EARLY_GATES, PACK))
         quantize_wc(2, 1, parts=2)
-        for b in range(I_GROUPS):
-            code_passes(1, b, b == 0, b == I_GROUPS - 1)
+        for t in range(PACK):
+            code_passes(1, t, [0])
+        for b in (1, 2):
+            for t in range(2):
+                code_passes(1, t, [b])
+        for t in range(2, PACK):
+            code_passes(1, t, CODE_ORDER[1, 1][1:])
         y0_woven = placed([P, S2, PACK], BF16, "y0_woven", "wc_raw10")
         first = slice(0, GPSIMD_WEAVE)
         nc.gpsimd.tensor_scalar(y0_woven[:, first, :], y0[:, :, first].rearrange("p t j -> p j t"), 1.0, -0.0, MULT, ADD)
         weave_columns(nc.scalar.copy, y0_woven, y0, slice(GPSIMD_WEAVE, S2))
-        products(1, y1, gate1, 1)
+        products(1, y1, gate1, 2)
         y1_woven = held([P, S2, PACK], BF16, "y1_woven")
         weave_columns(nc.scalar.copy, y1_woven, y1, slice(HALF, S2))
         y_words = [held([P, S2], U32, f"y_words{g}") for g in range(N_GROUPS)]
@@ -412,8 +422,8 @@ def tile_list_code_search_context_kernel(
                 out_1[g].rearrange("p m t -> p (m t)").bitcast(I32)[:, cols], y_words[g][:, cols].bitcast(I32)
             )
 
-        weave_columns(nc.vector.tensor_copy, y1_woven, y1, slice(0, HALF))
         quantize_y(0, y0_woven, slice(0, S2))
+        weave_columns(nc.vector.tensor_copy, y1_woven, y1, slice(0, HALF))
         for h in range(2):
             quantize_y(1, y1_woven, slice(h * HALF, (h + 1) * HALF))
         for quad, queue in enumerate([nc.sync, nc.sync, nc.scalar, nc.scalar]):

@@ -19,6 +19,7 @@ SIGMOID = mybir.ActivationFunctionType.Sigmoid
 COPY = mybir.ActivationFunctionType.Copy
 
 P = 128
+ALIGN = 256
 PACK = 4
 GROUP = P * PACK
 K_GROUPS = K // GROUP
@@ -49,7 +50,7 @@ def tile_list_code_search_context_kernel(
         psum = ctx.enter_context(tc.psum_pool(name="psum", bufs=1))
 
         def held(shape, dtype, name):
-            return keep.tile(shape, dtype, name=name, align_bytes=64)
+            return keep.tile(shape, dtype, name=name, align_bytes=ALIGN)
 
         def load_words(sb, dram):
             nc.sync.dma_start(sb[:].bitcast(I32), dram.rearrange("p n t -> p (n t)").bitcast(I32))
@@ -67,17 +68,17 @@ def tile_list_code_search_context_kernel(
 
         def gather_v(a, b, tag=None, pool=keep):
             name = f"v_words{a}{b}"
-            v_words[a, b] = pool.tile([P, PACK, P], U32, name=name, tag=tag or name, align_bytes=64)
+            v_words[a, b] = pool.tile([P, PACK, P], U32, name=name, tag=tag or name, align_bytes=ALIGN)
             nc.vector.tensor_copy(
                 v_words[a, b][:].rearrange("p t m -> p m t"),
                 v_table[a][:].indirect(list1[:, LIST_COLUMNS * b : LIST_COLUMNS * (b + 1)]),
             )
 
         with tc.tile_pool(name="head", bufs=1) as head:
-            v_table_scales = head.tile([P, T], U8, name="v_table_scales", align_bytes=64)
-            q_table_scales = head.tile([P, T2], U8, name="q_table_scales", align_bytes=64)
-            v_picked_scales = head.tile([P, S], U8, name="v_picked_scales", align_bytes=64)
-            q_picked_scales = head.tile([P, S2], U8, name="q_picked_scales", align_bytes=64)
+            v_table_scales = head.tile([P, T], U8, name="v_table_scales", align_bytes=ALIGN)
+            q_table_scales = head.tile([P, T2], U8, name="q_table_scales", align_bytes=ALIGN)
+            v_picked_scales = head.tile([P, S], U8, name="v_picked_scales", align_bytes=ALIGN)
+            q_picked_scales = head.tile([P, S2], U8, name="q_picked_scales", align_bytes=ALIGN)
 
             for window in (q_table_scales, v_table_scales):
                 nc.vector.memset(window[0:TABLE_ROW0, :].bitcast(I32), 0)
@@ -121,19 +122,19 @@ def tile_list_code_search_context_kernel(
         late = ctx.enter_context(tc.tile_pool(name="late", bufs=1))
 
         def placed(shape, dtype, name, tag):
-            return late.tile(shape, dtype, name=name, tag=tag, align_bytes=64)
+            return late.tile(shape, dtype, name=name, tag=tag, align_bytes=ALIGN)
 
         bias = {(b, h): placed([P, 2, S2], F32, f"bias{b}{h}", f"bias{b}{h}") for b in (0, 2) for h in range(2)}
         score = [
             held([P, PACK, S2], F32, "score0"),
-            late.tile([P, PACK, S2], F32, name="score1"),
+            late.tile([P, PACK, S2], F32, name="score1", align_bytes=ALIGN),
             held([P, PACK, S2], F32, "score2"),
         ]
         for h in range(2):
             bias[1, h] = score[1][:, 2 * h : 2 * h + 2, :]
         wd_early = placed([P, I_GROUPS - 1, 2 * N], U8, "wd_early", "wd_early")
         wd_last = placed([P, 2 * N], U8, "wd_last", "wd_last")
-        trust_sb = late.tile([P, I_GROUPS, 2 * PACK], F32, name="trust_sb", align_bytes=64)
+        trust_sb = late.tile([P, I_GROUPS, 2 * PACK], F32, name="trust_sb", align_bytes=ALIGN)
         q_table[1] = placed([P, T2], U32, "q_table1", "q_table1")
 
         def load_pathb(b):
@@ -318,7 +319,7 @@ def tile_list_code_search_context_kernel(
 
         for b in range(I_GROUPS):
             gather_v(0, b)
-        wd_staged = keep.tile([P, PACK, P], U8, name="wd_staged", tag="v_table0", align_bytes=64)
+        wd_staged = keep.tile([P, PACK, P], U8, name="wd_staged", tag="v_table0", align_bytes=ALIGN)
         nc.vector.tensor_copy(wd_staged[:], wd_raw_scales[:].rearrange("p (m t) -> p t m", t=PACK))
         load_pathb(2)
         nc.sync.dma_start(wd_last[:].bitcast(I32), wd_words[I_GROUPS - 1].bitcast(I32))

@@ -32,10 +32,10 @@ TABLE_ROWS = 16 * K_GROUPS
 TABLE_ROW0 = P - TABLE_ROWS
 WD_ROWS = 16 * N_GROUPS * I_GROUPS
 QUADRANT_ORDER = (0, 2, 1, 3)
-VECTOR_ROUNDING = {(1, 0): 40, (0, 1): 88, (2, 1): 88}
+VECTOR_ROUNDING = {(1, 0): 40, (0, 1): 88, (2, 1): 76}
 EARLY_GATES = 2
 CODE_ORDER = {(0, 0): (0, 1, 2), (0, 1): (2, 0, 1), (1, 0): (0, 1, 2), (1, 1): (0, 2, 1)}
-GPSIMD_ROUNDING = 48
+GPSIMD_ROUNDING = 60
 GPSIMD_WEAVE = 288
 PAIRED_GROUPS = (0,)
 

from contextlib import ExitStack

import concourse.mybir as mybir

K, T, S, T2, S2, N = 1024, 4096, 1536, 2048, 512, 1024
FLOPS = 2 * K * S * S2 + 2 * 2 * S * N * S2

F32 = mybir.dt.float32
BF16 = mybir.dt.bfloat16
I32 = mybir.dt.int32
U32 = mybir.dt.uint32
U16 = mybir.dt.uint16
U8 = mybir.dt.uint8
FP8X4 = mybir.dt.float8_e4m3fn_x4
FP4X4 = mybir.dt.float4_e2m1fn_x4
ADD = mybir.AluOpType.add
MULT = mybir.AluOpType.mult
SIGMOID = mybir.ActivationFunctionType.Sigmoid
COPY = mybir.ActivationFunctionType.Copy

P = 128
ALIGN = 256
PACK = 4
GROUP = P * PACK
K_GROUPS = K // GROUP
I_GROUPS = S // GROUP
N_GROUPS = N // GROUP
HALF = S2 // 2
LIST_COLUMNS = GROUP // 16
QUADRANT = 32
TABLE_ROWS = 16 * K_GROUPS
TABLE_ROW0 = P - TABLE_ROWS
WD_ROWS = 16 * N_GROUPS * I_GROUPS
QUADRANT_ORDER = (0, 2, 1, 3)
VECTOR_ROUNDING = {(1, 0): 40, (0, 1): 88, (2, 1): 76}
EARLY_GATES = 2
CODE_ORDER = {(0, 0): (0, 1, 2), (0, 1): (2, 0, 1), (1, 0): (0, 1, 2), (1, 1): (0, 2, 1)}
GPSIMD_ROUNDING = 60
GPSIMD_WEAVE = 288
PAIRED_GROUPS = (0,)


def tile_list_code_search_context_kernel(
    tc, tab_words, tab_scales, tab2_words, tab2_scales, offs, offs2, pathb, trust, wc, wd_words, wd_scales,
    out_0, out_1, out_2,
):
    nc = tc.nc
    with ExitStack() as ctx:
        keep = ctx.enter_context(tc.tile_pool(name="keep", bufs=1))
        psum = ctx.enter_context(tc.psum_pool(name="psum", bufs=1))

        def held(shape, dtype, name):
            return keep.tile(shape, dtype, name=name, align_bytes=ALIGN)

        def load_words(sb, dram):
            nc.sync.dma_start(sb[:].bitcast(I32), dram.rearrange("p n t -> p (n t)").bitcast(I32))

        list1 = keep.tile([P, S // 16], U16, name="list1")
        list2 = keep.tile([P, S2 // 16], U16, name="list2")
        v_table = [held([P, T], U32, f"v_table{a}") for a in range(K_GROUPS)]
        q_table = {0: held([P, T2], U32, "q_table0")}
        staged = held([P, S + S2], U8, "staged")
        score_planes = held([P, K_GROUPS, S2 + S], U8, "score_planes")
        wd_planes = held([P, N_GROUPS * I_GROUPS, GROUP], U8, "wd_planes")
        q_words = [held([P, S2], U32, f"q_words{a}") for a in range(K_GROUPS)]
        wd_raw_scales = held([P, GROUP], U8, "wd_raw_scales")
        v_words = {}

        def gather_v(a, b, tag=None, pool=keep):
            name = f"v_words{a}{b}"
            v_words[a, b] = pool.tile([P, PACK, P], U32, name=name, tag=tag or name, align_bytes=ALIGN)
            nc.vector.tensor_copy(
                v_words[a, b][:].rearrange("p t m -> p m t"),
                v_table[a][:].indirect(list1[:, LIST_COLUMNS * b : LIST_COLUMNS * (b + 1)]),
            )

        with tc.tile_pool(name="head", bufs=1) as head:
            v_table_scales = head.tile([P, T], U8, name="v_table_scales", align_bytes=ALIGN)
            q_table_scales = head.tile([P, T2], U8, name="q_table_scales", align_bytes=ALIGN)
            v_picked_scales = head.tile([P, S], U8, name="v_picked_scales", align_bytes=ALIGN)
            q_picked_scales = head.tile([P, S2], U8, name="q_picked_scales", align_bytes=ALIGN)

            for window in (q_table_scales, v_table_scales):
                nc.vector.memset(window[0:TABLE_ROW0, :].bitcast(I32), 0)
            nc.vector.memset(wd_raw_scales[WD_ROWS:P, :].bitcast(I32), 0)
            for planes in (score_planes, wd_planes):
                nc.gpsimd.memset(planes[:].rearrange("p c n -> p (c n)").bitcast(I32), 0)

            def load_table_scales(sb, dram):
                nc.sync.dma_start(sb[TABLE_ROW0:P, :].bitcast(I32), dram.rearrange("a q t -> q a t").bitcast(I32))

            warm = held([P, 1], F32, "warm")
            nc.gpsimd.memset(warm[:], 0.0)
            nc.scalar.activation(warm[:], warm[:], SIGMOID)

            nc.sync.dma_start(list2[:], offs2)
            load_table_scales(q_table_scales, tab2_scales)
            nc.sync.dma_start(list1[:], offs)
            load_table_scales(v_table_scales, tab_scales)
            load_words(v_table[0], tab_words[0])
            load_words(v_table[1], tab_words[1])
            load_words(q_table[0], tab2_words[0])
            nc.sync.dma_start(
                wd_raw_scales[0:WD_ROWS, :].bitcast(I32),
                wd_scales.rearrange("b q (g c) -> (q g) b c", g=N_GROUPS).bitcast(I32),
            )

            nc.vector.tensor_copy(q_picked_scales[:], q_table_scales[:].indirect(list2[:]))
            nc.vector.tensor_copy(v_picked_scales[:], v_table_scales[:].indirect(list1[:]))
            nc.vector.tensor_copy(staged[:, 0:S2].bitcast(U32), q_picked_scales[:].bitcast(U32))
            nc.vector.tensor_copy(
                staged[:, S2:].rearrange("p (b t m) -> p t b m", b=I_GROUPS, t=PACK),
                v_picked_scales[:].rearrange("p (b m t) -> p t b m", m=P, t=PACK),
            )
            rows = TABLE_ROWS // 4
            for quad in QUADRANT_ORDER:
                nc.sync.dma_start(
                    score_planes[QUADRANT * quad : QUADRANT * quad + 4, :, :].bitcast(I32),
                    staged[TABLE_ROW0 + rows * quad : TABLE_ROW0 + rows * (quad + 1), :].bitcast(I32),
                )

        late = ctx.enter_context(tc.tile_pool(name="late", bufs=1))

        def placed(shape, dtype, name, tag):
            return late.tile(shape, dtype, name=name, tag=tag, align_bytes=ALIGN)

        bias = {(b, h): placed([P, 2, S2], F32, f"bias{b}{h}", f"bias{b}{h}") for b in (0, 2) for h in range(2)}
        score = [
            held([P, PACK, S2], F32, "score0"),
            late.tile([P, PACK, S2], F32, name="score1", align_bytes=ALIGN),
            held([P, PACK, S2], F32, "score2"),
        ]
        for h in range(2):
            bias[1, h] = score[1][:, 2 * h : 2 * h + 2, :]
        wd_early = placed([P, I_GROUPS - 1, 2 * N], U8, "wd_early", "wd_early")
        wd_last = placed([P, 2 * N], U8, "wd_last", "wd_last")
        trust_sb = late.tile([P, I_GROUPS, 2 * PACK], F32, name="trust_sb", align_bytes=ALIGN)
        q_table[1] = placed([P, T2], U32, "q_table1", "q_table1")

        def load_pathb(b):
            dram = pathb[b * GROUP : (b + 1) * GROUP, :].rearrange("(p t) j -> p t j", t=PACK)
            for h in range(2):
                nc.sync.dma_start(bias[b, h][:], dram[:, 2 * h : 2 * h + 2, :])

        wc_raw = {}

        def load_wc(b, g):
            wc_raw[b, g] = placed([P, PACK, GROUP], F32, f"wc_raw{b}{g}", f"wc_raw{b}{g}")
            nc.sync.dma_start(
                wc_raw[b, g][:],
                wc[b * GROUP : (b + 1) * GROUP, g * GROUP : (g + 1) * GROUP].rearrange("(p t) n -> p t n", t=PACK),
            )

        wd_dealt = {}

        def deal_wd(engine_copy, b, raw, dealt):
            wd_dealt[b] = dealt
            engine_copy(dealt[:].bitcast(U16), raw.bitcast(U16).rearrange("p (g m t) -> p g t m", g=N_GROUPS, t=PACK))

        load_words(q_table[1], tab2_words[1])
        nc.sync.dma_start(wd_early[:].bitcast(I32), wd_words[0 : I_GROUPS - 1].rearrange("b p n -> p b n").bitcast(I32))
        for b in range(I_GROUPS - 1):
            deal_wd(nc.scalar.copy, b, wd_early[:, b, :], held([P, N_GROUPS, PACK, 2 * P], U8, f"wd_dealt{b}"))
        load_pathb(0)
        nc.sync.dma_start(trust_sb[:, :, 0:PACK], trust.rearrange("(b p t) -> p b t", p=P, t=PACK))
        load_pathb(1)

        banks = {}

        def accumulator(index, first):
            if first:
                banks[index] = psum.tile([P, S2], F32, name=f"bank{index}")
            return banks[index]

        def score_bank(b, t):
            return PACK * ((b + 1) % 2) + t

        def score_passes(b, a, first):
            v_plane = score_planes[:, a, S2 + b * GROUP : S2 + (b + 1) * GROUP]
            for t in range(PACK):
                nc.tensor.matmul_mx(
                    out=accumulator(score_bank(b, t), first)[:],
                    lhsT=v_words[a, b][:, t, :].bitcast(FP8X4),
                    lhsT_scale=v_plane[:, t * P : (t + 1) * P],
                    rhs=q_words[a][:].bitcast(FP8X4),
                    rhs_scale=score_planes[:, a, 0:S2],
                    start=first,
                    stop=not first,
                )

        p_slices = {}

        def relevance(b):
            for h in range(2):
                for t in (2 * h, 2 * h + 1):
                    nc.vector.tensor_tensor(score[b][:, t, :], banks[score_bank(b, t)][:], bias[b, h][:, t % 2, :], ADD)
                width = 1 if (b, h) == (0, 0) else 2
                for t in range(2 * h, 2 * h + 2, width):
                    part = score[b][:, t : t + width, :]
                    nc.scalar.activation(part, part, SIGMOID)

        def on_scalar(out, in_, factor):
            nc.scalar.activation(out, in_, COPY, scale=factor)

        def on_gpsimd(out, in_, factor):
            nc.gpsimd.tensor_scalar(out, in_, factor, 0.0, MULT, ADD)

        def on_vector(out, in_, factor):
            nc.vector.tensor_scalar(out, in_, factor, None, MULT)

        def trust_products(b, engines, tile):
            p_slices[b] = tile
            for t, product in enumerate(engines):
                out = tile[:, t // 2, :, t % 2] if b in PAIRED_GROUPS else tile[:, t, :]
                product(out, score[b][:, t, :], trust_sb[:, b, t : t + 1])

        def weave_columns(engine_copy, woven, slices, cols):
            engine_copy(
                woven[:, cols, :].rearrange("p (c e) t -> p c t e", e=4),
                slices[:, :, cols].rearrange("p t (c e) -> p c t e", e=4),
            )

        def weave(slices, name, tag):
            woven = placed([P, S2, PACK], BF16, name, tag)
            for h in range(2):
                weave_columns(nc.vector.tensor_copy, woven, slices, slice(h * HALF, (h + 1) * HALF))
            return woven[:].rearrange("p j t -> p (j t)")

        def quantize(woven, name, parts, tag=None):
            words = placed([P, GROUP], U32, name + "_words", tag) if tag else held([P, GROUP], U32, name + "_words")
            scales = held([P, GROUP], U8, name + "_scales")
            width = GROUP // parts
            for h in range(parts):
                nc.vector.quantize_mx(
                    out=words[:, h * width : (h + 1) * width].bitcast(FP8X4),
                    scales=scales[:, h * width : (h + 1) * width],
                    in_=woven[:, PACK * h * width : PACK * (h + 1) * width],
                )
            return words, scales

        p_q = {}

        def weave_pairs(pairs, name, tag):
            woven = placed([P, S2, PACK], BF16, name, tag)
            words = pairs[:].rearrange("p u j e -> p (u j e)").bitcast(I32).rearrange("p (u j) -> p j u", u=2)
            flat = woven[:].rearrange("p j t -> p (j t)")
            for h in range(2):
                cols = slice(h * HALF, (h + 1) * HALF)
                nc.vector.tensor_copy(flat.bitcast(I32).rearrange("p (j u) -> p j u", u=2)[:, cols, :], words[:, cols, :])
            return flat

        def quantize_p(b, tag):
            woven = (weave_pairs if b in PAIRED_GROUPS else weave)(p_slices[b], f"p_woven{b}", tag)
            p_q[b] = quantize(woven, f"p{b}", 2)

        wc_woven = {}
        wc_q = {}

        def round_wc(b, g, tag, engine_columns, cols):
            if (b, g) not in wc_woven:
                wc_woven[b, g] = placed([P, PACK, P, PACK], BF16, f"wc_woven{b}{g}", tag)
            raw = wc_raw[b, g][:].rearrange("p t (m s) -> p t m s", s=PACK)
            engine_columns(wc_woven[b, g][:, :, cols, :], raw[:, :, cols, :])

        def on_scalar_columns(woven, raw):
            nc.scalar.copy(woven.rearrange("p s m t -> p m t s"), raw.rearrange("p t m s -> p m t s"))

        def on_vector_columns(woven, raw):
            for slots in (slice(0, 2), slice(2, 4)):
                nc.vector.tensor_copy(
                    woven[:, slots].rearrange("p s m t -> p m t s"), raw[:, :, :, slots].rearrange("p t m s -> p m t s")
                )

        def on_gpsimd_columns(woven, raw):
            nc.gpsimd.tensor_scalar(
                woven.rearrange("p s m t -> p m s t"), raw.rearrange("p t m s -> p m s t"), 1.0, -0.0, MULT, ADD
            )

        def quantize_wc(b, g, parts=1):
            woven = wc_woven[b, g][:].rearrange("p s m t -> p (s m t)")
            wc_q[b, g] = quantize(woven, f"wc{b}{g}", parts)

        def doc_pass(g, t, b):
            nc.tensor.matmul_mx(
                out=accumulator(PACK * g + t, b == 0)[:],
                lhsT=wd_dealt[b][:, g, t, :].bitcast(FP4X4),
                lhsT_scale=wd_planes[:, g * I_GROUPS + b, t * P : (t + 1) * P],
                rhs=p_q[b][0][:].bitcast(FP8X4),
                rhs_scale=p_q[b][1][:],
                start=(b == 0),
                stop=(b == I_GROUPS - 1),
            )

        def code_passes(g, t, order):
            for b in order:
                words, scales = wc_q[b, g]
                first, last = b == CODE_ORDER[g, t // 2][0], b == CODE_ORDER[g, t // 2][-1]
                nc.tensor.matmul_mx(
                    out=accumulator(t, first)[:],
                    lhsT=words[:, t * P : (t + 1) * P].bitcast(FP8X4),
                    lhsT_scale=scales[:, t * P : (t + 1) * P],
                    rhs=p_q[b][0][:].bitcast(FP8X4),
                    rhs_scale=p_q[b][1][:],
                    start=first,
                    stop=last,
                )

        def gates(g, gate, slices):
            for t in slices:
                nc.scalar.activation(gate[t], banks[PACK * g + t][:], SIGMOID)

        def products(g, y, gate, slices_a_store):
            dram = out_0[g * GROUP : (g + 1) * GROUP, :].rearrange("(p t) j -> p t j", t=PACK)
            for t in range(PACK):
                nc.vector.tensor_tensor(y[:, t, :], banks[t][:], gate[t], MULT)
                if (t + 1) % slices_a_store == 0:
                    done = slice(t + 1 - slices_a_store, t + 1)
                    nc.sync.dma_start(dram[:, done, :], y[:, done, :])

        for b in range(I_GROUPS):
            gather_v(0, b)
        wd_staged = keep.tile([P, PACK, P], U8, name="wd_staged", tag="v_table0", align_bytes=ALIGN)
        nc.vector.tensor_copy(wd_staged[:], wd_raw_scales[:].rearrange("p (m t) -> p t m", t=PACK))
        load_pathb(2)
        nc.sync.dma_start(wd_last[:].bitcast(I32), wd_words[I_GROUPS - 1].bitcast(I32))
        rows = WD_ROWS // 4
        for quad in QUADRANT_ORDER:
            nc.sync.dma_start(
                wd_planes[QUADRANT * quad : QUADRANT * quad + 4, :, :].bitcast(I32),
                wd_staged[rows * quad : rows * (quad + 1), :, :].rearrange("p t m -> p (t m)").bitcast(I32),
            )
        for g in range(N_GROUPS):
            for b in range(I_GROUPS):
                load_wc(b, g)

        gather_v(1, 0)
        nc.vector.tensor_copy(q_words[0][:], q_table[0][:].indirect(list2[:]))
        gather_v(1, 1, "q_table0")
        nc.vector.tensor_copy(q_words[1][:], q_table[1][:].indirect(list2[:]))
        gather_v(1, 2, "q_table1", late)
        score_passes(0, 0, True)
        score_passes(0, 1, False)
        score_passes(1, 1, True)
        score_passes(1, 0, False)
        relevance(0)
        trust_products(0, [on_gpsimd] * 4, placed([P, 2, S2, 2], BF16, "p_slices0", "p_slices0"))
        relevance(1)
        score_passes(2, 0, True)
        score_passes(2, 1, False)
        relevance(2)
        trust_products(1, [on_gpsimd] * 2 + [on_scalar] * 2, placed([P, PACK, S2], BF16, "p_slices1", "p_slices1"))
        trust_products(2, [on_scalar] * 2 + [on_vector] * 2, held([P, PACK, S2], BF16, "p_slices2"))

        def doc_passes(g, b):
            for t in range(PACK):
                doc_pass(g, t, b)

        for b, tag in enumerate(("bias20", "wd_last", "p_slices1")):
            quantize_p(b, tag)
            if b == 0:
                last_dealt = placed([P, N_GROUPS, PACK, 2 * P], U8, "wd_dealt_last", "p_slices0")
                deal_wd(nc.vector.tensor_copy, I_GROUPS - 1, wd_last[:], last_dealt)
            for g in range(N_GROUPS):
                doc_passes(g, b)

        def round_shared(b, g, tag, first, columns):
            round_wc(b, g, tag, on_scalar_columns, slice(columns, P))
            round_wc(b, g, tag, first, slice(0, columns))

        round_wc(0, 0, "bias21", on_scalar_columns, slice(0, P))
        round_shared(1, 0, "wd_last", on_vector_columns, VECTOR_ROUNDING[1, 0])
        quantize_wc(0, 0)
        gate0 = placed([P, PACK, S2], F32, "gate0", "wc_raw10")
        gate0 = [gate0[:, t, :] for t in range(PACK)]
        gates(0, gate0, range(PACK))
        quantize_wc(1, 0)
        round_wc(2, 0, "bias21", on_vector_columns, slice(0, P))
        quantize_wc(2, 0, parts=2)
        round_shared(0, 1, "wd_last", on_vector_columns, VECTOR_ROUNDING[0, 1])
        quantize_wc(0, 1, parts=2)
        results = placed([P, N_GROUPS, PACK, S2], F32, "results", "wc_raw01")
        y0, y1 = results[:, 0], results[:, 1]
        gate1 = [y1[:, t, :] for t in range(EARLY_GATES)]
        gates(1, gate1, range(EARLY_GATES))
        for b in range(I_GROUPS):
            for t in range(2):
                code_passes(0, t, [b])
        for t in range(2, PACK):
            code_passes(0, t, CODE_ORDER[0, 1])
        round_shared(1, 1, "wd_last", on_gpsimd_columns, GPSIMD_ROUNDING)
        products(0, y0, gate0, PACK)

        quantize_wc(1, 1)
        round_shared(2, 1, "wc_raw10", on_vector_columns, VECTOR_ROUNDING[2, 1])
        last_gates = placed([P, PACK - EARLY_GATES, S2], F32, "last_gates", "wc_raw21")
        gate1 = gate1 + [last_gates[:, e, :] for e in range(PACK - EARLY_GATES)]
        gates(1, gate1, range(EARLY_GATES, PACK))
        quantize_wc(2, 1, parts=2)
        for t in range(PACK):
            code_passes(1, t, [0])
        for b in (1, 2):
            for t in range(2):
                code_passes(1, t, [b])
        for t in range(2, PACK):
            code_passes(1, t, CODE_ORDER[1, 1][1:])
        y0_woven = placed([P, S2, PACK], BF16, "y0_woven", "wc_raw10")
        first = slice(0, GPSIMD_WEAVE)
        nc.gpsimd.tensor_scalar(y0_woven[:, first, :], y0[:, :, first].rearrange("p t j -> p j t"), 1.0, -0.0, MULT, ADD)
        weave_columns(nc.scalar.copy, y0_woven, y0, slice(GPSIMD_WEAVE, S2))
        products(1, y1, gate1, 2)
        y1_woven = held([P, S2, PACK], BF16, "y1_woven")
        weave_columns(nc.scalar.copy, y1_woven, y1, slice(HALF, S2))
        y_words = [held([P, S2], U32, f"y_words{g}") for g in range(N_GROUPS)]
        y_scales = held([P, N_GROUPS, S2], U8, "y_scales")

        def quantize_y(g, woven, cols):
            nc.vector.quantize_mx(
                out=y_words[g][:, cols].bitcast(FP8X4),
                scales=y_scales[:, g, cols],
                in_=woven[:, cols, :].rearrange("p j t -> p (j t)"),
            )
            nc.sync.dma_start(
                out_1[g].rearrange("p m t -> p (m t)").bitcast(I32)[:, cols], y_words[g][:, cols].bitcast(I32)
            )

        quantize_y(0, y0_woven, slice(0, S2))
        weave_columns(nc.vector.tensor_copy, y1_woven, y1, slice(0, HALF))
        for h in range(2):
            quantize_y(1, y1_woven, slice(h * HALF, (h + 1) * HALF))
        for quad, queue in enumerate([nc.sync, nc.sync, nc.scalar, nc.scalar]):
            queue.dma_start(
                out_2[:, 4 * quad : 4 * quad + 4, :].rearrange("g r m -> r g m").bitcast(I32),
                y_scales[QUADRANT * quad : QUADRANT * quad + 4, :, :].bitcast(I32),
            )
